import numpy as np, ml_dtypes
CORES = [51,54,179,182]
N = 4
BF = ml_dtypes.bfloat16
def gentries(a):
    return np.ascontiguousarray(a.reshape(8, 16, -1).transpose(0, 2, 1)).reshape(8, -1)
def gtable(e):
    e = np.asarray(e); return np.ascontiguousarray(e.reshape(8, -1, 16).transpose(0, 2, 1)).reshape(128, -1).astype(np.int32)
W, Q, RO, END = 1536, 1536, 4, 2 ** 20 - 1
def rise(rng, n, lo, hi, e):
    return lo + (np.sort(rng.random(n)) ** e * (hi - lo - n)).astype(np.int64) + np.arange(n)
def split(rng, w, total):
    return 1 + rng.multinomial(total - len(w), np.minimum(w * np.reciprocal(np.sum(w)), 1.0))
def families(rng, L, dev, e, total):
    u = np.exp2(dev * rng.standard_normal(L)); nb0 = split(rng, u, total); like = rng.random(L) < 0.6; like[0] = True; like[1] = False
    rest = total - int(np.sum(nb0[like])); m = L - int(np.sum(like)); nb = np.tile(nb0, (N, 1))
    for r in range(N): nb[r, ~like] = split(rng, u[~like] * np.exp2(2 * rng.standard_normal(m)), rest)
    pad = rng.integers(1, 17, (N, L)); top = np.max(16 * nb - pad, axis=0); base = []
    for l in range(L):
        t = int(top[l]); more = (0, 1, t // 16)[int(rng.integers(0, 3))] if like[l] else t // 8
        base.append(rise(rng, max(1, t + more), 0, END, e))
    return nb, pad, base
def lay(rng, nb, pad, base, mode):
    ids = np.full((N, W * 16), END, np.int64); fst = np.zeros(nb.shape, np.int64)
    for r in range(N):
        at = 0
        for l in rng.permutation(nb.shape[1]):
            b = base[l]; n = int(nb[r, l]); c = 16 * n - int(pad[r, l]); fst[r, l] = at
            if c > 0:
                if mode == 1: v = b[len(b) - c:]
                else:
                    ix = np.sort(rng.permutation(len(b))[:c])
                    if mode == 2:
                        ix[-1] = len(b) - 1
                        if c > 1: ix[0] = 0
                    v = b[ix]
                ids[r, 16 * at:16 * at + c] = v
            at += n
    return np.ascontiguousarray(ids.reshape(N, W, 16).transpose(0, 2, 1)), fst
def starts(rng, nb, fst):
    L = nb.shape[1]; f = np.tile(rng.integers(0, L, Q), (N, 1))
    f = np.where((rng.random((N, Q)) < 0.5) & (rng.random(Q) < 0.125), rng.integers(0, L, (N, Q)), f)
    u = np.where(rng.random(Q) < 0.125, rng.random((N, Q)), rng.random(Q) * (rng.random(Q) < 0.5))
    m = np.take_along_axis(nb, f, 1)
    return np.take_along_axis(fst, f, 1) + np.minimum((u * m).astype(np.int64), m - 1)
def follow(a):
    last = np.concatenate([a[..., 15, :], np.full(a.shape[:-2] + (16,), END, a.dtype)], axis=-1)
    t = np.empty(a.shape, a.dtype); t[..., 0, :] = last[..., :W]
    for i in range(1, 16): t[..., i, :] = np.where(t[..., i - 1, :] == END, END, last[..., i:i + W])
    return t
def pack(ids, st):
    a = np.stack(ids, axis=1); s = np.stack(st, axis=1)
    return {"ids": a.reshape(N, 128, W).astype(np.int32), "tops": follow(a).reshape(N, 128, W).astype(np.int32), "st": np.stack([gtable(x) for x in s])}
def setup_inputs(rng):
    ids, st = [], []
    for g in range(8):
        nb, pad, base = families(rng, int(rng.integers(12, 49)), 1.5, 1.0, W)
        a, fst = lay(rng, nb, pad, base, 0); ids.append(a); st.append(starts(rng, nb, fst))
    return pack(ids, st)
def setup_inputs_far(rng):
    ids, st = [], []; dl = np.array([0, 1, 15, 16, 17, 31, 32, 33])
    for g in range(8):
        L = 6; nb = np.tile(63 + split(rng, rng.random(L) + 0.5, W - 63 * L), (N, 1)); pad = np.tile(rng.integers(1, 17, L), (N, 1))
        base = [rise(rng, int(16 * nb[0, l] - pad[0, l]), 0, END, 1.0) for l in range(L)]
        a, fst = lay(rng, nb, pad, base, 0)
        f = rng.integers(0, L, Q); k = 33 + (rng.random(Q) * (nb[0][f] - 34)).astype(np.int64)
        d = dl[rng.integers(0, np.where(rng.random(Q) < 0.75, 4, 8), (N, Q))]; d[:, :8] = dl
        d[rng.integers(0, N, Q), np.arange(Q)] = 0
        ids.append(a); st.append(np.take_along_axis(fst, np.tile(f, (N, 1)), 1) + k - d)
    return pack(ids, st)
def setup_inputs_ends(rng):
    ids, st = [], []
    for g in range(8):
        nb, pad, base = families(rng, W // 16, 2.0, 1.0, W - 5)
        base = [rise(rng, 1, 0, END, 1.0), np.array([END - 1]), np.array([0, END - 1]), np.array([0, int(rng.integers(1, END - 1)), END - 1]), rise(rng, 15, 0, END, 1.0)] + base
        for b in base[4:]:
            b[0] = 0; b[-1] = END - 1
        nb = np.concatenate([np.ones((N, 5), np.int64), nb], axis=1); pad = np.concatenate([np.tile(np.array([16, 15, 14, 13, 1]), (N, 1)), pad], axis=1)
        a, fst = lay(rng, nb, pad, base, 2); L = nb.shape[1]
        f = np.tile(np.where(rng.random(Q) < 0.25, rng.integers(0, 5, Q), rng.integers(0, L, Q)), (N, 1))
        k = np.where(rng.random(Q) < 0.75, rng.integers(0, 3, Q), rng.integers(0, 3, (N, Q)))
        m = np.take_along_axis(nb, f, 1); s = np.take_along_axis(fst, f, 1) + np.where(k == 0, 0, np.maximum(m - k, 0))
        s[:, 0] = 0; s[:, 1] = W - 1
        ids.append(a); st.append(s)
    return pack(ids, st)
def setup_inputs_alike(rng):
    ids, st = [], []
    for g in range(8):
        L = int(rng.integers(8, 21)); nb = np.tile(split(rng, rng.random(L) + 0.2, W), (N, 1)); pad = rng.integers(1, 17, (N, L)); base = []
        for l in range(L):
            b = np.add.accumulate(rng.choice(np.array([1, 1, 1, 1, 2, 5]), int(16 * nb[0, l] - 1)))
            base.append(b - b[-1] + END - 1 if l % 2 == 0 else b - b[0] + int(rng.integers(0, END - int(b[-1] - b[0]))))
        a, fst = lay(rng, nb, pad, base, 1)
        f = rng.integers(0, L, Q); k = (rng.random(Q) * nb[0][f]).astype(np.int64)
        if g % 2 == 1:
            i = rng.integers(0, 3, Q); f = f[i]; k = k[i]
        ids.append(a); st.append(np.take_along_axis(fst, np.tile(f, (N, 1)), 1) + k)
    return pack(ids, st)
def marks(rng, n):
    k = np.sort(rng.permutation(n // 16 - 1)[:15]) + 1; i = np.concatenate([np.array([-1]), 16 * k, np.array([n])]); v = []
    for m in range(16):
        p = rise(rng, int(i[m + 1] - i[m] - 1), 65536 * m, 65536 * m + 65535, 1.0)
        if rng.random() < 0.5: p[0] = 65536 * m
        v += [p, np.array([65536 * m + 65535])]
    return np.concatenate(v)[:-1]
def runs(n):
    h = n // 16 + 1
    return np.concatenate([np.arange(65536 * m - h // 2, 65536 * m - h // 2 + h) for m in range(1, 16)] + [np.arange(END - h, END)])
def setup_inputs_cases(rng):
    ids, st = [], []; L = 6; al = np.arange(L); aq = np.arange(Q); kinds = rng.permutation(8)
    for g in range(8):
        z = int(kinds[g]); nb = np.tile(63 + split(rng, rng.random(L) + 0.5, W - 63 * L), (N, 1)); m = nb[0]
        pad = np.tile(rng.integers(1, 17, L), (N, 1)); q = rng.integers(0, N, L); add = np.zeros((N, L), np.int64)
        if z == 0:
            add = 65536 * np.stack([rng.permutation(8)[:N] for l in range(L)], axis=1); add[:, 0] = 0; add[q[0], 0] = 65536
        if z == 2:
            add[:] = 1; add[q, al] = 0
        if z == 3:
            pad[:, :3] = 1; pad[q[:3], al[:3]] = 16; pad[:, 3:] = 16; add[q[3:], al[3:]] = 2 ** 19
        base = []
        for l in range(L):
            c = int(16 * m[l] - np.min(pad[:, l]))
            if z == 0: base.append(rise(rng, c, 0, 2 ** 19, 1.0))
            elif z == 1: base.append(marks(rng, c))
            elif z == 2: base.append(rise(rng, c, 1000100, END - 1, 1.0))
            elif z == 3 and l >= 3: base.append(rise(rng, c, 0, 2 ** 18, 1.0))
            elif z == 7: base.append(runs(c * 9 // 8))
            else: base.append(rise(rng, c, 0, END, 1.0))
        a, fst = lay(rng, nb, pad, base, 0 if z == 7 else 1)
        for r in range(N):
            for l in range(L):
                s = int(fst[r, l]); x = a[r, :, s:s + int(m[l])]
                a[r, :, s:s + int(m[l])] = np.where(x < END, x + add[r, l], END)
        f = rng.integers(0, L, Q); u = rng.random(Q); k = (u * m[f]).astype(np.int64); d = np.zeros((N, Q), np.int64)
        if z == 1:
            mk = np.stack([np.flatnonzero(b % 65536 == 65535) // 16 for b in base]); k = np.where(rng.random(Q) < 0.75, mk[f, rng.integers(0, 15, Q)], k)
        if z == 3:
            e = f >= 3; k = np.where(e, m[f] - 1, 16 + (u * (m[f] - 17)).astype(np.int64))
            d = np.where(rng.random((N, Q)) < 0.5, 15, rng.integers(0, 17, (N, Q))); d[:, :Q // 4] = 15; d = np.where(e, 16, d)
            d[q[f], aq] = np.where(e, k - rng.integers(0, 8, Q), 0)
        if z == 4:
            k = 16 + (u * (m[f] - 18)).astype(np.int64); d[q[0]] = rng.integers(1, 17, Q)
        if z == 5:
            o = rng.permutation(W)[:Q]; f = np.repeat(al, m)[o]; k = (np.arange(W) - np.repeat(np.add.accumulate(m) - m, m))[o]
        if z == 6:
            f[:] = int(np.argmax(fst[0])); k = 16 + (u[0] * (m[f] - 18)).astype(np.int64); d = np.tile(rng.integers(0, 17, (N, 1)), (1, Q)); d[q[0]] = 0
        if z == 7:
            k = np.maximum(k, 1); d = rng.integers(0, 2, (N, Q))
        ids.append(a); st.append(np.take_along_axis(fst, np.tile(f, (N, 1)), 1) + k - d)
    return pack(ids, st)
def setup_inputs_spread(rng):
    ids, st = [], []
    for g in range(8):
        nb, pad, base = families(rng, int(rng.integers(4, 65)), 3.0, float(rng.choice(np.array([1.0, 3.0, 8.0]))), W)
        a, fst = lay(rng, nb, pad, base, 0); s = starts(rng, nb, fst)
        ids.append(a); st.append(np.where(rng.random(Q) < 0.25, rng.integers(0, W, (N, Q)), s))
    return pack(ids, st)
def check_inputs(d):
    bad = []
    for k, lo, hi in (("ids", 0, END), ("st", 0, W - 1)):
        if np.min(d[k]) < lo or np.max(d[k]) > hi: bad.append("range of " + k)
    a = d["ids"].astype(np.int64).reshape(N, 8, 16, W); x, y = a[:, :, :-1], a[:, :, 1:]
    if not np.all((y > x) | ((x == END) & (y == END))): bad.append("order inside a block of ids")
    x, y = a[:, :, 15, :-1], a[:, :, 0, 1:]
    if not np.all((y > x) | (x == END)): bad.append("order from block to block of ids")
    if not np.all(a[:, :, 15, W - 1] == END): bad.append("end of the last list of ids")
    if not np.array_equal(d["tops"].astype(np.int64).reshape(N, 8, 16, W), follow(a)): bad.append("tops")
    return bad
def reference(ids, tops, st):
    a = ids.astype(np.int64).reshape(N, 8, 16, W); t = tops.astype(np.int64).reshape(N, 8, 16, W)
    b = np.stack([gentries(x) for x in st]).astype(np.int64)
    cur = np.take_along_axis(a[:, :, 0], b, 2)
    hits = np.zeros((8, Q), np.int64); total = np.zeros((8, Q), np.int64)
    for rnd in range(RO):
        v = np.max(cur, axis=0); hit = (np.min(cur, axis=0) == v) & (v < END)
        hits = hits + hit; total = total + np.where(hit, v, 0); v = v + hit
        n = np.sum(np.take_along_axis(t, b[:, :, None, :], 3) < v[None, :, None, :], axis=2)
        b = b + n
        x = np.take_along_axis(a, b[:, :, None, :], 3)
        p = np.sum(x < v[None, :, None, :], axis=2)
        cur = np.take_along_axis(x, np.minimum(p, 15)[:, :, None, :], 2)[:, :, 0]
    return {"yh": np.stack([gtable(hits)] * N).astype(np.float32), "ys": np.stack([gtable(total)] * N).astype(np.float32),
            "yb": np.stack([gtable(x) for x in b]).astype(np.float32), "yc": np.stack([gtable(x) for x in cur]).astype(np.float32)}

@@ -1,0 +1,375 @@
+import numpy as np
+from concourse.bass import DstId, RemoteDMATransfer
+from concourse.mybir import AluOpType, ActivationFunctionType, AxisListType
+
+CHUNKS = [512, 512, 512]
+RO, NR, W, END = 4, 4, 1536, 2 ** 20 - 1
+NC, N = len(CHUNKS), CHUNKS[0]
+L, NK = N // 16, N // 128
+RH = 16 // NK
+ZV, ZS = 704, 1216
+SEQ = [
+    0,4,1,2,8,10,9,12,11,39,301,13,15,170,38,3,5,6,7,16,17,19,20,21,22,23,24,25,31,40,41,42,171,30,43,14,44,302,37,32,177,
+    46,172,303,304,173,174,305,33,175,306,26,18,27,28,29,307,45,176,47,48,50,49,51,178,309,181,312,311,310,180,313,182,179,
+    52,53,308,55,54,314,183,315,34,184,56,57,58,59,185,187,186,316,317,60,61,62,63,188,318,64,66,319,189,190,320,65,67,321,
+    191,192,193,194,322,324,325,323,68,69,195,70,71,196,197,72,326,328,73,198,327,74,329,199,200,330,331,201,202,332,333,
+    203,334,76,77,79,78,204,335,336,205,80,104,81,36,75,206,105,82,106,83,107,84,85,337,108,86,87,88,207,208,209,210,338,
+    211,340,341,339,342,235,212,89,91,213,236,93,237,343,344,92,90,214,215,345,238,216,217,95,347,218,219,94,96,346,35,220,
+    348,97,98,349,350,99,100,222,223,351,221,353,352,354,239,224,226,101,225,102,227,103,355,228,357,229,356,230,358,231,
+    359,360,232,361,362,366,233,363,110,111,112,113,114,109,240,364,234,365,115,367,116,368,117,118,369,119,120,121,122,123,
+    124,125,126,241,243,244,242,372,374,245,375,373,376,127,246,377,128,129,247,378,371,370,248,249,379,130,250,251,131,132,
+    381,382,252,253,380,133,134,383,384,135,254,136,137,255,256,257,258,259,260,261,385,387,388,386,262,389,391,263,264,390,
+    392,393,265,395,394,266,396,267,140,139,141,142,143,397,398,432,144,269,138,145,433,434,399,268,146,435,147,148,149,400,
+    436,271,270,272,273,150,151,443,437,274,401,402,403,404,405,152,153,444,154,438,156,445,439,440,441,275,454,406,276,407,
+    155,277,278,446,408,279,280,158,410,281,282,409,157,159,411,160,161,412,413,162,447,455,283,285,286,414,284,416,417,415,
+    287,163,288,289,290,448,456,164,291,165,418,420,292,449,452,450,451,461,293,166,419,421,457,294,422,424,167,458,423,295,
+    425,296,426,427,297,459,428,298,429,460,168,299,430,169,300,431,442,462,453,463,464]
+
+SCRATCH = {
+    "x0": ("sbuf", [128, W], "int32"), "tt": ("sbuf", [128, W], "int32"), "ti": ("sbuf", [128, W], "int32"),
+    "stb": ("sbuf", [128, W // 16], "int32"), "indb": ("sbuf", [128, 8], "bfloat16"), "indf": ("sbuf", [128, 8], "float32"),
+    "sg": ("sbuf", [128, 8], "float32"), "sc": ("sbuf", [128, 1], "float32"), "cab": ("sbuf", [128, 3], "float32"),
+    "eyeb": ("sbuf", [128, 128], "bfloat16"), "dm": ("sbuf", [128, 128], "bfloat16"), "sr": ("sbuf", [128, 2048], "bfloat16"),
+    "bs": ("sbuf", [128, L], "bfloat16"), "bc": ("sbuf", [128, N], "bfloat16"), "cv": ("sbuf", [128, 128 * RH], "bfloat16"),
+    "oh": ("sbuf", [128, W // 16], "float16"), "ob": ("sbuf", [128, W // 16], "float32"), "oc": ("sbuf", [128, W // 16], "float32"),
+    "pf0": ("psum", [128, 512], "float32"), "pf1": ("psum", [128, 512], "float32"),
+}
+for _q in range(NC):
+    for _k, _s, _d in (("off", [128, L], "uint16"), ("rc", [128, RO * NR * L], "float32"),
+                       ("xx", [128, 2 * L], "float32"), ("mx", [128, L], "float32"), ("pc", [128, RO, 5 * L], "float16"),
+                       ("lt", [128, 128], "float16"), ("gt", [128, N], "float32"), ("cm", [128, N], "bfloat16"),
+                       ("ga", [128, N], "float32"), ("cc", [128, N], "bfloat16"), ("pp", [128, N], "float32"),
+                       ("hf", [128, RO * L], "bfloat16"), ("hv", [128, 2 * RO * L], "float16"), ("fa", [128, 128], "float16"),
+                       ("fb", [128, 256], "float16"), ("oo", [128, 2 * L], "float32"),
+                       ("yp", [128, 2 * L], "float16"), ("ft", [128, 128], "float16")):
+        SCRATCH["%s%d" % (_k, _q)] = ("sbuf", _s, _d)
+    SCRATCH["pv%d" % _q] = ("psum", [128, 512], "float32")
+    SCRATCH["po%d" % _q] = ("psum", [128, 512], "float32")
+
+SHARE = {"ct0": "va", "ca0": "va", "mu0": "va", "ct1": "vb", "ca1": "vb", "mu1": "vb", "pn0": "ta", "dd0": "ta", "ps0": "ta",
+         "pn1": "tc", "dd1": "tc", "ps1": "tc", "pt": "tp", "pb": "tp", "e3": "tp", "e5": "tp", "xx": "vx", "lo": "vx", "s0": "vx",
+         "ev": "so", "of": "so", "ob": "so", "e1": "vo", "e2": "vo", "e6": "vo", "hv": "vh",
+         "sn": "th", "h1": "th", "h3": "th", "hf": "sh", "h2": "sh", "h4": "sh", "e4": "sh"}
+
+
+def build():
+    ops, lastw, readers, bank = [], {}, {}, {}
+
+    def op(queue, sem, emit, reads, writes, ninc=1, after=(), banks=(), order=()):
+        n = len(ops)
+        if sem is not None and sem[:-1] in SHARE:
+            sem = SHARE[sem[:-1]] + sem[-1]
+        o = {"n": n, "q": queue, "sem": sem, "emit": emit, "ninc": ninc, "deps": set(after), "order": set(order)}
+        for t in reads:
+            if t in lastw:
+                o["deps"].add(lastw[t])
+        for t in writes:
+            if t in lastw:
+                o["deps"].add(lastw[t])
+            o["deps"].update(readers.get(t, ()))
+        for t in reads:
+            readers.setdefault(t, set()).add(n)
+        for t in writes:
+            lastw[t] = n
+            readers[t] = set()
+        for b in banks:
+            acc = bank.get(b, [])
+            o["deps"].update(i for i in acc if ops[i]["q"] != queue)
+            o["order"].update(i for i in acc if ops[i]["q"] == queue)
+            bank[b] = (acc if any(ops[i]["q"] == queue for i in acc) else []) + [n]
+        o["deps"].discard(n)
+        o["order"] -= o["deps"]
+        ops.append(o)
+        return n
+
+    A = AluOpType
+    F = ActivationFunctionType
+    CPY = F.Copy
+    V, S, P, G = "vector", "scalar", "tensor", "gpsimd"
+    ls = op("sync", "l_st", lambda g, T, x: [g.sync.dma_start(T.stb[:], T.st[:])], [], ["stb"], 16)
+    zz = op(V, "c_z", lambda g, T, x: [g.vector.memset(T.sr[:, 0:512], 0.0)], [], ["sra"])
+    za = op(V, "c_x0", lambda g, T, x: [g.vector.memset(T.x0[:, 0:ZV], 0)], [], [], order=(zz,))
+    zb = op(S, "c_x1", lambda g, T, x: [g.scalar.activation(T.x0[:, ZV:ZS], T.sr[:, 0:ZS - ZV], CPY)], ["sra"], [])
+    zc = op(G, "c_x2", lambda g, T, x: [g.iota(T.x0[:, ZS:W], [[0, W - ZS]], 0, 0)], [], [])
+    l0 = op("sync", "l_x0", lambda g, T, x: [g.sync.dma_start(T.x0[0:128:16, :], T.ids[0:128:16, :])], [], ["x0"], 16, after=(za, zb, zc), order=(ls,))
+    l1 = op("sync", "l_tt", lambda g, T, x: [g.sync.dma_start(T.tt[:], T.tops[:])], [], ["tt"], 16, order=(l0,))
+    op("sync", "l_ti", lambda g, T, x: [g.sync.dma_start(T.ti[:], T.ids[:])], [], ["ti"], 16, order=(l1,))
+    op(V, "c_m1", lambda g, T, x: [g.vector.memset(T.indb[:], 1.0)], [], ["indb"])
+    op(V, "c_m2", lambda g, T, x: [g.vector.memset(T.eyeb[:], 0.0)], [], ["eyeb"])
+    op(V, "c_m3", lambda g, T, x: [g.vector.memset(T.bs[:], 0.0)], [], ["bs"])
+    op(V, "c_m4", lambda g, T, x: [g.vector.memset(T.sr[:, 512:2048], 0.0)], [], ["srb"])
+    op(V, "c_m5", lambda g, T, x: [g.vector.memset(T.dm[:], 0.0)], [], ["dm"])
+    op(V, "c_m6", lambda g, T, x: [g.vector.memset(T.sg[:], 1.0)], [], ["sg"])
+    op(V, "c_m7", lambda g, T, x: [g.vector.memset(T.cab[64 * h:64 * h + 64, c:c + 1], v) for h, c, v in (
+        (0, 0, 1.0), (1, 0, -0.3125), (0, 1, 0.0), (1, 1, 0.125), (0, 2, 32.0), (1, 2, 1.0))], [], ["cab"], 6)
+    op(V, "c_m11", lambda g, T, x: [g.vector.memset(T.cv[:], 0.0)], [], ["cv"])
+
+    def sel(name, buf, sl, pat, cmp, fill, base, cm=1):
+        op(G, name, lambda g, T, x: [g.affine_select(T[buf][:, sl], T[buf][:, sl], pat, cmp, fill, base, cm)], [buf], [buf])
+    full = slice(0, 8)
+    sel("c_i1", "indb", full, [[-16, 8]], A.is_ge, 0.0, 0)
+    sel("c_i2", "indb", full, [[16, 8]], A.is_ge, 0.0, 15, -1)
+    sel("c_ey", "eyeb", slice(0, 128), [[-1, 128]], A.not_equal, 1.0, 0)
+    for pz in range(128 // L):
+        sel("c_b%d" % pz, "bs", slice(0, L), [[-1, L]], A.not_equal, 1.0, -L * pz)
+    sel("c_sg", "sg", full, [[-16, 8]], A.not_equal, -1.0, -15)
+    sel("c_d1", "dm", slice(0, 128), [[-1, 128]], A.not_equal, -1.0, 0)
+    sel("c_d2", "dm", slice(0, 128), [[-1, 128]], A.not_equal, 1.0, 1)
+    sel("c_d3", "dm", slice(0, 128, 16), [[-16, 8]], A.not_equal, 0.0, 1)
+    sel("c_d4", "dm", slice(0, 128, 16), [[-16, 8]], A.not_equal, 1.0, -15)
+    sel("c_d5", "dm", slice(15, 128, 16), [[-16, 8]], A.not_equal, 0.0, -15)
+    sel("c_d6", "dm", slice(15, 128, 16), [[-16, 8]], A.not_equal, -1.0, -14)
+    op(V, "c_sc", lambda g, T, x: [g.vector.tensor_reduce(T.sc[:], T.sg[:], AxisListType.X, A.min)], ["sg"], ["sc"])
+    op(S, "c_if", lambda g, T, x: [g.scalar.activation(T.indf[:], T.indb[:], CPY, scale=0.03125)], ["indb"], ["indf"])
+
+    def mksr(g, T, x):
+        return [g.scalar.activation(T.sr[:, 128 * r + r:128 * r + 128:16], T.indb[:], CPY) for r in range(16)]
+    op(S, "c_sr", mksr, ["indb"], ["sra", "srb"], 16)
+
+    def mkbc(g, T, x):
+        return [g.vector.tensor_scalar(T.bc[:, i:N:16], T.bs[:], T.cab[:, 2:3], None, A.mult) for i in range(16)]
+    op(V, "c_bc", mkbc, ["bs", "cab"], ["bc"], 16)
+    for h in range(RH):
+        def mkcv(g, T, x, h=h):
+            return [g.scalar.activation(T.cv[:, h * 128 + NK * h + k:h * 128 + 128:16], T.bs[:, 8 * k:8 * k + 8], CPY) for k in range(NK)]
+        op(S, "c_cv%d" % h, mkcv, ["bs", "cv"], ["cv_%d" % h], NK)
+    CV = ["cv_%d" % h for h in range(RH)]
+    op(V, "c_ob", lambda g, T, x: [g.vector.tensor_copy(T.oh[:], T.stb[:])], ["stb"], ["oh%d" % q for q in range(NC)])
+
+    def conv(o, parts):
+        def f(g, T, x):
+            steps = [(b, c, n, h) for b, c, n in parts for h in range(RH)]
+            return [g.tensor.matmul(o(T), T.cv[0:n, 128 * h:128 * h + 128], T[b][0:n, c + h:c + 128:RH], i == 0, i == len(steps) - 1)
+                    for i, (b, c, n, h) in enumerate(steps)]
+        return f
+
+    def hits(q, ra, pf):
+        Z = str(q)
+        n = str(ra)
+
+        def sn(g, T, x):
+            return [g.tensor.matmul(T[pf][:, 256 + r * L:256 + r * L + L], T.eyeb[:], T["pc" + Z][:, r, z * L:z * L + L], z == 2, z == 4)
+                    for r in (ra, ra + 1) for z in (2, 3, 4)]
+        op(P, "sn" + Z, sn, ["pc%d_%d_n" % (q, r) for r in (ra, ra + 1)] + ["eyeb"], [], 6, banks=[pf])
+        s = slice(ra * L, ra * L + 2 * L)
+        op(S, "hf" + Z, lambda g, T, x: [g.scalar.activation(T["hf" + Z][:, s], T[pf][:, 256 + ra * L:256 + ra * L + 2 * L], F.Relu, bias=0.25, scale=-0.25)],
+           [], ["hf" + n + Z], banks=[pf])
+
+        def hv(g, T, x):
+            return [g.vector.tensor_tensor(T["hv" + Z][:, (2 * r + a) * L:(2 * r + a) * L + L], T["pc" + Z][:, r, a * L:a * L + L],
+                                           T["hf" + Z][:, r * L:r * L + L], A.mult) for r in (ra, ra + 1) for a in (0, 1)]
+        op(V, "hv" + Z, hv, ["pc%d_%d_%s" % (q, r, t) for r in (ra, ra + 1) for t in "hl"] + ["hf" + n + Z], ["hv" + n + Z], 4)
+
+    def chunk(q):
+        cols = slice(L * q, L * q + L)
+        Z = str(q)
+        PV, PO = "pv" + Z, "po" + Z
+        H = N // 2
+
+        def nm(*a):
+            return [k + Z for k in a]
+
+        op(V, "oi" + Z, lambda g, T, x: [g.vector.tensor_copy(T["off" + Z][:], T.stb[:, cols])], ["stb"], nm("off"))
+        if q % 2 == 0:
+            op(S, "g0" + Z, lambda g, T, x: [g.scalar.activation(T["pp" + Z][:], T.x0[:, 0:W].indirect(T["off" + Z][:, 0:L]), CPY)],
+               ["x0"] + nm("off"), nm("ppA", "ppB"))
+        else:
+            op(V, "g0" + Z, lambda g, T, x: [g.vector.tensor_copy(T["pp" + Z][:], T.x0[:, 0:W].indirect(T["off" + Z][:, 0:L]))],
+               ["x0"] + nm("off"), nm("ppA", "ppB"))
+
+        def sums():
+            for a, t in ((0, "ppA"), (1, "ppB")):
+                def f(g, T, x, a=a):
+                    return [g.tensor.matmul(T[PV][:, 8 * k:8 * k + 8], T["pp" + Z][:, k:N:NK], T.indf[:], True, True) for k in range(a, NK, 2)]
+                op(P, "ps%d" % a + Z, f, nm(t) + ["indf"], [], NK // 2, banks=[PV])
+
+        def rc(T, r, a, b):
+            return T["rc" + Z][:, (r * NR + a) * L:(r * NR + b) * L]
+
+        def send(r):
+            sums()
+
+            def s0(g, T, x):
+                o, i = rc(T, r, x["rank"], x["rank"] + 1), T[PV][:, 0:L]
+                if x["rank"] == 1:
+                    return [g.vector.tensor_scalar(o, i, (END - 0.25) / 32.0, None, A.min)]
+                return [g.vector.tensor_copy(o, i)]
+            op(V, "s0" + Z, s0, [], ["own%d_%d" % (q, r)], banks=[PV])
+
+            def ex(g, T, x):
+                s = rc(T, r, x["rank"], x["rank"] + 1)
+                tr = [RemoteDMATransfer(dst_ids=[DstId(rid=a[0], pnc=a[1])], dma_engine_mask=m, remote_sem=T.sem["ar%d_%d" % (q, r)],
+                                        srcs=[s], dsts=[s], alu_op=0) for a, m in x["peers"]]
+                g.remote_dma_fused(tr, local_sem=T.sem["sent"])
+                return []
+            k = op(G, None, ex, ["own%d_%d" % (q, r)], [], 0)
+            op("remote", "ar%d_%d" % (q, r), None, [], ["arr%d_%d" % (q, r)], 0, after=(k,))
+
+        send(0)
+        for r in range(RO):
+            op(S, "gt" + Z, lambda g, T, x: [g.scalar.activation(T["gt" + Z][:], T.tt[:, 0:W].indirect(T["off" + Z][:, 0:L]), CPY)],
+               ["tt"] + nm("off"), nm("gt"))
+            src = ["arr%d_%d" % (q, r), "own%d_%d" % (q, r)]
+            mx = lambda T: T["mx" + Z][:]
+            pc = lambda T, a, b, r=r: T["pc" + Z][:, r, a * L:b * L]
+            xh = lambda T: (T["xx" + Z][:, 0:L], T["xx" + Z][:, L:2 * L])
+            pt = "pc%d_%d_" % (q, r)
+            op(V, "xx" + Z, lambda g, T, x, r=r: [g.vector.tensor_tensor(T["xx" + Z][:], rc(T, r, 0, 2), rc(T, r, 2, 4), A.max)], src, nm("xx"))
+            op(V, "ne" + Z, lambda g, T, x, r=r, pc=pc: [g.vector.tensor_tensor(pc(T, 2, 5), rc(T, r, 0, 3), rc(T, r, 1, 4), A.not_equal)], src, [pt + "n"])
+            op(V, "mx" + Z, lambda g, T, x, mx=mx: [g.vector.tensor_tensor(mx(T), xh(T)[0], xh(T)[1], A.max)], nm("xx"), nm("mx"))
+            op(V, "hi" + Z, lambda g, T, x, pc=pc: [g.vector.tensor_tensor(pc(T, 0, 1), xh(T)[0], xh(T)[1], A.max)], nm("xx"), [pt + "h"])
+            op(V, "lo" + Z, lambda g, T, x, mx=mx, pc=pc: [g.vector.tensor_tensor(pc(T, 1, 2), mx(T), pc(T, 0, 1), A.subtract)],
+               nm("mx") + [pt + "h"], [pt + "l"])
+
+            def tp(g, T, x, pc=pc):
+                return [g.tensor.matmul(T[PO][0:3 * L, 0:128], pc(T, 0, 3), T.eyeb[:], True, True),
+                        g.tensor.matmul(T[PO][3 * L:4 * L, 0:128], pc(T, 3, 4), T.eyeb[:], True, False),
+                        g.tensor.matmul(T[PO][3 * L:4 * L, 0:128], pc(T, 4, 5), T.eyeb[:], False, True)]
+            op(P, "pt" + Z, tp, [pt + "h", pt + "l", pt + "n", "eyeb"], [], 3, banks=[PO])
+            op(S, "ev" + Z, lambda g, T, x: [g.scalar.activation(T["lt" + Z][:], T[PO][:, 0:128], F.Identity, bias=T.cab[:, 1:2], scale=T.cab[:, 0:1])],
+               ["cab"], nm("lt"), banks=[PO])
+            op(P, "pb" + Z, lambda g, T, x: [
+                g.tensor.matmul(T[PV][:, k:N:NK], T.bc[:, 128 * k:128 * k + 128], T["lt" + Z][:], True, True) for k in range(NK)],
+               nm("lt") + ["bc"], [], NK, banks=[PV])
+            pn = lambda T: T[PO][:, 384:384 + L]
+            op(P, "bm" + Z, lambda g, T, x, pn=pn: [g.tensor.matmul(pn(T), T.eyeb[:], T.oh[:, cols], True, False)],
+               nm("oh") + ["eyeb"], [], banks=[PO])
+            for a in (0, 1):
+                op(V, "ct%d" % a + Z, lambda g, T, x, a=a: [
+                    g.vector.tensor_tensor(T["cm" + Z][:, a:N:2], T["gt" + Z][:, a:N:2], T[PV][:, a:N:2], A.is_lt)], nm("gt"), nm("cm%d" % a), banks=[PV])
+            for a in (0, 1):
+                def cnt(g, T, x, a=a, pn=pn):
+                    return [g.tensor.matmul(pn(T), T.sr[:, 128 * i:128 * i + 128], T["cm" + Z][:, i:N:16], False, i == 15) for i in range(a, 16, 2)]
+                op(P, "pn%d" % a + Z, cnt, nm("cm%d" % a) + ["sra", "srb"], [], 8, banks=[PO])
+            op(S, "of" + Z, lambda g, T, x, pn=pn: [g.scalar.activation(T["off" + Z][:], pn(T), CPY)], [], nm("off"), banks=[PO])
+            to = "oh" if r < RO - 1 else "ob"
+            op(S, "ob" + Z, lambda g, T, x, pn=pn, to=to: [g.scalar.activation(T[to][:, cols], pn(T), CPY)], [], nm(to), banks=[PO])
+            for a in (0, 1):
+                def gx(g, T, x, a=a):
+                    return [g.scalar.activation(T["ga" + Z][:, a * H:a * H + H], T.ti[:, 0:W].indirect(T["off" + Z][:, a * L // 2:a * L // 2 + L // 2]), CPY, scale=T.sc[:])]
+                op(S, "ga%d" % a + Z, gx, ["ti", "sc"] + nm("off"), nm("ga%d" % a))
+            for a in (0, 1):
+                h = slice(a * H, a * H + H)
+                op(V, "ca%d" % a + Z, lambda g, T, x, h=h: [
+                    g.vector.tensor_tensor(T["cc" + Z][:, h], T["ga" + Z][:, h], T[PV][:, h], A.is_lt)], nm("ga%d" % a), nm("cc%d" % a), banks=[PV])
+                op(P, "dd%d" % a + Z, lambda g, T, x, h=h: [g.tensor.matmul(T[PO][:, h], T.dm[:], T["cc" + Z][:, h], True, True)],
+                   nm("cc%d" % a) + ["dm"], [], banks=[PO])
+            for a, t in ((0, "ppA"), (1, "ppB")):
+                op(V, "mu%d" % a + Z, lambda g, T, x, a=a: [
+                    g.vector.tensor_tensor(T["pp" + Z][:, a:N:2], T["ga" + Z][:, a:N:2], T[PO][:, a:N:2], A.mult)], nm("ga0", "ga1"), nm(t), banks=[PO])
+            if r < RO - 1:
+                send(r + 1)
+            if r == 1:
+                hits(q, 0, "pf0")
+                op(P, "h1" + Z, lambda g, T, x: [g.tensor.matmul(T.pf0[:, 0:128], T["hv" + Z][:, 0:128], T.eyeb[:], True, True)],
+                   nm("hv0") + ["eyeb"], [], banks=["pf0"])
+                op(S, "h2" + Z, lambda g, T, x: [g.scalar.activation(T["fa" + Z][:], T.pf0[:, 0:128], CPY)], [], nm("fa"), banks=["pf0"])
+        sums()
+        op(V, "e1" + Z, lambda g, T, x: [g.vector.tensor_copy(T["yp" + Z][:, 0:L], T[PV][:, 0:L])], [], nm("ypa"), banks=[PV])
+        op(V, "e2" + Z, lambda g, T, x: [g.vector.tensor_tensor(T["yp" + Z][:, L:2 * L], T[PV][:, 0:L], T["yp" + Z][:, 0:L], A.subtract)],
+           nm("ypa"), nm("ypb"), banks=[PV])
+        op(P, "e3" + Z, lambda g, T, x: [g.tensor.matmul(T[PO][0:2 * L, 0:128], T["yp" + Z][:], T.eyeb[:], True, True)],
+           nm("ypa", "ypb") + ["eyeb"], [], banks=[PO])
+        op(S, "e4" + Z, lambda g, T, x: [g.scalar.activation(T["ft" + Z][0:2 * L, :], T[PO][0:2 * L, 0:128], CPY)], [], nm("ft"), banks=[PO])
+        op(P, "e5" + Z, conv(lambda T: T[PO][:, 384:384 + L], [("ft" + Z, 0, 2 * L)]), nm("ft") + CV, [], RH, banks=[PO])
+        op(V, "e6" + Z, lambda g, T, x: [g.vector.tensor_scalar(T.oc[:, cols], T[PO][:, 384:384 + L], 32.0, None, A.mult)], [], nm("oc"), banks=[PO])
+
+    def last(q):
+        cols = slice(L * q, L * q + L)
+        Z = str(q)
+        hits(q, 2, "pf0")
+        op(P, "h1" + Z, lambda g, T, x: [g.tensor.matmul(T.pf1[:, 0:128], T["hv" + Z][:, 128:256], T.eyeb[:], True, True),
+                                         g.tensor.matmul(T.pf1[:, 128:256], T["hf" + Z][:], T.eyeb[:], True, True)],
+           ["hv2" + Z, "hf0" + Z, "hf2" + Z, "eyeb"], [], 2, banks=["pf1"])
+        op(S, "h2" + Z, lambda g, T, x: [g.scalar.activation(T["fb" + Z][:], T.pf1[:, 0:256], CPY)], [], ["fb" + Z], banks=["pf1"])
+        c1 = conv(lambda T: T.pf1[:, 384:384 + L], [("fa" + Z, 0, 128), ("fb" + Z, 0, 128)])
+        c2 = conv(lambda T: T.pf1[:, 384 + L:384 + 2 * L], [("fb" + Z, 128, 128)])
+        op(P, "h3" + Z, lambda g, T, x: c1(g, T, x) + c2(g, T, x), ["fa" + Z, "fb" + Z] + CV, [], 3 * RH, banks=["pf1"])
+        op(S, "h4" + Z, lambda g, T, x: [g.scalar.activation(T["oo" + Z][:, 0:L], T.pf1[:, 384:384 + L], CPY, scale=128.0),
+                                         g.scalar.activation(T["oo" + Z][:, L:2 * L], T.pf1[:, 384 + L:384 + 2 * L], CPY, scale=4.0)],
+           [], ["oo" + Z], 2, banks=["pf1"])
+        for y, src, tok in (("yb", lambda T: T.ob[:, cols], "ob"), ("ys", lambda T: T["oo" + Z][:, 0:L], "oo"),
+                            ("yh", lambda T: T["oo" + Z][:, L:2 * L], "oo"), ("yc", lambda T: T.oc[:, cols], "oc")):
+            op("sync", "out", lambda g, T, x, y=y, src=src: [g.sync.dma_start(T[y][:, cols], src(T))], [tok + Z], [], 16)
+    for q in range(NC):
+        chunk(q)
+    for q in range(NC):
+        last(q)
+    return ops
+
+
+def plan():
+    ops, order = build(), SEQ
+    pos = {i: z for z, i in enumerate(order)}
+    assert len(pos) == len(ops) and all(pos[d] < pos[o["n"]] for o in ops for d in o["deps"] | o["order"])
+    known, clos, waits, waited = {}, {}, {}, set()
+    for i in order:
+        o = ops[i]
+        q = o["q"]
+        if q == "remote":
+            clos[i] = 1 << i
+            continue
+        k = known.get(q, 0)
+        ws = []
+        for d in sorted(o["deps"], key=lambda d: -pos[d]):
+            if not (k >> d) & 1:
+                if ops[d]["ninc"] == 0 and ops[d]["q"] != "remote":
+                    continue
+                ws.append(d)
+                k |= clos[d]
+        ws = [d for d in ws if not any(e != d and (clos[e] >> d) & 1 for e in ws)]
+        waits[i] = ws
+        waited.update(ws)
+        known[q] = k
+        clos[i] = k | (1 << i)
+    cnt, val = {}, {}
+    for i in order:
+        o = ops[i]
+        if o["q"] != "remote" and o["sem"] is not None and (i in waited or o["sem"] == "out"):
+            cnt[o["sem"]] = cnt.get(o["sem"], 0) + o["ninc"]
+            val[i] = cnt[o["sem"]]
+    return ops, order, waits, val, cnt
+
+
+OPS, ORDER, WAITS, VAL, CNT = plan()
+SEMAPHORES = sorted(CNT) + ["ar%d_%d" % (q, r) for q in range(NC) for r in range(RO)] + ["sent"]
+
+
+def rank_program(g, core, T, topo):
+    rank = T.rank_of(core)
+    if rank is None:
+        return
+    peers = [c for c in T.cores if c != core]
+    chip = topo.cores_of(core)
+    far = [c for c in peers if c not in chip]
+    near = [c for c in peers if c in chip]
+    masks = {}
+    used = []
+    for i, c in enumerate(far):
+        e = topo.engines(core, c)
+        e = e[i * (len(e) // len(far)):(i + 1) * (len(e) // len(far))]
+        used += e
+        masks[c] = e
+    for i, c in enumerate(near):
+        e = [k for k in topo.engines(core, c) if k not in used][4 * i:4 * i + 4]
+        masks[c] = e
+    inn = sum(len(masks[c]) for c in peers)
+    x = {"rank": rank, "peers": [(topo.addr(c, core), sum(1 << k for k in masks[c])) for c in far + near]}
+    queue = {"sync": g.sync, "scalar": g.scalar, "vector": g.vector, "tensor": g.tensor, "gpsimd": g}
+    sends = 0
+    for i in ORDER:
+        o = OPS[i]
+        if o["q"] == "remote":
+            continue
+        e = queue[o["q"]]
+        for d in WAITS[i]:
+            p = OPS[d]
+            e.wait_ge(T.sem[p["sem"]], inn if p["q"] == "remote" else VAL[d])
+        ins = o["emit"](g, T, x)
+        if o["sem"] is None:
+            sends += 1
+        if i in VAL:
+            for k in ins:
+                k.then_inc(T.sem[o["sem"]], o["ninc"] // len(ins))
+    g.sync.wait_ge(T.sem["out"], CNT["out"])
+    g.wait_ge(T.sem["sent"], inn * sends)

@@ -2,64 +2,49 @@ import numpy as np
 from concourse.bass import DstId, RemoteDMATransfer
 from concourse.mybir import AluOpType, ActivationFunctionType, AxisListType
 
-CHUNKS = [512, 512, 512]
 RO, NR, W, END = 4, 4, 1536, 2 ** 20 - 1
-NC, N = len(CHUNKS), CHUNKS[0]
-L, NK = N // 16, N // 128
-RH = 16 // NK
+NC = 3
+N = W // NC
+L, H, F = N // 16, N // 2, 32
 ZV, ZS = 704, 1216
-SEQ = [
-    0,4,1,2,8,10,9,12,11,39,301,13,15,170,38,3,5,6,7,16,17,19,20,21,22,23,24,25,31,40,41,42,171,30,43,14,44,302,37,32,177,
-    46,172,303,304,173,174,305,33,175,306,26,18,27,28,29,307,45,176,47,48,50,49,51,178,309,181,312,311,310,180,313,182,179,
-    52,53,308,55,54,314,183,315,34,184,56,57,58,59,185,187,186,316,317,60,61,62,63,188,318,64,66,319,189,190,320,65,67,321,
-    191,192,193,194,322,324,325,323,68,69,195,70,71,196,197,72,326,328,73,198,327,74,329,199,200,330,331,201,202,332,333,
-    203,334,76,77,79,78,204,335,336,205,80,104,81,36,75,206,105,82,106,83,107,84,85,337,108,86,87,88,207,208,209,210,338,
-    211,340,341,339,342,235,212,89,91,213,236,93,237,343,344,92,90,214,215,345,238,216,217,95,347,218,219,94,96,346,35,220,
-    348,97,98,349,350,99,100,222,223,351,221,353,352,354,239,224,226,101,225,102,227,103,355,228,357,229,356,230,358,231,
-    359,360,232,361,362,366,233,363,110,111,112,113,114,109,240,364,234,365,115,367,116,368,117,118,369,119,120,121,122,123,
-    124,125,126,241,243,244,242,372,374,245,375,373,376,127,246,377,128,129,247,378,371,370,248,249,379,130,250,251,131,132,
-    381,382,252,253,380,133,134,383,384,135,254,136,137,255,256,257,258,259,260,261,385,387,388,386,262,389,391,263,264,390,
-    392,393,265,395,394,266,396,267,140,139,141,142,143,397,398,432,144,269,138,145,433,434,399,268,146,435,147,148,149,400,
-    436,271,270,272,273,150,151,443,437,274,401,402,403,404,405,152,153,444,154,438,156,445,439,440,441,275,454,406,276,407,
-    155,277,278,446,408,279,280,158,410,281,282,409,157,159,411,160,161,412,413,162,447,455,283,285,286,414,284,416,417,415,
-    287,163,288,289,290,448,456,164,291,165,418,420,292,449,452,450,451,461,293,166,419,421,457,294,422,424,167,458,423,295,
-    425,296,426,427,297,459,428,298,429,460,168,299,430,169,300,431,442,462,453,463,464]
+TA = 24
+SEQ = [0,1,5,2,3,4,9,11,10,15,17,24,30,16,18,6,26,25,32,7,8,33,19,12,320,40,176,13,27,39,34,35,328,22,36,321,183,322,323,23,177,178,179,324,20,180,14,37,28,38,41,42,44,45,43,46,47,181,182,185,186,325,188,189,187,31,326,190,191,48,327,184,49,29,50,330,329,52,332,53,333,331,334,335,192,51,193,194,196,197,21,54,55,336,195,56,337,58,198,338,60,340,59,57,61,199,62,339,342,200,341,63,343,64,202,203,344,345,201,346,65,204,205,66,67,206,207,347,71,216,215,72,68,348,208,209,349,69,350,210,211,351,70,212,352,353,354,355,213,356,357,214,358,73,74,76,75,77,79,78,80,81,360,105,218,217,219,82,83,220,221,84,223,222,85,86,224,87,359,250,225,106,88,362,361,363,364,365,226,367,366,227,107,368,90,369,91,228,229,230,231,89,232,249,92,93,370,94,95,371,372,373,374,375,234,233,235,376,96,236,97,237,393,378,379,377,108,394,104,103,392,247,98,238,99,239,100,240,241,380,242,243,382,101,381,383,244,384,102,245,385,386,387,246,388,389,109,110,112,111,113,115,114,390,253,254,116,117,391,248,257,256,255,258,259,118,260,119,251,120,121,397,398,400,401,399,122,261,123,262,402,403,404,263,264,266,265,252,124,126,128,405,127,267,268,125,129,406,130,395,131,407,270,271,408,410,409,411,412,396,269,132,133,272,134,413,414,415,273,135,274,275,136,276,277,416,278,279,418,137,417,280,419,420,421,138,281,422,423,282,424,141,142,144,145,143,425,426,146,147,464,148,140,283,139,284,465,149,285,286,289,288,287,150,152,291,290,466,151,154,292,153,155,427,467,428,293,156,294,473,429,430,432,433,431,434,435,296,297,295,468,436,298,299,157,158,159,437,469,300,483,474,482,160,438,161,470,440,441,439,162,475,163,442,443,301,302,303,476,444,164,304,305,165,166,306,307,308,477,167,310,446,447,478,445,309,448,311,450,449,168,479,312,169,313,451,452,453,170,314,484,454,455,456,457,485,315,171,486,487,172,458,316,173,488,317,459,460,461,462,174,480,472,471,481,318,489,175,490,319,463]
+KEY = {n: z for z, n in enumerate(SEQ)}
 
 SCRATCH = {
     "x0": ("sbuf", [128, W], "int32"), "tt": ("sbuf", [128, W], "int32"), "ti": ("sbuf", [128, W], "int32"),
-    "stb": ("sbuf", [128, W // 16], "int32"), "indb": ("sbuf", [128, 8], "bfloat16"), "indf": ("sbuf", [128, 8], "float32"),
-    "sg": ("sbuf", [128, 8], "float32"), "sc": ("sbuf", [128, 1], "float32"), "cab": ("sbuf", [128, 3], "float32"),
-    "eyeb": ("sbuf", [128, 128], "bfloat16"), "dm": ("sbuf", [128, 128], "bfloat16"), "sr": ("sbuf", [128, 2048], "bfloat16"),
-    "bs": ("sbuf", [128, L], "bfloat16"), "bc": ("sbuf", [128, N], "bfloat16"), "cv": ("sbuf", [128, 128 * RH], "bfloat16"),
-    "oh": ("sbuf", [128, W // 16], "float16"), "ob": ("sbuf", [128, W // 16], "float32"), "oc": ("sbuf", [128, W // 16], "float32"),
-    "pf0": ("psum", [128, 512], "float32"), "pf1": ("psum", [128, 512], "float32"),
+    "stb": ("sbuf", [128, W // 16], "int32"), "off": ("sbuf", [128, W // 16], "uint16"),
+    "zz": ("sbuf", [128, ZS - ZV], "bfloat16"), "dif": ("sbuf", [128, 128], "float32"),
+    "indb": ("sbuf", [128, 8], "bfloat16"), "indf": ("sbuf", [128, 8], "float32"), "zt": ("sbuf", [128, 36], "float32"),
+    "sg": ("sbuf", [128, 8], "float32"), "sc": ("sbuf", [128, 1], "float32"), "cab": ("sbuf", [128, 1], "float32"),
+    "eyeb": ("sbuf", [128, 128], "bfloat16"), "dm": ("sbuf", [128, 128], "bfloat16"), "sr": ("sbuf", [128, 144], "bfloat16"),
+    "bs": ("sbuf", [128, 64], "bfloat16"), "bc": ("sbuf", [128, 512], "bfloat16"), "cv": ("sbuf", [128, 144], "bfloat16"),
+    "oh": ("sbuf", [128, W // 16], "float16"), "ob": ("sbuf", [128, W // 16], "float32"),
+    "pf0": ("psum", [128, 4, 128], "float32"), "pf1": ("psum", [128, 4, 128], "float32"),
 }
 for _q in range(NC):
-    for _k, _s, _d in (("off", [128, L], "uint16"), ("rc", [128, RO * NR * L], "float32"),
-                       ("xx", [128, 2 * L], "float32"), ("mx", [128, L], "float32"), ("pc", [128, RO, 5 * L], "float16"),
+    for _k, _s, _d in (("rc", [128, RO * NR * F], "float32"), ("xx", [128, 2 * F], "float32"), ("xn", [128, 2 * F], "float32"),
+                       ("mx", [128, F], "float32"), ("mn", [128, F], "float32"), ("pc", [128, RO, 3 * F], "float16"),
                        ("lt", [128, 128], "float16"), ("gt", [128, N], "float32"), ("cm", [128, N], "bfloat16"),
                        ("ga", [128, N], "float32"), ("cc", [128, N], "bfloat16"), ("pp", [128, N], "float32"),
-                       ("hf", [128, RO * L], "bfloat16"), ("hv", [128, 2 * RO * L], "float16"), ("fa", [128, 128], "float16"),
-                       ("fb", [128, 256], "float16"), ("oo", [128, 2 * L], "float32"),
-                       ("yp", [128, 2 * L], "float16"), ("ft", [128, 128], "float16")):
+                       ("hf", [128, RO, F], "bfloat16"), ("hv", [128, RO, 2, F], "float16"), ("fa", [128, 384], "float16"),
+                       ("oo", [128, 3 * L], "float32"), ("oc", [128, L], "float32"), ("ft", [128, 128], "float16"), ("yp", [128, 2 * F], "float16")):
         SCRATCH["%s%d" % (_k, _q)] = ("sbuf", _s, _d)
     SCRATCH["pv%d" % _q] = ("psum", [128, 512], "float32")
     SCRATCH["po%d" % _q] = ("psum", [128, 512], "float32")
 
 SHARE = {"ct0": "va", "ca0": "va", "mu0": "va", "ct1": "vb", "ca1": "vb", "mu1": "vb", "pn0": "ta", "dd0": "ta", "ps0": "ta",
          "pn1": "tc", "dd1": "tc", "ps1": "tc", "pt": "tp", "pb": "tp", "e3": "tp", "e5": "tp", "xx": "vx", "lo": "vx", "s0": "vx",
-         "ev": "so", "of": "so", "ob": "so", "e1": "vo", "e2": "vo", "e6": "vo", "hv": "vh",
-         "sn": "th", "h1": "th", "h3": "th", "hf": "sh", "h2": "sh", "h4": "sh", "e4": "sh"}
+         "e1": "vo", "e2": "vo", "e6": "vo", "hv": "vh", "h5": "vh", "h1": "th", "h3": "th", "hf": "sh", "h2": "sh", "h4": "sh", "e4": "sh"}
 
 
 def build():
-    ops, lastw, readers, bank = [], {}, {}, {}
+    ops, lastw, readers, bank, at = [], {}, {}, {}, [None, None]
 
-    def op(queue, sem, emit, reads, writes, ninc=1, after=(), banks=(), order=()):
+    def op(queue, name, emit, reads, writes, ninc=1, after=(), banks=(), order=()):
         n = len(ops)
-        if sem is not None and sem[:-1] in SHARE:
-            sem = SHARE[sem[:-1]] + sem[-1]
-        o = {"n": n, "q": queue, "sem": sem, "emit": emit, "ninc": ninc, "deps": set(after), "order": set(order)}
+        sem = name if at[0] is None or name == "out" else SHARE.get(name, name) + str(at[0])
+        o = {"n": n, "q": queue, "sem": sem, "name": name, "at": tuple(at), "emit": emit, "ninc": ninc, "deps": set(after), "order": set(order)}
         for t in reads:
             if t in lastw:
                 o["deps"].add(lastw[t])
@@ -83,118 +68,104 @@ def build():
         return n
 
     A = AluOpType
-    F = ActivationFunctionType
-    CPY = F.Copy
+    CPY = ActivationFunctionType.Copy
     V, S, P, G = "vector", "scalar", "tensor", "gpsimd"
-    ls = op("sync", "l_st", lambda g, T, x: [g.sync.dma_start(T.stb[:], T.st[:])], [], ["stb"], 16)
-    zz = op(V, "c_z", lambda g, T, x: [g.vector.memset(T.sr[:, 0:512], 0.0)], [], ["sra"])
-    za = op(V, "c_x0", lambda g, T, x: [g.vector.memset(T.x0[:, 0:ZV], 0)], [], [], order=(zz,))
-    zb = op(S, "c_x1", lambda g, T, x: [g.scalar.activation(T.x0[:, ZV:ZS], T.sr[:, 0:ZS - ZV], CPY)], ["sra"], [])
-    zc = op(G, "c_x2", lambda g, T, x: [g.iota(T.x0[:, ZS:W], [[0, W - ZS]], 0, 0)], [], [])
-    l0 = op("sync", "l_x0", lambda g, T, x: [g.sync.dma_start(T.x0[0:128:16, :], T.ids[0:128:16, :])], [], ["x0"], 16, after=(za, zb, zc), order=(ls,))
-    l1 = op("sync", "l_tt", lambda g, T, x: [g.sync.dma_start(T.tt[:], T.tops[:])], [], ["tt"], 16, order=(l0,))
-    op("sync", "l_ti", lambda g, T, x: [g.sync.dma_start(T.ti[:], T.ids[:])], [], ["ti"], 16, order=(l1,))
-    op(V, "c_m1", lambda g, T, x: [g.vector.memset(T.indb[:], 1.0)], [], ["indb"])
-    op(V, "c_m2", lambda g, T, x: [g.vector.memset(T.eyeb[:], 0.0)], [], ["eyeb"])
-    op(V, "c_m3", lambda g, T, x: [g.vector.memset(T.bs[:], 0.0)], [], ["bs"])
-    op(V, "c_m4", lambda g, T, x: [g.vector.memset(T.sr[:, 512:2048], 0.0)], [], ["srb"])
-    op(V, "c_m5", lambda g, T, x: [g.vector.memset(T.dm[:], 0.0)], [], ["dm"])
-    op(V, "c_m6", lambda g, T, x: [g.vector.memset(T.sg[:], 1.0)], [], ["sg"])
-    op(V, "c_m7", lambda g, T, x: [g.vector.memset(T.cab[64 * h:64 * h + 64, c:c + 1], v) for h, c, v in (
-        (0, 0, 1.0), (1, 0, -0.3125), (0, 1, 0.0), (1, 1, 0.125), (0, 2, 32.0), (1, 2, 1.0))], [], ["cab"], 6)
-    op(V, "c_m11", lambda g, T, x: [g.vector.memset(T.cv[:], 0.0)], [], ["cv"])
 
-    def sel(name, buf, sl, pat, cmp, fill, base, cm=1):
-        op(G, name, lambda g, T, x: [g.affine_select(T[buf][:, sl], T[buf][:, sl], pat, cmp, fill, base, cm)], [buf], [buf])
-    full = slice(0, 8)
-    sel("c_i1", "indb", full, [[-16, 8]], A.is_ge, 0.0, 0)
-    sel("c_i2", "indb", full, [[16, 8]], A.is_ge, 0.0, 15, -1)
-    sel("c_ey", "eyeb", slice(0, 128), [[-1, 128]], A.not_equal, 1.0, 0)
-    for pz in range(128 // L):
-        sel("c_b%d" % pz, "bs", slice(0, L), [[-1, L]], A.not_equal, 1.0, -L * pz)
-    sel("c_sg", "sg", full, [[-16, 8]], A.not_equal, -1.0, -15)
-    sel("c_d1", "dm", slice(0, 128), [[-1, 128]], A.not_equal, -1.0, 0)
-    sel("c_d2", "dm", slice(0, 128), [[-1, 128]], A.not_equal, 1.0, 1)
-    sel("c_d3", "dm", slice(0, 128, 16), [[-16, 8]], A.not_equal, 0.0, 1)
-    sel("c_d4", "dm", slice(0, 128, 16), [[-16, 8]], A.not_equal, 1.0, -15)
-    sel("c_d5", "dm", slice(15, 128, 16), [[-16, 8]], A.not_equal, 0.0, -15)
-    sel("c_d6", "dm", slice(15, 128, 16), [[-16, 8]], A.not_equal, -1.0, -14)
+    def load(name, dst, src, writes, **k):
+        return op("sync", name, lambda g, T, x: [g.sync.dma_start(dst(T), src(T))], [], writes, 16, **k)
+    ls = load("l_st", lambda T: T.stb[:], lambda T: T.st[:], ["stb"])
+    la = load("l_ta", lambda T: T.tt[0:TA, :], lambda T: T.tops[0:TA, :], ["tta"], order=(ls,))
+    zz = op(V, "c_z", lambda g, T, x: [g.vector.memset(T.zz[:], 0.0)], [], ["zz"])
+    za = op(V, "c_x0", lambda g, T, x: [g.vector.memset(T.x0[:, 0:ZV], 0)], [], [], order=(zz,))
+    zb = op(S, "c_x1", lambda g, T, x: [g.scalar.activation(T.x0[:, ZV:ZS], T.zz[:], CPY)], ["zz"], [])
+    zc = op(G, "c_x2", lambda g, T, x: [g.iota(T.x0[:, ZS:W], [[0, W - ZS]], 0, 0)], [], [])
+    l0 = load("l_x0", lambda T: T.x0[0:128:16, :], lambda T: T.ids[0:128:16, :], ["x0"], after=(za, zb, zc), order=(la,))
+    l1 = load("l_tt", lambda T: T.tt[TA:128, :], lambda T: T.tops[TA:128, :], ["ttb"], order=(l0,))
+    load("l_ti", lambda T: T.ti[:], lambda T: T.ids[:], ["ti"], order=(l1,))
+
+    def fill(name, buf, v):
+        op(V, name, lambda g, T, x: [g.vector.memset(T[buf][:], v)], [], [buf])
+    fill("c_m1", "indb", 1.0)
+    fill("c_m2", "sg", 1.0)
+    fill("c_m3", "sr", 0.0)
+    fill("c_m4", "cv", 0.0)
+    fill("c_m5", "zt", 0.0)
+    op(V, "c_m7", lambda g, T, x: [g.vector.memset(T.cab[0:64, :], 32.0), g.vector.memset(T.cab[64:128, :], 0.5)], [], ["cab"], 2)
+
+    def sel(name, buf, pat, cmp, v, base, cm=1):
+        op(G, name, lambda g, T, x: [g.affine_select(T[buf][:], T[buf][:], pat, cmp, v, base, cm)], [buf], [buf])
+    sel("c_i1", "indb", [[-16, 8]], A.is_ge, 0.0, 0)
+    sel("c_i2", "indb", [[16, 8]], A.is_ge, 0.0, 15, -1)
+    sel("c_sg", "sg", [[-16, 8]], A.not_equal, -1.0, -15)
+    op(G, "c_df", lambda g, T, x: [g.iota(T.dif[:], [[1, 128]], 0, -1, allow_small_or_imprecise_dtypes=True)], [], ["dif"])
+    op(V, "c_ey", lambda g, T, x: [g.vector.tensor_scalar(T.eyeb[:], T.dif[:], 0.0, None, A.is_equal)], ["dif"], ["eyeb"])
+    op(V, "c_d1", lambda g, T, x: [g.vector.tensor_tensor(T.dm[:, 1:128], T.eyeb[:, 0:127], T.eyeb[:, 1:128], A.subtract)], ["eyeb"], ["dm"])
+    op(V, "c_d2", lambda g, T, x: [g.vector.tensor_tensor(T.dm[:, 0:128:16], T.eyeb[:, 15:128:16], T.eyeb[:, 0:128:16], A.subtract),
+                                   g.vector.tensor_scalar(T.dm[:, 15:128:16], T.eyeb[:, 14:128:16], -1.0, None, A.mult)], ["eyeb"], ["dm"], 2)
+    op(V, "c_b1", lambda g, T, x: [g.vector.tensor_tensor(T.bs[:], T.eyeb[:, 0:64], T.eyeb[:, 64:128], A.add)], ["eyeb"], ["bs"])
+    op(V, "c_b2", lambda g, T, x: [g.vector.tensor_tensor(T.bs[:, 0:32], T.bs[:, 0:32], T.bs[:, 32:64], A.add)], ["bs"], ["bs"])
     op(V, "c_sc", lambda g, T, x: [g.vector.tensor_reduce(T.sc[:], T.sg[:], AxisListType.X, A.min)], ["sg"], ["sc"])
     op(S, "c_if", lambda g, T, x: [g.scalar.activation(T.indf[:], T.indb[:], CPY, scale=0.03125)], ["indb"], ["indf"])
-
-    def mksr(g, T, x):
-        return [g.scalar.activation(T.sr[:, 128 * r + r:128 * r + 128:16], T.indb[:], CPY) for r in range(16)]
-    op(S, "c_sr", mksr, ["indb"], ["sra", "srb"], 16)
-
-    def mkbc(g, T, x):
-        return [g.vector.tensor_scalar(T.bc[:, i:N:16], T.bs[:], T.cab[:, 2:3], None, A.mult) for i in range(16)]
-    op(V, "c_bc", mkbc, ["bs", "cab"], ["bc"], 16)
-    for h in range(RH):
-        def mkcv(g, T, x, h=h):
-            return [g.scalar.activation(T.cv[:, h * 128 + NK * h + k:h * 128 + 128:16], T.bs[:, 8 * k:8 * k + 8], CPY) for k in range(NK)]
-        op(S, "c_cv%d" % h, mkcv, ["bs", "cv"], ["cv_%d" % h], NK)
-    CV = ["cv_%d" % h for h in range(RH)]
+    op(S, "c_sr", lambda g, T, x: [g.scalar.activation(T.sr[:, 15:143:16], T.indb[:], CPY)], ["indb"], ["sr"])
+    op(S, "c_zt", lambda g, T, x: [g.scalar.activation(T.zt[:, 3:35:4], T.indb[:], CPY)], ["indb"], ["zt"])
+    op(V, "c_bc", lambda g, T, x: [g.vector.tensor_scalar(T.bc[:, i:512:16], T.bs[:, 0:F], T.cab[:], None, A.mult) for i in range(16)],
+       ["bs", "cab"], ["bc"], 16)
+    op(S, "c_cv", lambda g, T, x: [g.scalar.activation(T.cv[:, 12 + k:140:16], T.bs[:, 8 * k:8 * k + 8], CPY, scale=32.0) for k in range(4)],
+       ["bs"], ["cv"], 4)
+    op(V, "c_oi", lambda g, T, x: [g.vector.tensor_copy(T.off[:], T.stb[:])], ["stb"], ["off%d" % q for q in range(NC)])
     op(V, "c_ob", lambda g, T, x: [g.vector.tensor_copy(T.oh[:], T.stb[:])], ["stb"], ["oh%d" % q for q in range(NC)])
 
-    def conv(o, parts):
-        def f(g, T, x):
-            steps = [(b, c, n, h) for b, c, n in parts for h in range(RH)]
-            return [g.tensor.matmul(o(T), T.cv[0:n, 128 * h:128 * h + 128], T[b][0:n, c + h:c + 128:RH], i == 0, i == len(steps) - 1)
-                    for i, (b, c, n, h) in enumerate(steps)]
-        return f
+    def hits(q, ra):
+        Z, n, rr = str(q), str(ra), slice(ra, ra + 2)
+        pb = "pf1" if ra else "pf0"
+        op(V, "hv", lambda g, T, x: [g.vector.tensor_tensor(T["hv" + Z][:, rr, a, :], T["pc" + Z][:, rr, a * F:a * F + F], T["pc" + Z][:, rr, 2 * F:3 * F], A.mult)
+                                     for a in (0, 1)],
+           ["pc%d_%d_%s" % (q, r, t) for r in (ra, ra + 1) for t in "hln"], ["hv" + n + Z], 2)
+        op(S, "hf", lambda g, T, x: [g.scalar.activation(T["hf" + Z][:, rr, :], T["pc" + Z][:, rr, 2 * F:3 * F], CPY)],
+           ["pc%d_%d_n" % (q, r) for r in (ra, ra + 1)], ["hf" + n + Z])
+        src = [lambda T: T["hv" + Z][:, rr, :, :]] + ([lambda T: T["hf" + Z][:]] if ra else [])
+        op(P, "h1", lambda g, T, x: [g.tensor.matmul(T[pb][:, i, :], b(T), T.eyeb[:], True, True) for i, b in enumerate(src)],
+           ["hv" + n + Z, "hf0" + Z, "hf2" + Z, "eyeb"], [], len(src), banks=[pb])
+        op(S, "h2", lambda g, T, x: [g.scalar.activation(T["fa" + Z][:, 64 * ra:64 * ra + 128 * len(src)], T[pb][:, 0:len(src), :], CPY)],
+           [], ["fa" + n + Z], banks=[pb])
 
-    def hits(q, ra, pf):
-        Z = str(q)
-        n = str(ra)
-
-        def sn(g, T, x):
-            return [g.tensor.matmul(T[pf][:, 256 + r * L:256 + r * L + L], T.eyeb[:], T["pc" + Z][:, r, z * L:z * L + L], z == 2, z == 4)
-                    for r in (ra, ra + 1) for z in (2, 3, 4)]
-        op(P, "sn" + Z, sn, ["pc%d_%d_n" % (q, r) for r in (ra, ra + 1)] + ["eyeb"], [], 6, banks=[pf])
-        s = slice(ra * L, ra * L + 2 * L)
-        op(S, "hf" + Z, lambda g, T, x: [g.scalar.activation(T["hf" + Z][:, s], T[pf][:, 256 + ra * L:256 + ra * L + 2 * L], F.Relu, bias=0.25, scale=-0.25)],
-           [], ["hf" + n + Z], banks=[pf])
-
-        def hv(g, T, x):
-            return [g.vector.tensor_tensor(T["hv" + Z][:, (2 * r + a) * L:(2 * r + a) * L + L], T["pc" + Z][:, r, a * L:a * L + L],
-                                           T["hf" + Z][:, r * L:r * L + L], A.mult) for r in (ra, ra + 1) for a in (0, 1)]
-        op(V, "hv" + Z, hv, ["pc%d_%d_%s" % (q, r, t) for r in (ra, ra + 1) for t in "hl"] + ["hf" + n + Z], ["hv" + n + Z], 4)
+    def store(y, q, src, tok):
+        op("sync", "out", lambda g, T, x: [g.sync.dma_start(T[y][:, L * q:L * q + L], src(T))], [tok], [], 16)
 
     def chunk(q):
         cols = slice(L * q, L * q + L)
         Z = str(q)
         PV, PO = "pv" + Z, "po" + Z
-        H = N // 2
+        at[:] = [q, -1]
 
         def nm(*a):
             return [k + Z for k in a]
 
-        op(V, "oi" + Z, lambda g, T, x: [g.vector.tensor_copy(T["off" + Z][:], T.stb[:, cols])], ["stb"], nm("off"))
-        if q % 2 == 0:
-            op(S, "g0" + Z, lambda g, T, x: [g.scalar.activation(T["pp" + Z][:], T.x0[:, 0:W].indirect(T["off" + Z][:, 0:L]), CPY)],
-               ["x0"] + nm("off"), nm("ppA", "ppB"))
-        else:
-            op(V, "g0" + Z, lambda g, T, x: [g.vector.tensor_copy(T["pp" + Z][:], T.x0[:, 0:W].indirect(T["off" + Z][:, 0:L]))],
-               ["x0"] + nm("off"), nm("ppA", "ppB"))
+        def half(T, a):
+            return T.off[:, L * q + a * L // 2:L * q + a * L // 2 + L // 2]
 
-        def sums():
-            for a, t in ((0, "ppA"), (1, "ppB")):
-                def f(g, T, x, a=a):
-                    return [g.tensor.matmul(T[PV][:, 8 * k:8 * k + 8], T["pp" + Z][:, k:N:NK], T.indf[:], True, True) for k in range(a, NK, 2)]
-                op(P, "ps%d" % a + Z, f, nm(t) + ["indf"], [], NK // 2, banks=[PV])
+        def gather(name, out, table, a, reads, **k):
+            op(S, name, lambda g, T, x: [g.scalar.activation(T[out + Z][:, a * H:a * H + H], T[table][:, 0:W].indirect(half(T, a)), CPY,
+                                                             **{n: T[v][:] for n, v in k.items()})], reads + nm("off"), nm(out + str(a)))
+        gather("g0", "ga", "x0", 0, ["x0"])
+        op(V, "g1", lambda g, T, x: [g.vector.tensor_copy(T["ga" + Z][:, H:N], T.x0[:, 0:W].indirect(half(T, 1)))], ["x0"] + nm("off"), nm("ga1"))
 
         def rc(T, r, a, b):
-            return T["rc" + Z][:, (r * NR + a) * L:(r * NR + b) * L]
+            return T["rc" + Z][:, (r * NR + a) * F:(r * NR + b) * F]
+
+        def sums(b):
+            for a in (0, 1):
+                op(P, "ps%d" % a, lambda g, T, x, a=a: [
+                    g.tensor.matmul(T[PV][:, 8 * k:8 * k + 8], T[b + Z][:, k:N:4], T.indf[:], True, True) for k in (a, a + 2)],
+                   (nm("ga0", "ga1") if b == "ga" else nm(b + str(a))) + ["indf"], [], 2, banks=[PV])
 
         def send(r):
-            sums()
-
             def s0(g, T, x):
-                o, i = rc(T, r, x["rank"], x["rank"] + 1), T[PV][:, 0:L]
+                o, i = rc(T, r, x["rank"], x["rank"] + 1), T[PV][:, 0:F]
                 if x["rank"] == 1:
                     return [g.vector.tensor_scalar(o, i, (END - 0.25) / 32.0, None, A.min)]
                 return [g.vector.tensor_copy(o, i)]
-            op(V, "s0" + Z, s0, [], ["own%d_%d" % (q, r)], banks=[PV])
+            op(V, "s0", s0, [], ["own%d_%d" % (q, r)], banks=[PV])
 
             def ex(g, T, x):
                 s = rc(T, r, x["rank"], x["rank"] + 1)
@@ -202,95 +173,94 @@ def build():
                                         srcs=[s], dsts=[s], alu_op=0) for a, m in x["peers"]]
                 g.remote_dma_fused(tr, local_sem=T.sem["sent"])
                 return []
-            k = op(G, None, ex, ["own%d_%d" % (q, r)], [], 0)
-            op("remote", "ar%d_%d" % (q, r), None, [], ["arr%d_%d" % (q, r)], 0, after=(k,))
+            k = op(G, "ex", ex, ["own%d_%d" % (q, r)], [], 0)
+            ops[op("remote", "ar", None, [], ["arr%d_%d" % (q, r)], 0, after=(k,))]["sem"] = "ar%d_%d" % (q, r)
 
+        sums("ga")
         send(0)
         for r in range(RO):
-            op(S, "gt" + Z, lambda g, T, x: [g.scalar.activation(T["gt" + Z][:], T.tt[:, 0:W].indirect(T["off" + Z][:, 0:L]), CPY)],
-               ["tt"] + nm("off"), nm("gt"))
+            at[1] = r - 1
+            for a in (0, 1):
+                gather("gt%d" % a, "gt", "tt", a, ["tta", "ttb"])
+            if r == 2:
+                hits(q, 0)
+            at[1] = r
             src = ["arr%d_%d" % (q, r), "own%d_%d" % (q, r)]
-            mx = lambda T: T["mx" + Z][:]
-            pc = lambda T, a, b, r=r: T["pc" + Z][:, r, a * L:b * L]
-            xh = lambda T: (T["xx" + Z][:, 0:L], T["xx" + Z][:, L:2 * L])
+            pc = lambda T, a, b, r=r: T["pc" + Z][:, r, a * F:b * F]
             pt = "pc%d_%d_" % (q, r)
-            op(V, "xx" + Z, lambda g, T, x, r=r: [g.vector.tensor_tensor(T["xx" + Z][:], rc(T, r, 0, 2), rc(T, r, 2, 4), A.max)], src, nm("xx"))
-            op(V, "ne" + Z, lambda g, T, x, r=r, pc=pc: [g.vector.tensor_tensor(pc(T, 2, 5), rc(T, r, 0, 3), rc(T, r, 1, 4), A.not_equal)], src, [pt + "n"])
-            op(V, "mx" + Z, lambda g, T, x, mx=mx: [g.vector.tensor_tensor(mx(T), xh(T)[0], xh(T)[1], A.max)], nm("xx"), nm("mx"))
-            op(V, "hi" + Z, lambda g, T, x, pc=pc: [g.vector.tensor_tensor(pc(T, 0, 1), xh(T)[0], xh(T)[1], A.max)], nm("xx"), [pt + "h"])
-            op(V, "lo" + Z, lambda g, T, x, mx=mx, pc=pc: [g.vector.tensor_tensor(pc(T, 1, 2), mx(T), pc(T, 0, 1), A.subtract)],
-               nm("mx") + [pt + "h"], [pt + "l"])
 
-            def tp(g, T, x, pc=pc):
-                return [g.tensor.matmul(T[PO][0:3 * L, 0:128], pc(T, 0, 3), T.eyeb[:], True, True),
-                        g.tensor.matmul(T[PO][3 * L:4 * L, 0:128], pc(T, 3, 4), T.eyeb[:], True, False),
-                        g.tensor.matmul(T[PO][3 * L:4 * L, 0:128], pc(T, 4, 5), T.eyeb[:], False, True)]
-            op(P, "pt" + Z, tp, [pt + "h", pt + "l", pt + "n", "eyeb"], [], 3, banks=[PO])
-            op(S, "ev" + Z, lambda g, T, x: [g.scalar.activation(T["lt" + Z][:], T[PO][:, 0:128], F.Identity, bias=T.cab[:, 1:2], scale=T.cab[:, 0:1])],
-               ["cab"], nm("lt"), banks=[PO])
-            op(P, "pb" + Z, lambda g, T, x: [
-                g.tensor.matmul(T[PV][:, k:N:NK], T.bc[:, 128 * k:128 * k + 128], T["lt" + Z][:], True, True) for k in range(NK)],
-               nm("lt") + ["bc"], [], NK, banks=[PV])
+            def pair(name, out, a, b, alu, reads, writes):
+                op(V, name, lambda g, T, x: [g.vector.tensor_tensor(out(T), a(T), b(T), alu)], reads, writes)
+            whole = lambda b: lambda T: T[b + Z][:]
+            part = lambda b, a: lambda T: T[b + Z][:, a * F:a * F + F]
+            ranks = lambda a, r=r: lambda T: rc(T, r, a, a + 2)
+            plane = lambda a, pc=pc: lambda T: pc(T, a, a + 1)
+            pair("xx", whole("xx"), ranks(0), ranks(2), A.max, src, nm("xx"))
+            pair("xn", whole("xn"), ranks(0), ranks(2), A.min, src, nm("xn"))
+            pair("mn", whole("mn"), part("xn", 0), part("xn", 1), A.min, nm("xn"), nm("mn"))
+            pair("mx", whole("mx"), part("xx", 0), part("xx", 1), A.max, nm("xx"), nm("mx"))
+            pair("hi", plane(0), part("xx", 0), part("xx", 1), A.max, nm("xx"), [pt + "h"])
+            pair("lo", plane(1), whole("mx"), plane(0), A.subtract, nm("mx") + [pt + "h"], [pt + "l"])
+            pair("eq", plane(2), whole("mx"), whole("mn"), A.is_equal, nm("mx", "mn"), [pt + "n"])
+            op(P, "pt", lambda g, T, x, pc=pc: [g.tensor.matmul(T[PO][0:96, 0:128], pc(T, 0, 3), T.eyeb[:], True, True)],
+               [pt + "h", pt + "l", pt + "n", "eyeb"], [], banks=[PO])
+            op(S, "ev", lambda g, T, x: [g.scalar.activation(T["lt" + Z][0:96, :], T[PO][0:96, 0:128], CPY)], [], nm("lt"), banks=[PO])
+            op(P, "pb", lambda g, T, x: [
+                g.tensor.matmul(T[PV][:, k:N:4], T.bc[0:96, 128 * k:128 * k + 128], T["lt" + Z][0:96, :], True, True) for k in range(4)],
+               nm("lt") + ["bc"], [], 4, banks=[PV])
             pn = lambda T: T[PO][:, 384:384 + L]
-            op(P, "bm" + Z, lambda g, T, x, pn=pn: [g.tensor.matmul(pn(T), T.eyeb[:], T.oh[:, cols], True, False)],
-               nm("oh") + ["eyeb"], [], banks=[PO])
+            op(P, "bm", lambda g, T, x: [g.tensor.matmul(pn(T), T.eyeb[:], T.oh[:, cols], True, False)], nm("oh") + ["eyeb"], [], banks=[PO])
             for a in (0, 1):
-                op(V, "ct%d" % a + Z, lambda g, T, x, a=a: [
-                    g.vector.tensor_tensor(T["cm" + Z][:, a:N:2], T["gt" + Z][:, a:N:2], T[PV][:, a:N:2], A.is_lt)], nm("gt"), nm("cm%d" % a), banks=[PV])
+                op(V, "ct%d" % a, lambda g, T, x, a=a: [
+                    g.vector.tensor_tensor(T["cm" + Z][:, a:N:2], T["gt" + Z][:, a:N:2], T[PV][:, a:N:2], A.is_lt)],
+                   nm("gt0", "gt1"), nm("cm%d" % a), banks=[PV])
             for a in (0, 1):
-                def cnt(g, T, x, a=a, pn=pn):
-                    return [g.tensor.matmul(pn(T), T.sr[:, 128 * i:128 * i + 128], T["cm" + Z][:, i:N:16], False, i == 15) for i in range(a, 16, 2)]
-                op(P, "pn%d" % a + Z, cnt, nm("cm%d" % a) + ["sra", "srb"], [], 8, banks=[PO])
-            op(S, "of" + Z, lambda g, T, x, pn=pn: [g.scalar.activation(T["off" + Z][:], pn(T), CPY)], [], nm("off"), banks=[PO])
+                op(P, "pn%d" % a, lambda g, T, x, a=a: [
+                    g.tensor.matmul(pn(T), T.sr[:, 15 - i:143 - i], T["cm" + Z][:, i:N:16], False, i == 15) for i in range(a, 16, 2)],
+                   nm("cm%d" % a) + ["sr"], [], 8, banks=[PO])
+            op(S, "of", lambda g, T, x: [g.scalar.activation(T.off[:, cols], pn(T), CPY)], [], nm("off"), banks=[PO])
             to = "oh" if r < RO - 1 else "ob"
-            op(S, "ob" + Z, lambda g, T, x, pn=pn, to=to: [g.scalar.activation(T[to][:, cols], pn(T), CPY)], [], nm(to), banks=[PO])
+            op(S, "ob", lambda g, T, x, to=to: [g.scalar.activation(T[to][:, cols], pn(T), CPY)], [], nm(to), banks=[PO])
             for a in (0, 1):
-                def gx(g, T, x, a=a):
-                    return [g.scalar.activation(T["ga" + Z][:, a * H:a * H + H], T.ti[:, 0:W].indirect(T["off" + Z][:, a * L // 2:a * L // 2 + L // 2]), CPY, scale=T.sc[:])]
-                op(S, "ga%d" % a + Z, gx, ["ti", "sc"] + nm("off"), nm("ga%d" % a))
+                gather("ga%d" % a, "ga", "ti", a, ["ti", "sc"], scale="sc")
             for a in (0, 1):
                 h = slice(a * H, a * H + H)
-                op(V, "ca%d" % a + Z, lambda g, T, x, h=h: [
+                op(V, "ca%d" % a, lambda g, T, x, h=h: [
                     g.vector.tensor_tensor(T["cc" + Z][:, h], T["ga" + Z][:, h], T[PV][:, h], A.is_lt)], nm("ga%d" % a), nm("cc%d" % a), banks=[PV])
-                op(P, "dd%d" % a + Z, lambda g, T, x, h=h: [g.tensor.matmul(T[PO][:, h], T.dm[:], T["cc" + Z][:, h], True, True)],
+            for a in (0, 1):
+                h = slice(a * H, a * H + H)
+                op(P, "dd%d" % a, lambda g, T, x, h=h: [g.tensor.matmul(T[PO][:, h], T.dm[:], T["cc" + Z][:, h], True, True)],
                    nm("cc%d" % a) + ["dm"], [], banks=[PO])
-            for a, t in ((0, "ppA"), (1, "ppB")):
-                op(V, "mu%d" % a + Z, lambda g, T, x, a=a: [
-                    g.vector.tensor_tensor(T["pp" + Z][:, a:N:2], T["ga" + Z][:, a:N:2], T[PO][:, a:N:2], A.mult)], nm("ga0", "ga1"), nm(t), banks=[PO])
+            for a in (0, 1):
+                op(V, "mu%d" % a, lambda g, T, x, a=a: [g.vector.tensor_tensor(T["pp" + Z][:, a:N:2], T["ga" + Z][:, a:N:2], T[PO][:, a:N:2], A.mult)],
+                   nm("ga0", "ga1"), nm("pp%d" % a), banks=[PO])
+            sums("pp")
             if r < RO - 1:
                 send(r + 1)
-            if r == 1:
-                hits(q, 0, "pf0")
-                op(P, "h1" + Z, lambda g, T, x: [g.tensor.matmul(T.pf0[:, 0:128], T["hv" + Z][:, 0:128], T.eyeb[:], True, True)],
-                   nm("hv0") + ["eyeb"], [], banks=["pf0"])
-                op(S, "h2" + Z, lambda g, T, x: [g.scalar.activation(T["fa" + Z][:], T.pf0[:, 0:128], CPY)], [], nm("fa"), banks=["pf0"])
-        sums()
-        op(V, "e1" + Z, lambda g, T, x: [g.vector.tensor_copy(T["yp" + Z][:, 0:L], T[PV][:, 0:L])], [], nm("ypa"), banks=[PV])
-        op(V, "e2" + Z, lambda g, T, x: [g.vector.tensor_tensor(T["yp" + Z][:, L:2 * L], T[PV][:, 0:L], T["yp" + Z][:, 0:L], A.subtract)],
-           nm("ypa"), nm("ypb"), banks=[PV])
-        op(P, "e3" + Z, lambda g, T, x: [g.tensor.matmul(T[PO][0:2 * L, 0:128], T["yp" + Z][:], T.eyeb[:], True, True)],
-           nm("ypa", "ypb") + ["eyeb"], [], banks=[PO])
-        op(S, "e4" + Z, lambda g, T, x: [g.scalar.activation(T["ft" + Z][0:2 * L, :], T[PO][0:2 * L, 0:128], CPY)], [], nm("ft"), banks=[PO])
-        op(P, "e5" + Z, conv(lambda T: T[PO][:, 384:384 + L], [("ft" + Z, 0, 2 * L)]), nm("ft") + CV, [], RH, banks=[PO])
-        op(V, "e6" + Z, lambda g, T, x: [g.vector.tensor_scalar(T.oc[:, cols], T[PO][:, 384:384 + L], 32.0, None, A.mult)], [], nm("oc"), banks=[PO])
+        op(V, "e1", lambda g, T, x: [g.vector.tensor_copy(T["yp" + Z][:, 0:F], T[PV][:, 0:F])], [], nm("yp"), banks=[PV])
+        op(V, "e2", lambda g, T, x: [g.vector.tensor_tensor(T["yp" + Z][:, F:2 * F], T[PV][:, 0:F], T["yp" + Z][:, 0:F], A.subtract)],
+           nm("yp"), nm("yq"), banks=[PV])
+        op(P, "e3", lambda g, T, x: [g.tensor.matmul(T[PO][0:64, 0:128], T["yp" + Z][:], T.eyeb[:], True, True)], nm("yp", "yq") + ["eyeb"], [], banks=[PO])
+        op(S, "e4", lambda g, T, x: [g.scalar.activation(T["ft" + Z][0:64, :], T[PO][0:64, 0:128], CPY)], [], nm("ft"), banks=[PO])
+        op(P, "e5", lambda g, T, x: [g.tensor.matmul(T[PO][:, 384:384 + L], T.cv[0:64, 12 - 4 * w:140 - 4 * w], T["ft" + Z][0:64, w:128:4], w == 0, w == 3)
+                                     for w in range(4)], nm("ft") + ["cv"], [], 4, banks=[PO])
+        op(V, "e6", lambda g, T, x: [g.vector.tensor_copy(T["oc" + Z][:], T[PO][:, 384:384 + L])], [], nm("oc"), banks=[PO])
+        store("yb", q, lambda T: T.ob[:, cols], "ob" + Z)
+        store("yc", q, lambda T: T["oc" + Z][:], "oc" + Z)
 
     def last(q):
-        cols = slice(L * q, L * q + L)
         Z = str(q)
-        hits(q, 2, "pf0")
-        op(P, "h1" + Z, lambda g, T, x: [g.tensor.matmul(T.pf1[:, 0:128], T["hv" + Z][:, 128:256], T.eyeb[:], True, True),
-                                         g.tensor.matmul(T.pf1[:, 128:256], T["hf" + Z][:], T.eyeb[:], True, True)],
-           ["hv2" + Z, "hf0" + Z, "hf2" + Z, "eyeb"], [], 2, banks=["pf1"])
-        op(S, "h2" + Z, lambda g, T, x: [g.scalar.activation(T["fb" + Z][:], T.pf1[:, 0:256], CPY)], [], ["fb" + Z], banks=["pf1"])
-        c1 = conv(lambda T: T.pf1[:, 384:384 + L], [("fa" + Z, 0, 128), ("fb" + Z, 0, 128)])
-        c2 = conv(lambda T: T.pf1[:, 384 + L:384 + 2 * L], [("fb" + Z, 128, 128)])
-        op(P, "h3" + Z, lambda g, T, x: c1(g, T, x) + c2(g, T, x), ["fa" + Z, "fb" + Z] + CV, [], 3 * RH, banks=["pf1"])
-        op(S, "h4" + Z, lambda g, T, x: [g.scalar.activation(T["oo" + Z][:, 0:L], T.pf1[:, 384:384 + L], CPY, scale=128.0),
-                                         g.scalar.activation(T["oo" + Z][:, L:2 * L], T.pf1[:, 384 + L:384 + 2 * L], CPY, scale=4.0)],
-           [], ["oo" + Z], 2, banks=["pf1"])
-        for y, src, tok in (("yb", lambda T: T.ob[:, cols], "ob"), ("ys", lambda T: T["oo" + Z][:, 0:L], "oo"),
-                            ("yh", lambda T: T["oo" + Z][:, L:2 * L], "oo"), ("yc", lambda T: T.oc[:, cols], "oc")):
-            op("sync", "out", lambda g, T, x, y=y, src=src: [g.sync.dma_start(T[y][:, cols], src(T))], [tok + Z], [], 16)
+        at[:] = [q, RO - 1]
+        hits(q, 2)
+        op(P, "h3", lambda g, T, x: [
+            g.tensor.matmul(T.pf1[:, 0:3, 0:L], T.cv[:, 12 - 4 * w:140 - 4 * w], T["fa" + Z][:, w:384:4], w == 0, w == 3)
+            for w in range(4)], ["fa0" + Z, "fa2" + Z, "cv"], [], 4, banks=["pf1"])
+        op(S, "h4", lambda g, T, x: [g.scalar.activation(T["oo" + Z][:, 0:L], T.pf1[:, 0, 0:L], CPY),
+                                     g.scalar.activation(T["oo" + Z][:, L:2 * L], T.pf1[:, 2, 0:L], CPY, scale=0.03125)], [], ["oo" + Z], 2, banks=["pf1"])
+        op(V, "h5", lambda g, T, x: [g.vector.tensor_tensor(T["oo" + Z][:, 2 * L:3 * L], T["oo" + Z][:, 0:L], T.pf1[:, 1, 0:L], A.add)],
+           ["oo" + Z], ["os" + Z], banks=["pf1"])
+        store("yh", q, lambda T: T["oo" + Z][:, L:2 * L], "oo" + Z)
+        store("ys", q, lambda T: T["oo" + Z][:, 2 * L:3 * L], "os" + Z)
     for q in range(NC):
         chunk(q)
     for q in range(NC):
@@ -298,10 +268,28 @@ def build():
     return ops
 
 
+def schedule(ops, key):
+    after = {o["n"]: [] for o in ops}
+    for o in ops:
+        for d in o["deps"] | o["order"]:
+            after[d].append(o["n"])
+    left = {o["n"]: len(o["deps"] | o["order"]) for o in ops}
+    ready, order = [n for n in left if left[n] == 0], []
+    while ready:
+        n = min(ready, key=lambda k: (key[k], k))
+        order.append(n)
+        ready.remove(n)
+        for k in after[n]:
+            left[k] -= 1
+            if left[k] == 0:
+                ready.append(k)
+    return order
+
+
 def plan():
-    ops, order = build(), SEQ
+    ops = build()
+    order = schedule(ops, KEY or list(range(len(ops))))
     pos = {i: z for z, i in enumerate(order)}
-    assert len(pos) == len(ops) and all(pos[d] < pos[o["n"]] for o in ops for d in o["deps"] | o["order"])
     known, clos, waits, waited = {}, {}, {}, set()
     for i in order:
         o = ops[i]
@@ -325,7 +313,7 @@ def plan():
     cnt, val = {}, {}
     for i in order:
         o = ops[i]
-        if o["q"] != "remote" and o["sem"] is not None and (i in waited or o["sem"] == "out"):
+        if o["q"] != "remote" and o["ninc"] and (i in waited or o["sem"] == "out"):
             cnt[o["sem"]] = cnt.get(o["sem"], 0) + o["ninc"]
             val[i] = cnt[o["sem"]]
     return ops, order, waits, val, cnt
@@ -356,7 +344,6 @@ def rank_program(g, core, T, topo):
     inn = sum(len(masks[c]) for c in peers)
     x = {"rank": rank, "peers": [(topo.addr(c, core), sum(1 << k for k in masks[c])) for c in far + near]}
     queue = {"sync": g.sync, "scalar": g.scalar, "vector": g.vector, "tensor": g.tensor, "gpsimd": g}
-    sends = 0
     for i in ORDER:
         o = OPS[i]
         if o["q"] == "remote":
@@ -366,10 +353,8 @@ def rank_program(g, core, T, topo):
             p = OPS[d]
             e.wait_ge(T.sem[p["sem"]], inn if p["q"] == "remote" else VAL[d])
         ins = o["emit"](g, T, x)
-        if o["sem"] is None:
-            sends += 1
         if i in VAL:
             for k in ins:
                 k.then_inc(T.sem[o["sem"]], o["ninc"] // len(ins))
     g.sync.wait_ge(T.sem["out"], CNT["out"])
-    g.wait_ge(T.sem["sent"], inn * sends)
+    g.wait_ge(T.sem["sent"], inn * NC * RO)

@@ -8,7 +8,9 @@ N = W // NC
 L, H, F = N // 16, N // 2, 32
 ZV, ZS = 704, 1216
 TA = 24
-SEQ = [0,1,5,2,3,4,9,11,10,15,17,24,30,16,18,6,26,25,32,7,8,33,19,12,320,40,176,13,27,39,34,35,328,22,36,321,183,322,323,23,177,178,179,324,20,180,14,37,28,38,41,42,44,45,43,46,47,181,182,185,186,325,188,189,187,31,326,190,191,48,327,184,49,29,50,330,329,52,332,53,333,331,334,335,192,51,193,194,196,197,21,54,55,336,195,56,337,58,198,338,60,340,59,57,61,199,62,339,342,200,341,63,343,64,202,203,344,345,201,346,65,204,205,66,67,206,207,347,71,216,215,72,68,348,208,209,349,69,350,210,211,351,70,212,352,353,354,355,213,356,357,214,358,73,74,76,75,77,79,78,80,81,360,105,218,217,219,82,83,220,221,84,223,222,85,86,224,87,359,250,225,106,88,362,361,363,364,365,226,367,366,227,107,368,90,369,91,228,229,230,231,89,232,249,92,93,370,94,95,371,372,373,374,375,234,233,235,376,96,236,97,237,393,378,379,377,108,394,104,103,392,247,98,238,99,239,100,240,241,380,242,243,382,101,381,383,244,384,102,245,385,386,387,246,388,389,109,110,112,111,113,115,114,390,253,254,116,117,391,248,257,256,255,258,259,118,260,119,251,120,121,397,398,400,401,399,122,261,123,262,402,403,404,263,264,266,265,252,124,126,128,405,127,267,268,125,129,406,130,395,131,407,270,271,408,410,409,411,412,396,269,132,133,272,134,413,414,415,273,135,274,275,136,276,277,416,278,279,418,137,417,280,419,420,421,138,281,422,423,282,424,141,142,144,145,143,425,426,146,147,464,148,140,283,139,284,465,149,285,286,289,288,287,150,152,291,290,466,151,154,292,153,155,427,467,428,293,156,294,473,429,430,432,433,431,434,435,296,297,295,468,436,298,299,157,158,159,437,469,300,483,474,482,160,438,161,470,440,441,439,162,475,163,442,443,301,302,303,476,444,164,304,305,165,166,306,307,308,477,167,310,446,447,478,445,309,448,311,450,449,168,479,312,169,313,451,452,453,170,314,484,454,455,456,457,485,315,171,486,487,172,458,316,173,488,317,459,460,461,462,174,480,472,471,481,318,489,175,490,319,463]
+FIN = (2,)
+H2 = "scalar"
+SEQ = [0,1,5,2,3,4,6,7,8,10,9,19,16,18,17,31,20,14,36,11,38,41,39,42,37,15,23,24,43,26,40,12,202,27,28,365,13,21,364,367,368,22,369,201,204,205,206,44,25,366,203,30,45,372,47,209,35,32,210,373,207,208,29,34,46,370,371,48,49,51,52,50,53,54,211,55,212,214,215,56,221,213,375,374,217,59,216,60,61,62,376,378,218,377,58,63,64,65,66,384,219,220,380,379,57,381,67,382,222,226,223,227,224,228,225,69,70,68,385,71,386,387,72,229,388,230,389,73,74,390,76,391,231,232,233,392,75,393,394,395,396,77,234,78,235,79,236,80,239,84,85,33,248,411,410,247,237,81,240,241,397,238,82,83,242,243,96,399,244,398,400,402,401,245,246,403,404,383,405,406,407,408,409,86,87,89,90,88,91,92,93,249,422,94,250,253,252,251,97,98,99,254,255,100,256,412,413,415,416,414,101,102,103,104,257,259,105,106,107,108,417,260,261,418,262,264,419,263,109,110,265,266,420,267,423,424,425,111,268,269,270,271,114,427,428,112,115,426,116,272,273,429,113,430,117,118,274,119,275,277,278,279,431,433,432,434,435,122,123,448,449,285,286,276,280,281,437,282,436,438,440,120,121,439,441,442,95,443,444,445,124,125,127,128,126,258,129,130,421,131,283,284,132,287,288,291,290,289,135,292,136,137,293,138,446,447,134,139,140,294,296,450,451,141,142,295,297,454,453,452,298,455,299,300,456,301,143,460,302,303,304,305,457,458,145,146,306,144,147,307,308,309,148,461,462,149,152,465,466,463,464,150,153,154,310,311,467,468,151,155,469,156,312,315,157,313,314,470,471,472,316,317,473,487,161,486,323,160,318,319,474,320,158,159,321,322,475,172,478,476,477,479,480,481,482,483,484,485,162,163,166,165,164,167,168,169,133,459,171,498,170,325,326,173,174,175,327,176,328,329,331,330,488,332,489,491,492,334,493,490,522,324,523,524,177,178,179,180,525,335,181,529,333,336,184,183,530,340,337,494,338,339,341,495,185,342,343,496,186,499,500,501,182,531,344,526,346,347,502,187,188,503,504,505,506,189,190,348,349,497,507,345,532,191,192,350,508,509,536,533,510,511,351,537,513,352,353,512,514,354,355,516,193,356,538,539,357,194,517,540,515,358,195,518,196,359,197,360,519,198,361,527,542,541,520,534,535,528,199,362,521,200,363]
 KEY = {n: z for z, n in enumerate(SEQ)}
 
 SCRATCH = {
@@ -16,26 +18,28 @@ SCRATCH = {
     "stb": ("sbuf", [128, W // 16], "int32"), "off": ("sbuf", [128, W // 16], "uint16"),
     "zz": ("sbuf", [128, ZS - ZV], "bfloat16"), "dif": ("sbuf", [128, 128], "float32"),
     "indb": ("sbuf", [128, 8], "bfloat16"), "indf": ("sbuf", [128, 8], "float32"), "zt": ("sbuf", [128, 36], "float32"),
-    "sg": ("sbuf", [128, 8], "float32"), "sc": ("sbuf", [128, 1], "float32"), "cab": ("sbuf", [128, 1], "float32"),
+    "sg": ("sbuf", [128, 8], "float32"), "sc": ("sbuf", [128, 1], "float32"), "cw": ("sbuf", [128, 32], "bfloat16"),
     "eyeb": ("sbuf", [128, 128], "bfloat16"), "dm": ("sbuf", [128, 128], "bfloat16"), "sr": ("sbuf", [128, 144], "bfloat16"),
-    "bs": ("sbuf", [128, 64], "bfloat16"), "bc": ("sbuf", [128, 512], "bfloat16"), "cv": ("sbuf", [128, 144], "bfloat16"),
+    "bs": ("sbuf", [128, 64], "bfloat16"), "b2": ("sbuf", [128, 16], "bfloat16"), "bc": ("sbuf", [128, 512], "bfloat16"), "cx": ("sbuf", [128, 32], "bfloat16"),
+    "cv": ("sbuf", [128, 144], "bfloat16"), "cu": ("sbuf", [128, 144], "bfloat16"),
     "oh": ("sbuf", [128, W // 16], "float16"), "ob": ("sbuf", [128, W // 16], "float32"),
-    "pf0": ("psum", [128, 4, 128], "float32"), "pf1": ("psum", [128, 4, 128], "float32"),
+    "pf0": ("psum", [128, 4, 128], "float32"), "pf1": ("psum", [128, 512], "float32"),
 }
 for _q in range(NC):
     for _k, _s, _d in (("rc", [128, RO * NR * F], "float32"), ("xx", [128, 2 * F], "float32"), ("xn", [128, 2 * F], "float32"),
-                       ("mx", [128, F], "float32"), ("mn", [128, F], "float32"), ("pc", [128, RO, 3 * F], "float16"),
-                       ("lt", [128, 128], "float16"), ("gt", [128, N], "float32"), ("cm", [128, N], "bfloat16"),
-                       ("ga", [128, N], "float32"), ("cc", [128, N], "bfloat16"), ("pp", [128, N], "float32"),
-                       ("hf", [128, RO, F], "bfloat16"), ("hv", [128, RO, 2, F], "float16"), ("fa", [128, 384], "float16"),
-                       ("oo", [128, 3 * L], "float32"), ("oc", [128, L], "float32"), ("ft", [128, 128], "float16"), ("yp", [128, 2 * F], "float16")):
+                       ("mx", [128, F], "float32"), ("mn", [128, F], "float32"), ("pc", [128, RO, 4, 4, 8], "float16"),
+                       ("lt", [128, 2, 2, 32], "float16"), ("gt", [128, N], "float32"), ("cm", [128, N], "bfloat16"),
+                       ("ga", [128, N], "float32"), ("cc", [128, N], "bfloat16"), ("pp", [128, L, 4, 4], "float32"),
+                       ("hf", [128, 2, 128], "bfloat16"), ("hv", [128, 2, 2 * RO, 16], "float16"), ("fa", [128, 512], "float16"),
+                       ("oo", [128, 2 * L], "float32"), ("oc", [128, 4 * L], "float32"), ("ft", [128, 128], "float16"), ("yp", [128, 2 * F], "float16")):
         SCRATCH["%s%d" % (_k, _q)] = ("sbuf", _s, _d)
-    SCRATCH["pv%d" % _q] = ("psum", [128, 512], "float32")
+    SCRATCH["pv%d" % _q] = ("psum", [128, 2, H], "float32")
     SCRATCH["po%d" % _q] = ("psum", [128, 512], "float32")
 
 SHARE = {"ct0": "va", "ca0": "va", "mu0": "va", "ct1": "vb", "ca1": "vb", "mu1": "vb", "pn0": "ta", "dd0": "ta", "ps0": "ta",
-         "pn1": "tc", "dd1": "tc", "ps1": "tc", "pt": "tp", "pb": "tp", "e3": "tp", "e5": "tp", "xx": "vx", "lo": "vx", "s0": "vx",
-         "e1": "vo", "e2": "vo", "e6": "vo", "hv": "vh", "h5": "vh", "h1": "th", "h3": "th", "hf": "sh", "h2": "sh", "h4": "sh", "e4": "sh"}
+         "ct2": "va", "ct3": "vb", "pn2": "ta", "pn3": "tc", "mu2": "va", "ps2": "ta",
+         "pn1": "tc", "dd1": "tc", "ps1": "tc", "pb": "tp", "e3": "tp", "e5": "tp", "xx": "vx", "lo": "vx", "vt": "vx", "s0": "vx",
+         "e1": "vo", "e2": "vo", "e6": "vo", "hv": "vh", "h1": "th", "h3": "th", "hf": "sh", "h4": "sh", "e4": "sh"}
 
 
 def build():
@@ -85,12 +89,10 @@ def build():
 
     def fill(name, buf, v):
         op(V, name, lambda g, T, x: [g.vector.memset(T[buf][:], v)], [], [buf])
-    fill("c_m1", "indb", 1.0)
-    fill("c_m2", "sg", 1.0)
-    fill("c_m3", "sr", 0.0)
-    fill("c_m4", "cv", 0.0)
-    fill("c_m5", "zt", 0.0)
-    op(V, "c_m7", lambda g, T, x: [g.vector.memset(T.cab[0:64, :], 32.0), g.vector.memset(T.cab[64:128, :], 0.5)], [], ["cab"], 2)
+    for z, (buf, v) in enumerate((("indb", 1.0), ("sg", 1.0), ("sr", 0.0), ("cv", 0.0), ("zt", 0.0), ("cu", 0.0))):
+        fill("c_m%d" % z, buf, v)
+    op(V, "c_m7", lambda g, T, x: [g.vector.memset(T.cw[:, a:b], v) for a, b, v in ((0, 16, 32.0), (16, 24, 0.5), (24, 32, 0.0))]
+       + [g.vector.memset(T.cx[:], 0.0)], [], ["cw", "cx"], 4)
 
     def sel(name, buf, pat, cmp, v, base, cm=1):
         op(G, name, lambda g, T, x: [g.affine_select(T[buf][:], T[buf][:], pat, cmp, v, base, cm)], [buf], [buf])
@@ -99,35 +101,36 @@ def build():
     sel("c_sg", "sg", [[-16, 8]], A.not_equal, -1.0, -15)
     op(G, "c_df", lambda g, T, x: [g.iota(T.dif[:], [[1, 128]], 0, -1, allow_small_or_imprecise_dtypes=True)], [], ["dif"])
     op(V, "c_ey", lambda g, T, x: [g.vector.tensor_scalar(T.eyeb[:], T.dif[:], 0.0, None, A.is_equal)], ["dif"], ["eyeb"])
-    op(V, "c_d1", lambda g, T, x: [g.vector.tensor_tensor(T.dm[:, 1:128], T.eyeb[:, 0:127], T.eyeb[:, 1:128], A.subtract)], ["eyeb"], ["dm"])
+
+    def two(name, out, a, b, alu, reads, writes):
+        op(V, name, lambda g, T, x: [g.vector.tensor_tensor(out(T), a(T), b(T), alu)], reads, writes)
+
+    def fold(name, to, buf, n):
+        two(name, lambda T: T[to][:, 0:n], lambda T: T[buf][:, 0:n], lambda T: T[buf][:, n:2 * n], A.add, [buf], [to])
+    two("c_d1", lambda T: T.dm[:, 1:128], lambda T: T.eyeb[:, 0:127], lambda T: T.eyeb[:, 1:128], A.subtract, ["eyeb"], ["dm"])
     op(V, "c_d2", lambda g, T, x: [g.vector.tensor_tensor(T.dm[:, 0:128:16], T.eyeb[:, 15:128:16], T.eyeb[:, 0:128:16], A.subtract),
                                    g.vector.tensor_scalar(T.dm[:, 15:128:16], T.eyeb[:, 14:128:16], -1.0, None, A.mult)], ["eyeb"], ["dm"], 2)
-    op(V, "c_b1", lambda g, T, x: [g.vector.tensor_tensor(T.bs[:], T.eyeb[:, 0:64], T.eyeb[:, 64:128], A.add)], ["eyeb"], ["bs"])
-    op(V, "c_b2", lambda g, T, x: [g.vector.tensor_tensor(T.bs[:, 0:32], T.bs[:, 0:32], T.bs[:, 32:64], A.add)], ["bs"], ["bs"])
+    fold("c_b1", "bs", "eyeb", 64)
+    fold("c_b2", "bs", "bs", 32)
+    fold("c_b6", "b2", "bs", 16)
+    two("c_b3", lambda T: T.cw[:], lambda T: T.cw[:], lambda T: T.bs[:, 0:32], A.mult, ["bs", "cw"], ["cw"])
+    fold("c_b4", "cw", "cw", 16)
+    op(V, "c_b5", lambda g, T, x: [g.vector.tensor_tensor(T.cx[32 * b:32 * b + 32, 8 * b:8 * b + 8], T.cw[32 * b:32 * b + 32, 0:8], T.cw[32 * b:32 * b + 32, 8:16], A.add)
+                                   for b in range(4)], ["cw"], ["cx"], 4)
+    op(V, "c_bc", lambda g, T, x: [g.vector.tensor_copy(T.bc[:, i:512:16], T.cx[:]) for i in range(16)], ["cx"], ["bc"], 16)
     op(V, "c_sc", lambda g, T, x: [g.vector.tensor_reduce(T.sc[:], T.sg[:], AxisListType.X, A.min)], ["sg"], ["sc"])
     op(S, "c_if", lambda g, T, x: [g.scalar.activation(T.indf[:], T.indb[:], CPY, scale=0.03125)], ["indb"], ["indf"])
     op(S, "c_sr", lambda g, T, x: [g.scalar.activation(T.sr[:, 15:143:16], T.indb[:], CPY)], ["indb"], ["sr"])
     op(S, "c_zt", lambda g, T, x: [g.scalar.activation(T.zt[:, 3:35:4], T.indb[:], CPY)], ["indb"], ["zt"])
-    op(V, "c_bc", lambda g, T, x: [g.vector.tensor_scalar(T.bc[:, i:512:16], T.bs[:, 0:F], T.cab[:], None, A.mult) for i in range(16)],
-       ["bs", "cab"], ["bc"], 16)
-    op(S, "c_cv", lambda g, T, x: [g.scalar.activation(T.cv[:, 12 + k:140:16], T.bs[:, 8 * k:8 * k + 8], CPY, scale=32.0) for k in range(4)],
-       ["bs"], ["cv"], 4)
+    op(S, "c_cu", lambda g, T, x: [g.scalar.activation(T.cu[:, 14 + k:142:16], T.b2[:, 8 * k:8 * k + 8], CPY, scale=32.0) for k in range(2)], ["b2"], ["cu"], 2)
+    op(S, "c_cv", lambda g, T, x: [g.scalar.activation(T.cv[:, 12 + k:140:16], T.bs[:, 8 * k:8 * k + 8], CPY, scale=32.0) for k in range(4)], ["bs"], ["cv"], 4)
     op(V, "c_oi", lambda g, T, x: [g.vector.tensor_copy(T.off[:], T.stb[:])], ["stb"], ["off%d" % q for q in range(NC)])
     op(V, "c_ob", lambda g, T, x: [g.vector.tensor_copy(T.oh[:], T.stb[:])], ["stb"], ["oh%d" % q for q in range(NC)])
 
-    def hits(q, ra):
-        Z, n, rr = str(q), str(ra), slice(ra, ra + 2)
-        pb = "pf1" if ra else "pf0"
-        op(V, "hv", lambda g, T, x: [g.vector.tensor_tensor(T["hv" + Z][:, rr, a, :], T["pc" + Z][:, rr, a * F:a * F + F], T["pc" + Z][:, rr, 2 * F:3 * F], A.mult)
-                                     for a in (0, 1)],
-           ["pc%d_%d_%s" % (q, r, t) for r in (ra, ra + 1) for t in "hln"], ["hv" + n + Z], 2)
-        op(S, "hf", lambda g, T, x: [g.scalar.activation(T["hf" + Z][:, rr, :], T["pc" + Z][:, rr, 2 * F:3 * F], CPY)],
-           ["pc%d_%d_n" % (q, r) for r in (ra, ra + 1)], ["hf" + n + Z])
-        src = [lambda T: T["hv" + Z][:, rr, :, :]] + ([lambda T: T["hf" + Z][:]] if ra else [])
-        op(P, "h1", lambda g, T, x: [g.tensor.matmul(T[pb][:, i, :], b(T), T.eyeb[:], True, True) for i, b in enumerate(src)],
-           ["hv" + n + Z, "hf0" + Z, "hf2" + Z, "eyeb"], [], len(src), banks=[pb])
-        op(S, "h2", lambda g, T, x: [g.scalar.activation(T["fa" + Z][:, 64 * ra:64 * ra + 128 * len(src)], T[pb][:, 0:len(src), :], CPY)],
-           [], ["fa" + n + Z], banks=[pb])
+    def hits(q, r):
+        Z = str(q)
+        op(V, "hv", lambda g, T, x: [g.vector.tensor_tensor(T["hv" + Z][:, :, 2 * r + a, :], T["pc" + Z][:, r, :, a, :], T["pc" + Z][:, r, :, 2, :], A.mult)
+                                     for a in (0, 1)], ["pc%d_%d_%s" % (q, r, t) for t in "hln"], ["hv%d" % r + Z], 2)
 
     def store(y, q, src, tok):
         op("sync", "out", lambda g, T, x: [g.sync.dma_start(T[y][:, L * q:L * q + L], src(T))], [tok], [], 16)
@@ -153,19 +156,20 @@ def build():
         def rc(T, r, a, b):
             return T["rc" + Z][:, (r * NR + a) * F:(r * NR + b) * F]
 
-        def sums(b):
-            for a in (0, 1):
-                op(P, "ps%d" % a, lambda g, T, x, a=a: [
-                    g.tensor.matmul(T[PV][:, 8 * k:8 * k + 8], T[b + Z][:, k:N:4], T.indf[:], True, True) for k in (a, a + 2)],
-                   (nm("ga0", "ga1") if b == "ga" else nm(b + str(a))) + ["indf"], [], 2, banks=[PV])
+        def sums(a, b):
+            def block(T, k):
+                return T["ga" + Z][:, a * H + k:a * H + H:2] if b == "ga" else T["pp" + Z][:, a * L // 2:a * L // 2 + L // 2, :, k:4:2]
+            op(P, "ps%d" % a, lambda g, T, x: [
+                g.tensor.matmul(T[PO][:, H + 16 * a + 8 * k:H + 16 * a + 8 * k + 8], block(T, k), T.indf[:], True, True) for k in (0, 1)],
+               nm(b + str(a)) + ["indf"], [], 2, banks=[PO])
 
         def send(r):
             def s0(g, T, x):
-                o, i = rc(T, r, x["rank"], x["rank"] + 1), T[PV][:, 0:F]
+                o, i = rc(T, r, x["rank"], x["rank"] + 1), T[PO][:, H:H + F]
                 if x["rank"] == 1:
                     return [g.vector.tensor_scalar(o, i, (END - 0.25) / 32.0, None, A.min)]
                 return [g.vector.tensor_copy(o, i)]
-            op(V, "s0", s0, [], ["own%d_%d" % (q, r)], banks=[PV])
+            op(V, "s0", s0, [], ["own%d_%d" % (q, r)], banks=[PO])
 
             def ex(g, T, x):
                 s = rc(T, r, x["rank"], x["rank"] + 1)
@@ -176,48 +180,43 @@ def build():
             k = op(G, "ex", ex, ["own%d_%d" % (q, r)], [], 0)
             ops[op("remote", "ar", None, [], ["arr%d_%d" % (q, r)], 0, after=(k,))]["sem"] = "ar%d_%d" % (q, r)
 
-        sums("ga")
+        op(V, "pz", lambda g, T, x: [g.vector.memset(T["pc" + Z][:, :, :, 3, :], 0.0), g.vector.memset(T["hf" + Z][:, :, 64:128], 0.0)], [], nm("pz"), 2)
+        sums(0, "ga")
+        sums(1, "ga")
         send(0)
         for r in range(RO):
             at[1] = r - 1
             for a in (0, 1):
                 gather("gt%d" % a, "gt", "tt", a, ["tta", "ttb"])
-            if r == 2:
-                hits(q, 0)
             at[1] = r
             src = ["arr%d_%d" % (q, r), "own%d_%d" % (q, r)]
-            pc = lambda T, a, b, r=r: T["pc" + Z][:, r, a * F:b * F]
             pt = "pc%d_%d_" % (q, r)
-
-            def pair(name, out, a, b, alu, reads, writes):
-                op(V, name, lambda g, T, x: [g.vector.tensor_tensor(out(T), a(T), b(T), alu)], reads, writes)
             whole = lambda b: lambda T: T[b + Z][:]
             part = lambda b, a: lambda T: T[b + Z][:, a * F:a * F + F]
             ranks = lambda a, r=r: lambda T: rc(T, r, a, a + 2)
-            plane = lambda a, pc=pc: lambda T: pc(T, a, a + 1)
-            pair("xx", whole("xx"), ranks(0), ranks(2), A.max, src, nm("xx"))
-            pair("xn", whole("xn"), ranks(0), ranks(2), A.min, src, nm("xn"))
-            pair("mn", whole("mn"), part("xn", 0), part("xn", 1), A.min, nm("xn"), nm("mn"))
-            pair("mx", whole("mx"), part("xx", 0), part("xx", 1), A.max, nm("xx"), nm("mx"))
-            pair("hi", plane(0), part("xx", 0), part("xx", 1), A.max, nm("xx"), [pt + "h"])
-            pair("lo", plane(1), whole("mx"), plane(0), A.subtract, nm("mx") + [pt + "h"], [pt + "l"])
-            pair("eq", plane(2), whole("mx"), whole("mn"), A.is_equal, nm("mx", "mn"), [pt + "n"])
-            op(P, "pt", lambda g, T, x, pc=pc: [g.tensor.matmul(T[PO][0:96, 0:128], pc(T, 0, 3), T.eyeb[:], True, True)],
-               [pt + "h", pt + "l", pt + "n", "eyeb"], [], banks=[PO])
-            op(S, "ev", lambda g, T, x: [g.scalar.activation(T["lt" + Z][0:96, :], T[PO][0:96, 0:128], CPY)], [], nm("lt"), banks=[PO])
+            plane = lambda a, r=r: lambda T: T["pc" + Z][:, r, :, a, :]
+            two("xx", whole("xx"), ranks(0), ranks(2), A.max, src, nm("xx"))
+            two("xn", whole("xn"), ranks(0), ranks(2), A.min, src, nm("xn"))
+            two("mn", whole("mn"), part("xn", 0), part("xn", 1), A.min, nm("xn"), nm("mn"))
+            two("mx", whole("mx"), part("xx", 0), part("xx", 1), A.max, nm("xx"), nm("mx"))
+            two("hi", plane(0), part("xx", 0), part("xx", 1), A.max, nm("xx"), [pt + "h"])
+            two("lo", plane(1), whole("mx"), plane(0), A.subtract, nm("mx") + [pt + "h"], [pt + "l"])
+            two("eq", plane(2), whole("mx"), whole("mn"), A.is_equal, nm("mx", "mn"), [pt + "n"])
+            op(V, "vt", lambda g, T, x, r=r: [g.vector.transpose(T["lt" + Z][:], T["pc" + Z][:, r])], [pt + "h", pt + "l", pt + "n"] + nm("pz"), nm("lt"))
             op(P, "pb", lambda g, T, x: [
-                g.tensor.matmul(T[PV][:, k:N:4], T.bc[0:96, 128 * k:128 * k + 128], T["lt" + Z][0:96, :], True, True) for k in range(4)],
-               nm("lt") + ["bc"], [], 4, banks=[PV])
+                g.tensor.matmul(T[PV][:, :, 64 * b + k:64 * b + 64:2], T.bc[:, 128 * b:128 * b + 128], T["lt" + Z][:, :, k, :], True, True)
+                for k in (0, 1) for b in range(4)], nm("lt") + ["bc"], [], 8, banks=[PV])
+            hits(q, r)
             pn = lambda T: T[PO][:, 384:384 + L]
             op(P, "bm", lambda g, T, x: [g.tensor.matmul(pn(T), T.eyeb[:], T.oh[:, cols], True, False)], nm("oh") + ["eyeb"], [], banks=[PO])
-            for a in (0, 1):
+            for a in range(4):
                 op(V, "ct%d" % a, lambda g, T, x, a=a: [
-                    g.vector.tensor_tensor(T["cm" + Z][:, a:N:2], T["gt" + Z][:, a:N:2], T[PV][:, a:N:2], A.is_lt)],
+                    g.vector.tensor_tensor(T["cm" + Z][:, a:N:4], T["gt" + Z][:, a:N:4], T[PV][:, :, a:H:4], A.is_lt)],
                    nm("gt0", "gt1"), nm("cm%d" % a), banks=[PV])
-            for a in (0, 1):
+            for a in range(4):
                 op(P, "pn%d" % a, lambda g, T, x, a=a: [
-                    g.tensor.matmul(pn(T), T.sr[:, 15 - i:143 - i], T["cm" + Z][:, i:N:16], False, i == 15) for i in range(a, 16, 2)],
-                   nm("cm%d" % a) + ["sr"], [], 8, banks=[PO])
+                    g.tensor.matmul(pn(T), T.sr[:, 15 - i:143 - i], T["cm" + Z][:, i:N:16], False, i == 15) for i in range(a, 16, 4)],
+                   nm("cm%d" % a) + ["sr"], [], 4, banks=[PO])
             op(S, "of", lambda g, T, x: [g.scalar.activation(T.off[:, cols], pn(T), CPY)], [], nm("off"), banks=[PO])
             to = "oh" if r < RO - 1 else "ob"
             op(S, "ob", lambda g, T, x, to=to: [g.scalar.activation(T[to][:, cols], pn(T), CPY)], [], nm(to), banks=[PO])
@@ -225,42 +224,76 @@ def build():
                 gather("ga%d" % a, "ga", "ti", a, ["ti", "sc"], scale="sc")
             for a in (0, 1):
                 h = slice(a * H, a * H + H)
-                op(V, "ca%d" % a, lambda g, T, x, h=h: [
-                    g.vector.tensor_tensor(T["cc" + Z][:, h], T["ga" + Z][:, h], T[PV][:, h], A.is_lt)], nm("ga%d" % a), nm("cc%d" % a), banks=[PV])
+                op(V, "ca%d" % a, lambda g, T, x, h=h, a=a: [
+                    g.vector.tensor_tensor(T["cc" + Z][:, h], T["ga" + Z][:, h], T[PV][:, a], A.is_lt)], nm("ga%d" % a), nm("cc%d" % a), banks=[PV])
+            if r == RO - 1 and q not in FIN:
+                break
+            for a, b, pd in ((0, PO, lambda T: T[PO][:, 0:H]), (1, PV, lambda T: T[PV][:, 0])):
+                h = slice(a * H, a * H + H)
+                op(P, "dd%d" % a, lambda g, T, x, h=h, pd=pd: [g.tensor.matmul(pd(T), T.dm[:], T["cc" + Z][:, h], True, True)],
+                   nm("cc%d" % a) + ["dm"], [], banks=[b])
+                if a == 1 and r < RO - 1:
+                    for k in (0, 1):
+                        op(V, "mu%d" % (1 + k), lambda g, T, x, k=k: [
+                            g.vector.tensor_tensor(T["pp" + Z][:, L // 2:L, :, k:4:2], T["ga" + Z][:, H + k:N:2], T[PV][:, 0, k:H:2], A.mult)],
+                           nm("ga1"), nm("pp1", "pp2")[k:k + 1], banks=[b])
+                    for k in (0, 1):
+                        op(P, "ps%d" % (1 + k), lambda g, T, x, k=k: [
+                            g.tensor.matmul(T[PO][:, H + 16 + 8 * k:H + 24 + 8 * k], T["pp" + Z][:, L // 2:L, :, k:4:2], T.indf[:], True, True)],
+                           nm("pp1", "pp2")[k:k + 1] + ["indf"], [], banks=[PO])
+                    continue
+                op(V, "mu%d" % a, lambda g, T, x, a=a, h=h, pd=pd: [
+                    g.vector.tensor_tensor(T["pp" + Z][:, a * L // 2:a * L // 2 + L // 2], T["ga" + Z][:, h], pd(T), A.mult)],
+                   nm("ga%d" % a), nm("pp%d" % a, "pp%d" % (2 * a)), banks=[b])
+                if r < RO - 1:
+                    sums(a, "pp")
+                else:
+                    op(P, "ps%d" % a, lambda g, T, x, a=a: [
+                        g.tensor.matmul(T[PO][0:32, H + 64 * a:H + 64 * a + 64], T.zt[:, 3 - k:35 - k],
+                                        T["pp" + Z][:, a * L // 2:a * L // 2 + L // 2, k, :], k == 0, k == 3) for k in range(4)],
+                       nm("pp%d" % a) + ["zt"], [], 4, banks=[PO])
+            if r < RO - 1:
+                send(r + 1)
+        if q in FIN:
+            op(V, "e6", lambda g, T, x: [g.vector.tensor_copy(T["oc" + Z][0:32, L * b:L * b + L], T[PO][0:32, H + b:H + 128:4]) for b in range(4)],
+               [], nm("oc"), 4, banks=[PO])
+        else:
             for a in (0, 1):
                 h = slice(a * H, a * H + H)
                 op(P, "dd%d" % a, lambda g, T, x, h=h: [g.tensor.matmul(T[PO][:, h], T.dm[:], T["cc" + Z][:, h], True, True)],
                    nm("cc%d" % a) + ["dm"], [], banks=[PO])
             for a in (0, 1):
-                op(V, "mu%d" % a, lambda g, T, x, a=a: [g.vector.tensor_tensor(T["pp" + Z][:, a:N:2], T["ga" + Z][:, a:N:2], T[PO][:, a:N:2], A.mult)],
-                   nm("ga0", "ga1"), nm("pp%d" % a), banks=[PO])
-            sums("pp")
-            if r < RO - 1:
-                send(r + 1)
-        op(V, "e1", lambda g, T, x: [g.vector.tensor_copy(T["yp" + Z][:, 0:F], T[PV][:, 0:F])], [], nm("yp"), banks=[PV])
-        op(V, "e2", lambda g, T, x: [g.vector.tensor_tensor(T["yp" + Z][:, F:2 * F], T[PV][:, 0:F], T["yp" + Z][:, 0:F], A.subtract)],
-           nm("yp"), nm("yq"), banks=[PV])
-        op(P, "e3", lambda g, T, x: [g.tensor.matmul(T[PO][0:64, 0:128], T["yp" + Z][:], T.eyeb[:], True, True)], nm("yp", "yq") + ["eyeb"], [], banks=[PO])
-        op(S, "e4", lambda g, T, x: [g.scalar.activation(T["ft" + Z][0:64, :], T[PO][0:64, 0:128], CPY)], [], nm("ft"), banks=[PO])
-        op(P, "e5", lambda g, T, x: [g.tensor.matmul(T[PO][:, 384:384 + L], T.cv[0:64, 12 - 4 * w:140 - 4 * w], T["ft" + Z][0:64, w:128:4], w == 0, w == 3)
-                                     for w in range(4)], nm("ft") + ["cv"], [], 4, banks=[PO])
-        op(V, "e6", lambda g, T, x: [g.vector.tensor_copy(T["oc" + Z][:], T[PO][:, 384:384 + L])], [], nm("oc"), banks=[PO])
+                op(V, "mu%d" % a, lambda g, T, x, a=a: [g.vector.tensor_tensor(T["pp" + Z][:, :, :, a:4:2], T["ga" + Z][:, a:N:2], T[PO][:, a:N:2], A.mult)],
+                   nm("ga0", "ga1"), nm("pp%d" % a, "pp%d" % (2 * a)), banks=[PO])
+            for a in (0, 1):
+                op(P, "ps%d" % a, lambda g, T, x, a=a: [
+                    g.tensor.matmul(T[PV][:, 0, 8 * k:8 * k + 8], T["pp" + Z][:, :, :, k], T.indf[:], True, True) for k in (a, a + 2)],
+                   nm("pp%d" % a) + ["indf"], [], 2, banks=[PV])
+            op(V, "e1", lambda g, T, x: [g.vector.tensor_copy(T["yp" + Z][:, 0:F], T[PV][:, 0, 0:F])], [], nm("yp"), banks=[PV])
+            op(V, "e2", lambda g, T, x: [g.vector.tensor_tensor(T["yp" + Z][:, F:2 * F], T[PV][:, 0, 0:F], T["yp" + Z][:, 0:F], A.subtract)],
+               nm("yp"), nm("yq"), banks=[PV])
+            op(P, "e3", lambda g, T, x: [g.tensor.matmul(T[PO][0:64, 0:128], T["yp" + Z][:], T.eyeb[:], True, True)], nm("yp", "yq") + ["eyeb"], [], banks=[PO])
+            op(S, "e4", lambda g, T, x: [g.scalar.activation(T["ft" + Z][0:64, :], T[PO][0:64, 0:128], CPY)], [], nm("ft"), banks=[PO])
+            op(P, "e5", lambda g, T, x: [g.tensor.matmul(T[PO][:, 384:384 + L], T.cv[0:64, 12 - 4 * w:140 - 4 * w], T["ft" + Z][0:64, w:128:4], w == 0, w == 3)
+                                         for w in range(4)], nm("ft") + ["cv"], [], 4, banks=[PO])
+            op(V, "e6", lambda g, T, x: [g.vector.tensor_copy(T["oc" + Z][:, 0:L], T[PO][:, 384:384 + L])], [], nm("oc"), banks=[PO])
         store("yb", q, lambda T: T.ob[:, cols], "ob" + Z)
-        store("yc", q, lambda T: T["oc" + Z][:], "oc" + Z)
+        store("yc", q, lambda T: T["oc" + Z][0:32, :] if q in FIN else T["oc" + Z][:, 0:L], "oc" + Z)
 
     def last(q):
         Z = str(q)
         at[:] = [q, RO - 1]
-        hits(q, 2)
-        op(P, "h3", lambda g, T, x: [
-            g.tensor.matmul(T.pf1[:, 0:3, 0:L], T.cv[:, 12 - 4 * w:140 - 4 * w], T["fa" + Z][:, w:384:4], w == 0, w == 3)
-            for w in range(4)], ["fa0" + Z, "fa2" + Z, "cv"], [], 4, banks=["pf1"])
-        op(S, "h4", lambda g, T, x: [g.scalar.activation(T["oo" + Z][:, 0:L], T.pf1[:, 0, 0:L], CPY),
-                                     g.scalar.activation(T["oo" + Z][:, L:2 * L], T.pf1[:, 2, 0:L], CPY, scale=0.03125)], [], ["oo" + Z], 2, banks=["pf1"])
-        op(V, "h5", lambda g, T, x: [g.vector.tensor_tensor(T["oo" + Z][:, 2 * L:3 * L], T["oo" + Z][:, 0:L], T.pf1[:, 1, 0:L], A.add)],
-           ["oo" + Z], ["os" + Z], banks=["pf1"])
+        op(S, "hf", lambda g, T, x: [g.scalar.activation(T["hf" + Z][:, h, 0:64], T["pc" + Z][:, :, 2 * h:2 * h + 2, 2, :], CPY, scale=0.03125) for h in (0, 1)],
+           ["pc%d_%d_n" % (q, r) for r in range(RO)], ["hf" + Z], 2)
+        op(P, "h1", lambda g, T, x: [g.tensor.matmul(T.pf0[:, 2 * i + h, :], T[b + Z][:, h], T.eyeb[:], True, True) for i, b in enumerate(("hv", "hf")) for h in (0, 1)],
+           ["hv%d" % r + Z for r in range(RO)] + ["hf" + Z, "pz" + Z, "eyeb"], [], 4, banks=["pf0"])
+        op(H2, "h2", lambda g, T, x: [g.scalar.activation(T["fa" + Z][:], T.pf0[:], CPY) if H2 == S else g.vector.tensor_copy(T["fa" + Z][:], T.pf0[:])],
+           [], ["fa" + Z], banks=["pf0"])
+        op(P, "h3", lambda g, T, x: [g.tensor.matmul(T.pf1[:, 0:2 * L], T.cu[:, 14 - 2 * w:142 - 2 * w], T["fa" + Z][:, w:512:8], w == 0, w == 7)
+                                     for w in range(8)], ["fa" + Z, "cu"], [], 8, banks=["pf1"])
+        op(S, "h4", lambda g, T, x: [g.scalar.activation(T["oo" + Z][:], T.pf1[:, 0:2 * L], CPY)], [], ["oo" + Z], banks=["pf1"])
         store("yh", q, lambda T: T["oo" + Z][:, L:2 * L], "oo" + Z)
-        store("ys", q, lambda T: T["oo" + Z][:, 2 * L:3 * L], "os" + Z)
+        store("ys", q, lambda T: T["oo" + Z][:, 0:L], "oo" + Z)
     for q in range(NC):
         chunk(q)
     for q in range(NC):

@@ -3,14 +3,135 @@ from concourse.bass import DstId, RemoteDMATransfer
 from concourse.mybir import AluOpType, ActivationFunctionType, AxisListType
 
 RO, NR, W, END = 4, 4, 1536, 2 ** 20 - 1
-NC = 3
-N = W // NC
-L, H, F = N // 16, N // 2, 32
+BIG = float(2 ** 21)
+BL = (4, 4, 4)
+NC = len(BL)
+FIN = None
 ZV, ZS = 704, 1216
 TA = 24
-FIN = (2,)
-H2 = "scalar"
-SEQ = [0,1,5,2,3,4,6,7,8,10,9,19,16,18,17,31,20,14,36,11,38,41,39,42,37,15,23,24,43,26,40,12,202,27,28,365,13,21,364,367,368,22,369,201,204,205,206,44,25,366,203,30,45,372,47,209,35,32,210,373,207,208,29,34,46,370,371,48,49,51,52,50,53,54,211,55,212,214,215,56,221,213,375,374,217,59,216,60,61,62,376,378,218,377,58,63,64,65,66,384,219,220,380,379,57,381,67,382,222,226,223,227,224,228,225,69,70,68,385,71,386,387,72,229,388,230,389,73,74,390,76,391,231,232,233,392,75,393,394,395,396,77,234,78,235,79,236,80,239,84,85,33,248,411,410,247,237,81,240,241,397,238,82,83,242,243,96,399,244,398,400,402,401,245,246,403,404,383,405,406,407,408,409,86,87,89,90,88,91,92,93,249,422,94,250,253,252,251,97,98,99,254,255,100,256,412,413,415,416,414,101,102,103,104,257,259,105,106,107,108,417,260,261,418,262,264,419,263,109,110,265,266,420,267,423,424,425,111,268,269,270,271,114,427,428,112,115,426,116,272,273,429,113,430,117,118,274,119,275,277,278,279,431,433,432,434,435,122,123,448,449,285,286,276,280,281,437,282,436,438,440,120,121,439,441,442,95,443,444,445,124,125,127,128,126,258,129,130,421,131,283,284,132,287,288,291,290,289,135,292,136,137,293,138,446,447,134,139,140,294,296,450,451,141,142,295,297,454,453,452,298,455,299,300,456,301,143,460,302,303,304,305,457,458,145,146,306,144,147,307,308,309,148,461,462,149,152,465,466,463,464,150,153,154,310,311,467,468,151,155,469,156,312,315,157,313,314,470,471,472,316,317,473,487,161,486,323,160,318,319,474,320,158,159,321,322,475,172,478,476,477,479,480,481,482,483,484,485,162,163,166,165,164,167,168,169,133,459,171,498,170,325,326,173,174,175,327,176,328,329,331,330,488,332,489,491,492,334,493,490,522,324,523,524,177,178,179,180,525,335,181,529,333,336,184,183,530,340,337,494,338,339,341,495,185,342,343,496,186,499,500,501,182,531,344,526,346,347,502,187,188,503,504,505,506,189,190,348,349,497,507,345,532,191,192,350,508,509,536,533,510,511,351,537,513,352,353,512,514,354,355,516,193,356,538,539,357,194,517,540,515,358,195,518,196,359,197,360,519,198,361,527,542,541,520,534,535,528,199,362,521,200,363]
+CT = 4
+GA = ((0, 2), (2, 3), (3, 4))
+GT = ((0, 2), (2, 4))
+G0 = ((0, 1, "vector"), (1, 2, "scalar"), (2, 3, "vector"), (3, 4, "scalar"))
+PESUM, RELU, COUNT = False, False, "f32"
+GL = ((0, 2), (2, 4))
+PSB, CA, CL, DD, MU, LAST = "pv", None, None, None, None, 8
+S0Q, TJ, HB, HIQ = "vector", 1, ("pf", "pf", "pf"), "vector"
+TJQ, KEEP, TI, TIW = "scalar", False, 1, None
+YQ = ("sync", "scalar", "sync", "scalar")
+OFQ, OBQ, H2Q, H6Q = "scalar", "scalar", "scalar", "scalar"
+SEQ = [
+    0,5,2,3,1,4,6,9,18,14,13,17,47,7,441,244,12,19,36,11,15,21,41,16,22,45,24,27,46,28,44,10,20,267,464,23,70,48,8,50,49,52,53,54,245,35,51,55,42,248,60,
+    246,56,31,29,249,32,33,57,250,30,61,247,34,443,442,251,445,252,454,446,253,254,59,444,447,25,257,256,448,449,450,455,37,258,453,26,451,38,58,62,66,63,
+    64,65,255,67,68,39,69,263,259,260,71,75,72,76,73,74,264,77,78,452,261,456,262,460,457,79,265,458,459,83,266,461,80,81,85,462,463,87,84,91,268,269,270,
+    82,271,105,86,465,272,273,274,89,275,88,92,276,93,469,90,94,95,466,96,278,280,282,467,97,98,99,100,470,468,471,472,281,279,101,284,115,283,286,102,
+    473,288,285,290,106,289,287,292,291,294,479,477,295,480,293,475,478,474,277,296,297,481,485,476,301,312,298,104,486,483,487,482,303,484,498,299,489,
+    488,490,40,43,103,491,492,493,494,495,496,107,302,111,499,108,109,112,110,500,113,114,116,300,117,304,118,119,305,306,308,309,307,120,121,122,123,124,
+    126,310,311,509,497,501,125,128,505,502,503,132,313,317,314,315,316,318,506,319,320,130,129,504,321,136,127,134,507,508,325,133,323,131,137,140,135,
+    138,142,143,510,514,326,333,327,329,511,512,513,139,328,141,324,515,516,517,144,145,518,334,330,331,335,160,146,147,519,337,332,151,520,526,336,322,
+    338,521,339,527,340,341,342,522,523,528,343,357,524,529,530,149,348,525,344,531,532,533,534,346,536,537,538,347,535,539,554,540,150,541,148,156,545,
+    544,152,345,543,153,154,155,157,158,159,349,161,351,350,353,162,163,164,352,354,165,166,167,168,169,171,542,355,356,550,546,548,547,173,358,359,360,
+    361,175,172,549,551,362,363,364,177,365,179,174,181,366,552,553,176,180,368,178,183,370,182,187,374,555,184,556,185,186,188,559,189,560,190,557,558,
+    369,371,372,191,373,561,562,378,375,376,380,563,196,379,192,565,382,377,170,367,381,384,385,386,566,573,567,383,569,568,387,205,571,564,575,570,388,
+    402,195,574,389,576,572,391,577,393,578,579,581,582,580,194,583,584,599,585,588,193,197,586,201,589,198,199,590,392,202,200,203,204,206,207,390,394,
+    208,398,587,209,395,396,399,210,211,397,400,212,213,214,401,591,215,595,403,407,404,408,405,406,218,216,222,220,592,593,409,410,411,217,224,596,594,
+    631,219,226,221,413,597,598,223,225,415,227,414,600,232,228,233,632,601,421,419,416,229,230,604,605,417,422,602,423,633,634,603,424,231,420,412,606,
+    607,418,608,427,234,235,425,635,429,428,610,426,612,611,614,236,237,430,431,618,432,613,619,238,616,433,609,621,637,434,622,239,620,615,435,436,623,
+    617,240,636,437,241,438,627,624,625,242,243,439,440,639,628,638,626,629,630,640]
+SEQ = [
+0,2,3,5,40,9,4,15,14,19,20,13,24,1,11,16,17,6,7,25,33,10,38,21,28,26,41,42,22,46,27,43,29,18,32,45,8,47,48,30,
+230,229,49,50,232,51,52,53,54,233,416,414,231,413,234,235,236,23,237,417,56,238,418,57,425,241,228,415,419,420,31,412,
+240,421,44,422,34,12,35,239,55,424,58,62,59,36,60,63,61,64,242,246,65,66,243,244,247,423,426,245,248,428,249,69,70,
+71,72,250,430,427,431,73,75,74,429,432,253,76,433,434,77,79,83,67,254,255,256,68,81,251,437,438,257,258,259,260,261,
+439,440,441,443,80,87,82,442,267,84,85,88,89,86,252,444,91,268,263,435,90,265,92,93,94,445,264,95,96,269,266,447,97,
+270,271,98,272,449,277,278,448,273,275,451,450,436,274,455,452,453,457,279,276,280,456,454,459,458,78,284,99,468,461,
+281,462,463,100,460,464,102,106,282,104,103,107,465,466,105,108,109,110,37,112,446,111,467,101,283,113,114,115,116,286,
+117,290,287,288,291,285,469,39,118,289,292,293,470,119,474,120,121,294,472,471,475,295,473,476,297,477,262,125,123,298,
+122,299,144,127,478,126,300,301,303,124,129,133,481,302,304,305,131,482,483,484,485,487,128,130,137,307,309,132,135,486,
+488,489,134,136,308,296,310,138,139,140,480,313,315,479,141,314,321,142,491,316,322,311,492,499,495,497,312,317,493,500,
+319,145,512,496,318,320,494,498,323,329,503,513,328,143,324,504,501,505,325,502,490,146,506,507,508,150,326,147,148,151,
+149,152,509,153,327,155,510,154,156,157,158,159,160,330,334,331,161,162,163,335,332,336,511,333,339,337,518,514,164,165,
+338,519,515,516,306,520,167,517,168,521,175,341,342,343,344,522,524,340,188,169,170,171,176,189,345,347,346,172,173,177,
+348,349,174,181,525,526,527,528,182,179,529,178,180,351,523,530,353,352,355,183,184,185,531,532,533,354,359,357,356,166,
+186,361,360,363,535,358,362,365,364,366,536,537,538,539,373,367,541,542,372,557,368,543,540,369,187,545,556,549,544,547,
+546,190,194,550,551,548,552,191,195,192,196,193,370,553,554,197,200,198,199,224,225,534,201,202,203,204,350,205,371,378,
+374,207,379,376,375,380,377,226,555,206,208,383,381,382,384,558,562,559,227,408,560,209,563,561,564,385,565,386,213,409,
+566,387,388,389,568,567,391,410,569,570,571,390,392,211,572,573,575,212,393,411,395,397,214,215,574,216,217,576,577,592,
+593,218,396,398,579,219,220,221,399,400,401,402,594,222,580,581,223,595,582,403,404,583,584,585,586,394,210,598,597,578,
+405,406,407,596,587,588,589,590,591,601,600,602,599]
+SEQ2 = SEQ
+GA = CA = CL = MU = ((0, 2), (2, 4))
+COUNT, CT, DD, PSB, LAST, HB, S0Q = "list", 2, ((0, 2, "po", 0), (2, 4, "pv", 0)), "po", 4, ("pf", "pz", "pf"), "scalar"
+SEQ = [
+2,0,1,3,15,14,5,19,20,9,24,44,16,4,10,38,21,25,28,18,13,29,17,33,39,32,6,47,48,49,50,7,8,205,203,206,204,360,51,52,53,54,55,56,
+30,359,207,208,209,210,362,59,214,215,22,361,211,363,212,45,31,364,46,365,366,202,12,57,26,71,58,367,368,11,34,43,27,42,358,23,227,
+383,60,64,371,35,213,216,36,40,370,220,217,218,221,369,65,62,219,222,61,372,223,63,66,224,376,67,374,68,373,228,229,230,231,377,375,
+378,70,379,380,72,73,232,74,75,234,384,386,235,236,385,76,237,238,239,387,240,78,80,242,243,82,79,241,244,81,388,390,245,246,84,83,86,
+391,247,85,392,233,87,88,89,90,249,393,394,395,91,396,397,262,37,69,226,248,251,255,225,77,250,253,252,398,256,254,399,400,401,402,403,
+106,257,381,92,258,95,99,93,41,96,97,100,259,405,263,264,404,389,101,98,407,265,406,94,266,411,267,268,102,103,408,409,412,410,413,414,
+415,107,108,418,269,284,419,271,109,110,420,270,272,111,273,274,421,422,113,115,275,276,114,116,277,278,117,118,279,280,423,425,281,119,
+120,105,426,282,121,122,123,124,424,283,382,297,427,428,125,429,430,126,112,285,431,432,129,141,433,127,104,261,290,286,291,260,434,435,
+436,437,438,287,288,440,292,289,417,128,295,293,453,130,294,134,131,132,135,133,136,298,137,138,441,439,299,442,446,300,301,142,143,443,
+447,444,144,145,302,304,448,445,416,146,303,449,296,450,140,306,148,454,455,456,457,150,152,149,151,305,153,154,155,308,307,156,157,158,
+159,458,461,309,459,310,311,160,161,460,462,147,312,463,313,314,315,316,464,452,465,176,163,319,164,466,467,468,451,469,470,471,472,475,
+139,162,165,332,169,166,317,167,170,473,318,168,171,476,320,172,174,488,175,325,321,173,326,474,177,322,198,178,323,327,324,330,199,179,
+180,181,200,477,328,481,182,329,478,479,482,183,201,184,331,480,354,483,333,355,335,484,334,485,486,185,186,336,337,187,188,338,339,489,
+490,487,190,189,341,192,340,491,492,493,496,510,356,495,343,494,342,514,344,191,193,194,498,348,511,497,195,500,196,499,512,513,357,516,
+345,347,346,502,349,350,501,503,504,351,352,197,515,353,505,506,507,508,509,517,520,518,519]
+SEQ3 = SEQ
+TJQ, TJ, TI, KEEP, HB = "vector", 2, 2, True, ("pf", "pf", "pf")
+SEQ = [
+5,0,1,2,3,10,4,20,6,16,48,17,21,11,18,22,346,25,46,34,19,14,45,197,26,49,51,50,52,47,29,199,200,201,7,348,61,30,33,53,8,9,54,
+55,56,57,58,39,198,31,347,32,202,203,204,205,206,359,207,40,349,358,350,60,351,352,353,210,354,43,355,59,209,356,23,44,62,66,64,63,
+208,357,67,12,41,65,68,211,69,215,70,212,213,27,216,214,73,74,217,360,364,218,24,361,365,75,76,28,362,77,78,366,219,222,224,363,223,
+225,15,367,79,368,80,82,81,84,226,227,371,372,228,83,229,373,374,375,86,376,85,87,231,230,88,89,90,232,220,233,234,235,377,236,237,91,
+378,238,380,239,240,72,379,382,392,381,71,383,35,384,36,221,13,385,386,387,388,92,94,93,95,241,99,97,96,100,370,98,391,389,37,101,369,
+102,103,244,248,245,246,249,243,106,107,250,247,390,104,105,108,251,393,397,394,395,398,242,109,110,111,252,255,396,399,112,256,257,253,
+254,258,259,400,113,401,114,404,405,115,117,116,260,118,261,262,406,407,408,119,409,120,263,402,121,122,123,410,264,265,266,268,269,267,
+270,271,272,411,124,412,127,413,414,273,415,416,417,126,418,419,420,421,38,403,422,276,425,125,132,128,133,129,130,134,274,42,423,131,
+135,277,281,275,136,278,279,282,139,140,283,280,426,430,284,428,138,427,431,286,424,137,141,142,143,285,144,429,145,432,288,290,433,434,
+289,291,146,147,159,292,148,437,438,149,150,151,439,440,293,152,153,436,154,294,155,295,297,441,296,156,435,298,299,300,442,157,444,443,
+287,301,302,457,445,303,446,447,304,305,306,160,158,448,449,161,165,450,451,452,453,454,162,455,163,309,166,164,167,458,168,169,307,171,
+170,308,193,172,173,310,314,311,315,194,312,316,456,174,175,176,177,195,313,179,196,319,317,318,459,463,178,320,461,460,342,343,464,321,
+462,465,322,468,323,466,324,325,467,326,181,183,344,180,182,327,470,471,472,473,328,474,345,476,184,185,329,331,330,332,469,187,186,491,
+334,333,478,188,477,479,492,189,190,191,480,336,335,475,495,481,482,493,484,483,485,494,497,192,337,338,339,340,341,496,486,487,488,489,
+490,499,498,500,501]
+KEEP, HB, PESUM = False, ("pf", "pz", "pf"), True
+SEQ = [
+5,0,2,3,20,1,4,40,10,16,21,6,7,23,8,9,48,17,18,26,22,27,46,35,14,41,30,50,11,19,49,51,52,28,206,208,31,53,54,55,56,361,57,364,
+58,32,205,62,204,207,365,362,363,61,366,209,33,210,60,211,216,212,213,214,367,368,369,217,218,44,360,24,45,370,59,63,47,64,65,215,373,
+374,371,34,67,68,66,219,69,372,385,229,223,70,29,71,220,375,221,224,74,75,222,376,377,73,379,225,380,378,25,381,76,77,226,72,78,79,
+230,231,80,382,386,387,82,232,233,388,81,83,389,234,235,84,236,228,85,86,87,237,390,88,89,238,90,91,15,384,239,240,241,242,243,92,93,
+392,394,393,391,244,245,246,247,248,396,108,97,395,227,398,397,95,249,96,253,399,36,37,400,401,402,403,94,98,102,404,420,251,407,264,
+13,383,405,100,99,12,42,38,409,101,103,104,107,106,250,254,105,109,258,252,111,255,256,110,259,408,406,112,113,114,115,257,260,261,262,
+116,410,263,412,411,265,413,266,414,415,267,268,117,119,416,118,417,269,120,270,421,422,121,271,122,273,123,124,272,423,424,425,274,426,
+125,126,275,127,276,128,427,277,132,278,279,429,280,428,281,282,143,299,283,431,430,433,130,288,432,435,434,419,436,437,438,418,284,131,
+129,137,133,134,135,439,136,444,443,286,455,442,287,285,138,139,140,39,440,289,144,291,290,293,146,145,292,43,294,141,142,441,295,445,
+297,298,147,148,296,447,446,300,301,149,150,449,450,152,448,151,153,302,303,304,451,154,155,156,305,452,307,157,456,306,457,308,158,159,
+160,161,162,163,458,459,460,461,167,309,453,310,311,312,313,462,454,463,314,464,315,316,317,318,164,466,178,465,323,468,334,467,319,320,
+168,469,470,165,170,169,171,172,166,321,173,174,177,471,472,473,176,474,475,477,322,175,200,179,324,325,478,201,328,479,326,329,181,327,
+330,331,180,182,333,332,183,356,335,476,484,480,336,184,186,482,185,481,485,483,337,338,339,486,487,202,188,357,341,187,342,490,190,189,
+491,492,489,193,493,494,495,488,343,340,191,358,203,344,194,345,192,346,348,347,498,500,512,195,497,499,196,197,198,496,502,501,349,350,
+516,503,513,514,515,504,505,359,506,518,199,351,352,353,354,355,517,507,508,509,510,511,522,519,521,520]
+SEQ5 = SEQ
+TJQ, TI, TIW, ZS, OBQ = None, 2, 2, 1120, "vector"
+SEQ = [
+2,3,10,4,5,40,46,17,206,20,366,0,21,18,35,41,22,44,26,45,23,11,19,1,6,47,7,8,48,49,50,14,368,34,209,208,210,51,52,53,54,27,55,
+72,207,16,370,367,60,211,212,213,30,369,28,31,59,12,214,56,371,372,373,374,218,215,216,32,15,375,392,376,9,219,58,232,42,220,217,24,
+378,221,36,29,379,380,25,381,33,57,61,66,62,37,226,38,13,63,64,67,377,65,222,68,69,223,382,224,227,383,386,73,74,225,384,387,228,70,
+385,230,75,76,77,71,231,79,390,229,388,389,80,233,235,234,236,237,393,81,83,391,395,239,82,84,85,240,394,86,87,88,396,397,241,89,90,
+91,399,242,243,244,245,246,247,248,96,400,249,250,251,95,92,401,97,403,252,78,402,404,94,405,406,407,39,408,93,98,108,256,238,409,410,
+411,102,257,268,415,412,255,99,100,103,414,101,416,417,104,253,258,398,105,106,413,428,259,260,262,43,254,109,110,263,261,264,107,111,
+418,266,267,112,265,113,419,420,422,269,271,421,423,270,272,424,425,114,115,117,116,118,119,121,429,430,431,273,275,120,276,432,433,123,
+122,124,277,278,125,126,127,435,279,280,281,282,283,128,436,434,437,284,285,286,287,132,438,439,133,130,290,440,441,442,129,288,144,427,
+426,443,444,445,446,447,138,134,131,292,274,136,464,293,135,137,304,139,448,140,141,452,289,294,143,142,295,296,298,449,451,291,145,146,
+453,450,297,299,147,148,149,300,301,454,302,458,303,456,455,151,305,307,306,308,457,459,153,155,152,460,309,311,154,156,461,465,466,157,
+158,312,313,159,160,314,467,468,469,463,161,162,163,471,315,317,310,316,318,473,472,164,319,320,321,322,323,168,474,150,475,476,169,326,
+324,477,478,340,166,180,479,480,462,328,481,482,165,483,174,170,172,171,173,329,175,325,488,489,176,177,178,167,179,484,485,487,327,486,
+334,202,470,203,330,181,332,331,182,333,335,336,490,338,183,184,185,337,339,187,188,492,491,341,494,500,186,493,362,363,495,342,343,344,
+345,496,497,499,189,190,498,348,501,502,191,192,346,194,503,504,347,505,196,350,204,205,364,349,193,506,352,507,351,522,508,195,197,354,
+509,198,355,523,199,511,510,353,356,200,512,515,516,513,514,524,357,358,526,359,360,525,201,361,365,528,527,517,518,519,520,521,529,530,
+531,532]
 KEY = {n: z for z, n in enumerate(SEQ)}
 
 SCRATCH = {
@@ -19,55 +140,46 @@ SCRATCH = {
     "zz": ("sbuf", [128, ZS - ZV], "bfloat16"), "dif": ("sbuf", [128, 128], "float32"),
     "indb": ("sbuf", [128, 8], "bfloat16"), "indf": ("sbuf", [128, 8], "float32"), "zt": ("sbuf", [128, 36], "float32"),
     "sg": ("sbuf", [128, 8], "float32"), "sc": ("sbuf", [128, 1], "float32"), "cw": ("sbuf", [128, 32], "bfloat16"),
-    "eyeb": ("sbuf", [128, 128], "bfloat16"), "dm": ("sbuf", [128, 128], "bfloat16"), "sr": ("sbuf", [128, 144], "bfloat16"),
-    "bs": ("sbuf", [128, 64], "bfloat16"), "b2": ("sbuf", [128, 16], "bfloat16"), "bc": ("sbuf", [128, 512], "bfloat16"), "cx": ("sbuf", [128, 32], "bfloat16"),
-    "cv": ("sbuf", [128, 144], "bfloat16"), "cu": ("sbuf", [128, 144], "bfloat16"),
-    "oh": ("sbuf", [128, W // 16], "float16"), "ob": ("sbuf", [128, W // 16], "float32"),
-    "pf0": ("psum", [128, 4, 128], "float32"), "pf1": ("psum", [128, 512], "float32"),
+    "eyeb": ("sbuf", [128, 128], "bfloat16"), "eyep": ("sbuf", [128, 4, 32], "bfloat16"), "eyeq": ("sbuf", [128, 128], "float32"),
+    "dm": ("sbuf", [128, 128], "bfloat16"), "sr": ("sbuf", [128, 144], "bfloat16"), "bs": ("sbuf", [128, 64], "bfloat16"),
+    "bc": ("sbuf", [128, 512], "bfloat16"), "cx": ("sbuf", [128, 32], "bfloat16"), "b8": ("sbuf", [128, 16], "bfloat16"),
+    "pm": ("sbuf", [128, 128], "float32" if COUNT == "f32" else "bfloat16"), "cu": ("sbuf", [128, 2, 132], "bfloat16"), "sm": ("sbuf", [128, 128], "float32"),
+    "wk": ("sbuf", [128, 6, 16], "float32"), "wq": ("sbuf", [128, 6], "float32"),
+    "oh": ("sbuf", [128, W // 16], "float16"), "ob": ("sbuf", [128, W // 16], "float32"), "oo": ("sbuf", [128, 4, W // 16], "float32"),
+    "tj": ("sbuf", [128, W], "float32"), "sb": ("sbuf", [128, 2], "float32"), "pl": ("sbuf", [128, 2, 32, 4, 2], "float32"), "oc": ("sbuf", [128, W // 16], "float32"),
+    "pz": ("psum", [128, 4, 32, 2, 2], "float32"), "pf": ("psum", [128, 4, 32, 2, 2], "float32"),
 }
-for _q in range(NC):
-    for _k, _s, _d in (("rc", [128, RO * NR * F], "float32"), ("xx", [128, 2 * F], "float32"), ("xn", [128, 2 * F], "float32"),
-                       ("mx", [128, F], "float32"), ("mn", [128, F], "float32"), ("pc", [128, RO, 4, 4, 8], "float16"),
-                       ("lt", [128, 2, 2, 32], "float16"), ("gt", [128, N], "float32"), ("cm", [128, N], "bfloat16"),
-                       ("ga", [128, N], "float32"), ("cc", [128, N], "bfloat16"), ("pp", [128, L, 4, 4], "float32"),
-                       ("hf", [128, 2, 128], "bfloat16"), ("hv", [128, 2, 2 * RO, 16], "float16"), ("fa", [128, 512], "float16"),
-                       ("oo", [128, 2 * L], "float32"), ("oc", [128, 4 * L], "float32"), ("ft", [128, 128], "float16"), ("yp", [128, 2 * F], "float16")):
+for _q, _b in enumerate(BL):
+    for _k, _s, _d in (("rc", [128, RO * NR * 8 * _b], "float32"), ("xx", [128, 16 * _b], "float32"), ("xn", [128, 16 * _b], "float32"),
+                       ("mx", [128, 8 * _b], "float32"), ("mn", [128, 8 * _b], "float32"), ("pc", [128, _b, 128], "float16"),
+                       ("lt", [128, 32 * _b], "float16"), ("gt", [128, 128 * _b], "float32"), ("cm", [128, 128 * _b], "bfloat16"),
+                       ("ga", [128, 128 * _b], "float32"), ("cc", [128, 128 * _b], "bfloat16"), ("pp", [128, 128 * _b], "float32"),
+                       ("fa", [128, 128 * _b], "float16"), ("zr", [128, 32 * _b], "float32"),
+                       ("nb", [128, 32], "bfloat16"), ("nt", [128, 32], "float32" if COUNT == "f32" else "bfloat16")):
         SCRATCH["%s%d" % (_k, _q)] = ("sbuf", _s, _d)
-    SCRATCH["pv%d" % _q] = ("psum", [128, 2, H], "float32")
-    SCRATCH["po%d" % _q] = ("psum", [128, 512], "float32")
-
-SHARE = {"ct0": "va", "ca0": "va", "mu0": "va", "ct1": "vb", "ca1": "vb", "mu1": "vb", "pn0": "ta", "dd0": "ta", "ps0": "ta",
-         "ct2": "va", "ct3": "vb", "pn2": "ta", "pn3": "tc", "mu2": "va", "ps2": "ta",
-         "pn1": "tc", "dd1": "tc", "ps1": "tc", "pb": "tp", "e3": "tp", "e5": "tp", "xx": "vx", "lo": "vx", "vt": "vx", "s0": "vx",
-         "e1": "vo", "e2": "vo", "e6": "vo", "hv": "vh", "h1": "th", "h3": "th", "hf": "sh", "h4": "sh", "e4": "sh"}
+    SCRATCH["pv%d" % _q] = ("psum", [128, 4, 128], "float32")
+    SCRATCH["po%d" % _q] = ("psum", [128, 4, 32, 2, 2], "float32")
 
 
 def build():
-    ops, lastw, readers, bank, at = [], {}, {}, {}, [None, None]
+    ops, lastw, readers, at = [], {}, {}, [None, -1]
 
     def op(queue, name, emit, reads, writes, ninc=1, after=(), banks=(), order=()):
         n = len(ops)
-        sem = name if at[0] is None or name == "out" else SHARE.get(name, name) + str(at[0])
-        o = {"n": n, "q": queue, "sem": sem, "name": name, "at": tuple(at), "emit": emit, "ninc": ninc, "deps": set(after), "order": set(order)}
+        o = {"n": n, "q": queue, "name": name, "at": tuple(at), "emit": emit, "ninc": ninc, "deps": set(after), "order": set(order), "banks": banks}
         for t in reads:
             if t in lastw:
                 o["deps"].add(lastw[t])
         for t in writes:
-            if t in lastw:
-                o["deps"].add(lastw[t])
-            o["deps"].update(readers.get(t, ()))
+            for i in ([lastw[t]] if t in lastw else []) + list(readers.get(t, ())):
+                o["order" if t[0] == "@" and ops[i]["q"] == queue else "deps"].add(i)
         for t in reads:
             readers.setdefault(t, set()).add(n)
         for t in writes:
             lastw[t] = n
             readers[t] = set()
-        for b in banks:
-            acc = bank.get(b, [])
-            o["deps"].update(i for i in acc if ops[i]["q"] != queue)
-            o["order"].update(i for i in acc if ops[i]["q"] == queue)
-            bank[b] = (acc if any(ops[i]["q"] == queue for i in acc) else []) + [n]
         o["deps"].discard(n)
-        o["order"] -= o["deps"]
+        o["order"] -= o["deps"] | {n}
         ops.append(o)
         return n
 
@@ -85,14 +197,14 @@ def build():
     zc = op(G, "c_x2", lambda g, T, x: [g.iota(T.x0[:, ZS:W], [[0, W - ZS]], 0, 0)], [], [])
     l0 = load("l_x0", lambda T: T.x0[0:128:16, :], lambda T: T.ids[0:128:16, :], ["x0"], after=(za, zb, zc), order=(la,))
     l1 = load("l_tt", lambda T: T.tt[TA:128, :], lambda T: T.tops[TA:128, :], ["ttb"], order=(l0,))
-    load("l_ti", lambda T: T.ti[:], lambda T: T.ids[:], ["ti"], order=(l1,))
+    for z in range(TI):
+        c = slice(z * W // TI, (z + 1) * W // TI)
+        l1 = load("l_ti%d" % z, lambda T, c=c: T.ti[:, c], lambda T, c=c: T.ids[:, c], ["ti%d" % z], order=(l1,))
+    ti = ["ti%d" % z for z in range(TI)]
 
-    def fill(name, buf, v):
-        op(V, name, lambda g, T, x: [g.vector.memset(T[buf][:], v)], [], [buf])
-    for z, (buf, v) in enumerate((("indb", 1.0), ("sg", 1.0), ("sr", 0.0), ("cv", 0.0), ("zt", 0.0), ("cu", 0.0))):
-        fill("c_m%d" % z, buf, v)
-    op(V, "c_m7", lambda g, T, x: [g.vector.memset(T.cw[:, a:b], v) for a, b, v in ((0, 16, 32.0), (16, 24, 0.5), (24, 32, 0.0))]
-       + [g.vector.memset(T.cx[:], 0.0)], [], ["cw", "cx"], 4)
+    for z, (buf, v) in enumerate((("indb", 1.0), ("sg", 1.0), ("zt", 0.0), ("cu", 0.0), ("cx", 0.0), ("wk", 0.0))):
+        op(V, "c_m%d" % z, lambda g, T, x, buf=buf, v=v: [g.vector.memset(T[buf][:], v)], [], [buf])
+    op(V, "c_cw", lambda g, T, x: [g.vector.memset(T.cw[:, a:b], v) for a, b, v in ((0, 8, 0.5), (8, 24, 32.0), (24, 32, 0.0))], [], ["cw"], 3)
 
     def sel(name, buf, pat, cmp, v, base, cm=1):
         op(G, name, lambda g, T, x: [g.affine_select(T[buf][:], T[buf][:], pat, cmp, v, base, cm)], [buf], [buf])
@@ -101,9 +213,15 @@ def build():
     sel("c_sg", "sg", [[-16, 8]], A.not_equal, -1.0, -15)
     op(G, "c_df", lambda g, T, x: [g.iota(T.dif[:], [[1, 128]], 0, -1, allow_small_or_imprecise_dtypes=True)], [], ["dif"])
     op(V, "c_ey", lambda g, T, x: [g.vector.tensor_scalar(T.eyeb[:], T.dif[:], 0.0, None, A.is_equal)], ["dif"], ["eyeb"])
+    if PESUM:
+        op(V, "c_eq", lambda g, T, x: [g.vector.tensor_scalar(T.eyeq[:], T.dif[:], 0.0, 1.0 / NR, A.is_equal, A.mult)], ["dif"], ["eyeq"])
+    op(S, "c_ep", lambda g, T, x: [g.scalar.activation(T.eyep[:, b], T.eyeb[:, b:128:4], CPY) for b in range(4)], ["eyeb"], ["eyep"], 4)
 
-    def two(name, out, a, b, alu, reads, writes):
-        op(V, name, lambda g, T, x: [g.vector.tensor_tensor(out(T), a(T), b(T), alu)], reads, writes)
+    def copy(queue, name, out, src, reads, writes, **k):
+        return op(queue, name, lambda g, T, x: [g.vector.tensor_copy(out(T), src(T)) if queue == V else g.scalar.activation(out(T), src(T), CPY)], reads, writes, **k)
+
+    def two(name, out, a, b, alu, reads, writes, **k):
+        return op(V, name, lambda g, T, x: [g.vector.tensor_tensor(out(T), a(T), b(T), alu)], reads, writes, **k)
 
     def fold(name, to, buf, n):
         two(name, lambda T: T[to][:, 0:n], lambda T: T[buf][:, 0:n], lambda T: T[buf][:, n:2 * n], A.add, [buf], [to])
@@ -112,7 +230,8 @@ def build():
                                    g.vector.tensor_scalar(T.dm[:, 15:128:16], T.eyeb[:, 14:128:16], -1.0, None, A.mult)], ["eyeb"], ["dm"], 2)
     fold("c_b1", "bs", "eyeb", 64)
     fold("c_b2", "bs", "bs", 32)
-    fold("c_b6", "b2", "bs", 16)
+    fold("c_b6", "b8", "bs", 16)
+    fold("c_b7", "b8", "b8", 8)
     two("c_b3", lambda T: T.cw[:], lambda T: T.cw[:], lambda T: T.bs[:, 0:32], A.mult, ["bs", "cw"], ["cw"])
     fold("c_b4", "cw", "cw", 16)
     op(V, "c_b5", lambda g, T, x: [g.vector.tensor_tensor(T.cx[32 * b:32 * b + 32, 8 * b:8 * b + 8], T.cw[32 * b:32 * b + 32, 0:8], T.cw[32 * b:32 * b + 32, 8:16], A.add)
@@ -120,23 +239,47 @@ def build():
     op(V, "c_bc", lambda g, T, x: [g.vector.tensor_copy(T.bc[:, i:512:16], T.cx[:]) for i in range(16)], ["cx"], ["bc"], 16)
     op(V, "c_sc", lambda g, T, x: [g.vector.tensor_reduce(T.sc[:], T.sg[:], AxisListType.X, A.min)], ["sg"], ["sc"])
     op(S, "c_if", lambda g, T, x: [g.scalar.activation(T.indf[:], T.indb[:], CPY, scale=0.03125)], ["indb"], ["indf"])
-    op(S, "c_sr", lambda g, T, x: [g.scalar.activation(T.sr[:, 15:143:16], T.indb[:], CPY)], ["indb"], ["sr"])
+    wk = [(r, 3 * r, 3 * r + 1, 1, BIG) for r in range(RO)] + [(r, 3 * r + 1, 3 * r + 3, 1, 32.0) for r in range(RO + 1)] + [(5, 0, 12, 3, 1.0)]
+    wa = list(enumerate((0, 32, 64, 96, 0, 96)))
+    if not RELU:
+        wk = [(3, 0, 12, 3, 32.0), (3, 1, 12, 3, 32.0), (4, 12, 14, 1, 32.0), (5, 2, 12, 3, 1.0)]
+        wa = [(3, 64), (4, 0), (5, 96)]
+    op(V, "c_w2", lambda g, T, x: [g.vector.memset(T.wk[:, z, a:b:s], v) for z, a, b, s, v in wk], ["wk"], ["wk"], len(wk))
+    sel("c_w3", "wk", [[0, 6], [-8, 16]], A.is_ge, 0.0, 0)
+    sel("c_w4", "wk", [[0, 6], [8, 16]], A.is_ge, 0.0, 7, -1)
+    op(V, "c_w5", lambda g, T, x: [g.vector.tensor_reduce(T.wq[:, k:k + 1], T.wk[:, k], AxisListType.X, A.add) for k in range(6)], ["wk"], ["wq"], 6)
+    if COUNT == "list":
+        op(V, "c_r1", lambda g, T, x: [g.vector.memset(T.sr[:], 0.0)], [], ["sr"])
+        op(S, "c_sr", lambda g, T, x: [g.scalar.activation(T.sr[:, 15:143:16], T.indb[:], CPY)], ["indb"], ["sr"])
     op(S, "c_zt", lambda g, T, x: [g.scalar.activation(T.zt[:, 3:35:4], T.indb[:], CPY)], ["indb"], ["zt"])
-    op(S, "c_cu", lambda g, T, x: [g.scalar.activation(T.cu[:, 14 + k:142:16], T.b2[:, 8 * k:8 * k + 8], CPY, scale=32.0) for k in range(2)], ["b2"], ["cu"], 2)
-    op(S, "c_cv", lambda g, T, x: [g.scalar.activation(T.cv[:, 12 + k:140:16], T.bs[:, 8 * k:8 * k + 8], CPY, scale=32.0) for k in range(4)], ["bs"], ["cv"], 4)
+    op(S, "c_cu", lambda g, T, x: [g.scalar.activation(T.cu[:, z // 4 if RELU else 1, 3 + a:35 + a:4], T.b8[:, 0:8], CPY, scale=T.wq[:, z:z + 1])
+                                   for z, a in wa], ["b8", "wq", "cu"], ["cu"], len(wa))
+    if COUNT != "list":
+        op(V, "c_p1", lambda g, T, x: [g.vector.memset(T.pm[:], 1.0)], [], ["pm"])
+        sel("c_pm", "pm", [[1, 8], [8, 4], [32, 4]], A.is_equal, 0.0, 0, -1)
+    if RELU:
+        op(V, "c_s1", lambda g, T, x: [g.vector.memset(T.sm[:], 0.0)], [], ["sm"])
+        op(S, "c_sm", lambda g, T, x: [g.scalar.activation(T.sm[:, 64:96], T.bs[:, 0:32], CPY)], ["bs"], ["sm"])
+    if S0Q == S and TJQ == V:
+        for z in range(TJ):
+            ops[op(V, "c_tj%d" % z, lambda g, T, x, c=slice(z * W // TJ, (z + 1) * W // TJ): [
+                g.vector.tensor_scalar(T.tj[:, c], T.ti[:, c], END - 0.25, None, A.min)], [ti[z * TI // TJ]], ["tj%d" % z])]["only"] = 1
+    elif S0Q == S and TJQ:
+        ops[op(V, "c_sb", lambda g, T, x: [g.vector.tensor_scalar(T.sb[:, z:z + 1], T.sc[:], v, None, A.mult) for z, v in enumerate((-1.0, END - 0.25))],
+               ["sc"], ["sb"], 2)]["only"] = 1
+        for z in range(TJ):
+            ops[op(S, "c_tj%d" % z, lambda g, T, x, c=slice(z * W // TJ, (z + 1) * W // TJ): [
+                g.scalar.activation(T.tj[:, c], T.ti[:, c], ActivationFunctionType.Relu, END - 0.25, -1.0)], [ti[z * TI // TJ]], ["tj%d" % z])]["only"] = 1
     op(V, "c_oi", lambda g, T, x: [g.vector.tensor_copy(T.off[:], T.stb[:])], ["stb"], ["off%d" % q for q in range(NC)])
     op(V, "c_ob", lambda g, T, x: [g.vector.tensor_copy(T.oh[:], T.stb[:])], ["stb"], ["oh%d" % q for q in range(NC)])
-
-    def hits(q, r):
-        Z = str(q)
-        op(V, "hv", lambda g, T, x: [g.vector.tensor_tensor(T["hv" + Z][:, :, 2 * r + a, :], T["pc" + Z][:, r, :, a, :], T["pc" + Z][:, r, :, 2, :], A.mult)
-                                     for a in (0, 1)], ["pc%d_%d_%s" % (q, r, t) for t in "hln"], ["hv%d" % r + Z], 2)
-
-    def store(y, q, src, tok):
-        op("sync", "out", lambda g, T, x: [g.sync.dma_start(T[y][:, L * q:L * q + L], src(T))], [tok], [], 16)
+    if KEEP:
+        keep = op(P, "c_bm", lambda g, T, x: [g.tensor.matmul(T.pz[:, 0, 0:24], T.eyeb[:], T.oh[:], True, False)], ["oh0", "eyeb"],
+                  ["@pk%d" % q for q in range(NC)], banks=["pz"])
 
     def chunk(q):
-        cols = slice(L * q, L * q + L)
+        B = BL[q]
+        N, L, c0 = 128 * B, 8 * B, 8 * sum(BL[:q])
+        cols = slice(c0, c0 + L)
         Z = str(q)
         PV, PO = "pv" + Z, "po" + Z
         at[:] = [q, -1]
@@ -144,160 +287,228 @@ def build():
         def nm(*a):
             return [k + Z for k in a]
 
-        def half(T, a):
-            return T.off[:, L * q + a * L // 2:L * q + a * L // 2 + L // 2]
+        def nb(k, a, b):
+            return ["%s%d_%d" % (k, q, i) for i in range(a, b)]
 
-        def gather(name, out, table, a, reads, **k):
-            op(S, name, lambda g, T, x: [g.scalar.activation(T[out + Z][:, a * H:a * H + H], T[table][:, 0:W].indirect(half(T, a)), CPY,
-                                                             **{n: T[v][:] for n, v in k.items()})], reads + nm("off"), nm(out + str(a)))
-        gather("g0", "ga", "x0", 0, ["x0"])
-        op(V, "g1", lambda g, T, x: [g.vector.tensor_copy(T["ga" + Z][:, H:N], T.x0[:, 0:W].indirect(half(T, 1)))], ["x0"] + nm("off"), nm("ga1"))
+        def rows(T, buf, a, b):
+            return T[buf + Z][:, 128 * a:128 * b]
+
+        def gather(name, out, table, a, b, reads, queue=S, **k):
+            def emit(g, T, x):
+                i = T[table][:, 0:W].indirect(T.off[:, c0 + 8 * a:c0 + 8 * b])
+                if queue == V:
+                    return [g.vector.tensor_copy(rows(T, out, a, b), i)]
+                return [g.scalar.activation(rows(T, out, a, b), i, CPY, **{n: T[v][:] for n, v in k.items()})]
+            op(queue, name, emit, reads + nm("off"), nb(out, a, b))
+
+        PS, pst = (PV, nm("@pv0")) if PSB == "pv" else (PO, nm("@pm"))
 
         def rc(T, r, a, b):
-            return T["rc" + Z][:, (r * NR + a) * F:(r * NR + b) * F]
+            return T["rc" + Z][:, (r * NR + a) * L:(r * NR + b) * L]
 
-        def sums(a, b):
-            def block(T, k):
-                return T["ga" + Z][:, a * H + k:a * H + H:2] if b == "ga" else T["pp" + Z][:, a * L // 2:a * L // 2 + L // 2, :, k:4:2]
-            op(P, "ps%d" % a, lambda g, T, x: [
-                g.tensor.matmul(T[PO][:, H + 16 * a + 8 * k:H + 16 * a + 8 * k + 8], block(T, k), T.indf[:], True, True) for k in (0, 1)],
-               nm(b + str(a)) + ["indf"], [], 2, banks=[PO])
+        def sums(b, buf):
+            op(P, "ps%d" % b, lambda g, T, x: [g.tensor.matmul(T[PV][:, 0, 8 * b:8 * b + 8] if PS == PV else T[PO][:, 2, 2 * b:2 * b + 2],
+                                                               rows(T, buf, b, b + 1), T.indf[:], True, True)],
+               nb(buf, b, b + 1) + ["indf"], pst + nb("@ps", b, b + 1) + (nm("@open") if PS == PO else []), banks=[PS])
 
         def send(r):
             def s0(g, T, x):
-                o, i = rc(T, r, x["rank"], x["rank"] + 1), T[PO][:, H:H + F]
-                if x["rank"] == 1:
+                o, i = rc(T, r, x["rank"], x["rank"] + 1), T[PV][:, 0, 0:L] if PS == PV else T[PO][:, 2, 0:8]
+                if r and S0Q == S:
+                    return [g.scalar.activation(o, i, CPY)]
+                if x["rank"] == 1 and TJQ:
                     return [g.vector.tensor_scalar(o, i, (END - 0.25) / 32.0, None, A.min)]
                 return [g.vector.tensor_copy(o, i)]
-            op(V, "s0", s0, [], ["own%d_%d" % (q, r)], banks=[PO])
+            op(S0Q if r else V, "s0", s0, nb("@ps", 0, B) + pst, ["own%d_%d" % (q, r)], banks=[PS])
 
             def ex(g, T, x):
                 s = rc(T, r, x["rank"], x["rank"] + 1)
-                tr = [RemoteDMATransfer(dst_ids=[DstId(rid=a[0], pnc=a[1])], dma_engine_mask=m, remote_sem=T.sem["ar%d_%d" % (q, r)],
-                                        srcs=[s], dsts=[s], alu_op=0) for a, m in x["peers"]]
+                tr = [RemoteDMATransfer(dst_ids=[DstId(rid=a[0], pnc=a[1]) for a in to], dma_engine_mask=m, remote_sem=T.sem["ar%d_%d" % (q, r)],
+                                        srcs=[s], dsts=[s] * len(to), alu_op=0) for to, m in x["peers"]]
                 g.remote_dma_fused(tr, local_sem=T.sem["sent"])
                 return []
             k = op(G, "ex", ex, ["own%d_%d" % (q, r)], [], 0)
             ops[op("remote", "ar", None, [], ["arr%d_%d" % (q, r)], 0, after=(k,))]["sem"] = "ar%d_%d" % (q, r)
 
-        op(V, "pz", lambda g, T, x: [g.vector.memset(T["pc" + Z][:, :, :, 3, :], 0.0), g.vector.memset(T["hf" + Z][:, :, 64:128], 0.0)], [], nm("pz"), 2)
-        sums(0, "ga")
-        sums(1, "ga")
+        op(V, "pz", lambda g, T, x: [g.vector.memset(T["pc" + Z][:], 0.0)], [], nb("pc", 0, 16))
+        plane = lambda a: lambda T: T["pc" + Z][:, :, 8 * a:8 * a + 8]
+        for z, (a, b, queue) in enumerate(G0):
+            gather("g%d" % z, "ga", "x0", a, b, ["x0"], queue)
+        for b in range(B):
+            sums(b, "ga")
         send(0)
+        pvs = nm("@pv0", "@pv1", "@pv2", "@pv3")[:B]
+        pos = ["@d%d0" % q, "@d%d1" % q, "@pm" + Z, "@pn" + Z]
         for r in range(RO):
             at[1] = r - 1
-            for a in (0, 1):
-                gather("gt%d" % a, "gt", "tt", a, ["tta", "ttb"])
-            at[1] = r
+            for z, (a, b) in enumerate(GT):
+                gather("gt%d" % z, "gt", "tt", a, b, ["tta", "ttb"])
             src = ["arr%d_%d" % (q, r), "own%d_%d" % (q, r)]
-            pt = "pc%d_%d_" % (q, r)
+            eq = 3 * r + (0 if RELU else 2)
             whole = lambda b: lambda T: T[b + Z][:]
-            part = lambda b, a: lambda T: T[b + Z][:, a * F:a * F + F]
+            part = lambda b, a: lambda T: T[b + Z][:, a * L:a * L + L]
             ranks = lambda a, r=r: lambda T: rc(T, r, a, a + 2)
-            plane = lambda a, r=r: lambda T: T["pc" + Z][:, r, :, a, :]
+            mean = lambda T: T[PV][:, 1, 0:L]
+            if TJQ is None:
+                op(V, "cl", lambda g, T, x, r=r: [g.vector.tensor_scalar(T["mn" + Z][:], rc(T, r, x["rank"], x["rank"] + 1), (END - 0.25) / 32.0, None, A.min)],
+                   src[1:], nm("mn"))
+                k = op(P, "sa", lambda g, T, x: [g.tensor.matmul(mean(T), T.eyeq[:], T["mn" + Z][:], True, False)], nm("mn") + ["eyeq"], nm("@pv1", "@pv0"), banks=[PV])
+            elif PESUM:
+                k = op(P, "sa", lambda g, T, x, r=r: [g.tensor.matmul(mean(T), T.eyeq[:], rc(T, r, x["rank"], x["rank"] + 1), True, False)],
+                       src[1:] + ["eyeq"], nm("@pv1", "@pv0"), banks=[PV])
+            at[1] = r
             two("xx", whole("xx"), ranks(0), ranks(2), A.max, src, nm("xx"))
-            two("xn", whole("xn"), ranks(0), ranks(2), A.min, src, nm("xn"))
-            two("mn", whole("mn"), part("xn", 0), part("xn", 1), A.min, nm("xn"), nm("mn"))
             two("mx", whole("mx"), part("xx", 0), part("xx", 1), A.max, nm("xx"), nm("mx"))
-            two("hi", plane(0), part("xx", 0), part("xx", 1), A.max, nm("xx"), [pt + "h"])
-            two("lo", plane(1), whole("mx"), plane(0), A.subtract, nm("mx") + [pt + "h"], [pt + "l"])
-            two("eq", plane(2), whole("mx"), whole("mn"), A.is_equal, nm("mx", "mn"), [pt + "n"])
-            op(V, "vt", lambda g, T, x, r=r: [g.vector.transpose(T["lt" + Z][:], T["pc" + Z][:, r])], [pt + "h", pt + "l", pt + "n"] + nm("pz"), nm("lt"))
-            op(P, "pb", lambda g, T, x: [
-                g.tensor.matmul(T[PV][:, :, 64 * b + k:64 * b + 64:2], T.bc[:, 128 * b:128 * b + 128], T["lt" + Z][:, :, k, :], True, True)
-                for k in (0, 1) for b in range(4)], nm("lt") + ["bc"], [], 8, banks=[PV])
-            hits(q, r)
-            pn = lambda T: T[PO][:, 384:384 + L]
-            op(P, "bm", lambda g, T, x: [g.tensor.matmul(pn(T), T.eyeb[:], T.oh[:, cols], True, False)], nm("oh") + ["eyeb"], [], banks=[PO])
-            for a in range(4):
-                op(V, "ct%d" % a, lambda g, T, x, a=a: [
-                    g.vector.tensor_tensor(T["cm" + Z][:, a:N:4], T["gt" + Z][:, a:N:4], T[PV][:, :, a:H:4], A.is_lt)],
-                   nm("gt0", "gt1"), nm("cm%d" % a), banks=[PV])
-            for a in range(4):
-                op(P, "pn%d" % a, lambda g, T, x, a=a: [
-                    g.tensor.matmul(pn(T), T.sr[:, 15 - i:143 - i], T["cm" + Z][:, i:N:16], False, i == 15) for i in range(a, 16, 4)],
-                   nm("cm%d" % a) + ["sr"], [], 4, banks=[PO])
-            op(S, "of", lambda g, T, x: [g.scalar.activation(T.off[:, cols], pn(T), CPY)], [], nm("off"), banks=[PO])
-            to = "oh" if r < RO - 1 else "ob"
-            op(S, "ob", lambda g, T, x, to=to: [g.scalar.activation(T[to][:, cols], pn(T), CPY)], [], nm(to), banks=[PO])
-            for a in (0, 1):
-                gather("ga%d" % a, "ga", "ti", a, ["ti", "sc"], scale="sc")
-            for a in (0, 1):
-                h = slice(a * H, a * H + H)
-                op(V, "ca%d" % a, lambda g, T, x, h=h, a=a: [
-                    g.vector.tensor_tensor(T["cc" + Z][:, h], T["ga" + Z][:, h], T[PV][:, a], A.is_lt)], nm("ga%d" % a), nm("cc%d" % a), banks=[PV])
-            if r == RO - 1 and q not in FIN:
-                break
-            for a, b, pd in ((0, PO, lambda T: T[PO][:, 0:H]), (1, PV, lambda T: T[PV][:, 0])):
-                h = slice(a * H, a * H + H)
-                op(P, "dd%d" % a, lambda g, T, x, h=h, pd=pd: [g.tensor.matmul(pd(T), T.dm[:], T["cc" + Z][:, h], True, True)],
-                   nm("cc%d" % a) + ["dm"], [], banks=[b])
-                if a == 1 and r < RO - 1:
-                    for k in (0, 1):
-                        op(V, "mu%d" % (1 + k), lambda g, T, x, k=k: [
-                            g.vector.tensor_tensor(T["pp" + Z][:, L // 2:L, :, k:4:2], T["ga" + Z][:, H + k:N:2], T[PV][:, 0, k:H:2], A.mult)],
-                           nm("ga1"), nm("pp1", "pp2")[k:k + 1], banks=[b])
-                    for k in (0, 1):
-                        op(P, "ps%d" % (1 + k), lambda g, T, x, k=k: [
-                            g.tensor.matmul(T[PO][:, H + 16 + 8 * k:H + 24 + 8 * k], T["pp" + Z][:, L // 2:L, :, k:4:2], T.indf[:], True, True)],
-                           nm("pp1", "pp2")[k:k + 1] + ["indf"], [], banks=[PO])
-                    continue
-                op(V, "mu%d" % a, lambda g, T, x, a=a, h=h, pd=pd: [
-                    g.vector.tensor_tensor(T["pp" + Z][:, a * L // 2:a * L // 2 + L // 2], T["ga" + Z][:, h], pd(T), A.mult)],
-                   nm("ga%d" % a), nm("pp%d" % a, "pp%d" % (2 * a)), banks=[b])
-                if r < RO - 1:
-                    sums(a, "pp")
+            if HIQ == V:
+                two("hi", plane(eq + 1), part("xx", 0), part("xx", 1), A.max, nm("xx"), nb("pc", eq + 1, eq + 2))
+            else:
+                copy(S, "hi", plane(eq + 1), whole("mx"), nm("mx"), nb("pc", eq + 1, eq + 2))
+            two("lo", plane(eq + 2), whole("mx"), plane(eq + 1), A.subtract, nm("mx") + nb("pc", eq + 1, eq + 2), nb("pc", eq + 2, eq + 3))
+            if PESUM:
+                op(P, "sb", lambda g, T, x, r=r: [g.tensor.matmul(mean(T), T.eyeq[:], rc(T, r, a, a + 1), False, z == NR - 2)
+                                                  for z, a in enumerate(a for a in range(NR) if a != x["rank"])], src[:1] + ["eyeq"], nm("@pv1"), NR - 1, banks=[PV], order=(k,))
+                two("eq", plane(eq), whole("mx"), mean, A.is_equal, nm("mx", "@pv1"), nb("pc", eq, eq + 1), banks=[PV])
+            else:
+                two("xn", whole("xn"), ranks(0), ranks(2), A.min, src, nm("xn"))
+                two("mn", whole("mn"), part("xn", 0), part("xn", 1), A.min, nm("xn"), nm("mn"))
+                two("eq", plane(eq), whole("mx"), whole("mn"), A.is_equal, nm("mx", "mn"), nb("pc", eq, eq + 1))
+            op(V, "vt", lambda g, T, x, eq=eq: [g.vector.transpose(T["lt" + Z][:], T["pc" + Z][:, :, 8 * eq:8 * eq + 32])], nb("pc", eq, eq + 4), nm("lt"))
+            op(P, "pb", lambda g, T, x: [g.tensor.matmul(T[PV][:, 0:B, 32 * b:32 * b + 32], T.bc[:, 128 * b:128 * b + 128], T["lt" + Z][:], True, True)
+                                         for b in range(4)], nm("lt") + ["bc"], pvs, 4, banks=[PV])
+            for a in () if RELU else (0, 1):
+                two("hv%d" % a, plane(3 * r + a), plane(eq + 1 + a), plane(eq), A.mult, nb("pc", eq, eq + 1) + nb("pc", eq + 1 + a, eq + 2 + a),
+                    nb("pc", 3 * r + a, 3 * r + a + 1))
+            pn = lambda T: T.pz[:, 0, 8 * q:8 * q + 8] if KEEP else T[PO][:, 3, 0:L // 4]
+            bm = lambda g, T: g.tensor.matmul(pn(T), T.eyeb[:], T.oh[:, cols], True, False)
+            PN, pnt = ("pz", nm("@pk")) if KEEP else (PO, nm("@pn"))
+            if KEEP:
+                k = keep
+            elif COUNT == "list":
+                k = op(P, "bm", lambda g, T, x: [bm(g, T)], nm("oh") + ["eyeb"], nm("@pn", "@open"), banks=[PO])
+            for a in range(CT):
+                two("ct%d" % a, lambda T, a=a: T["cm" + Z][:, a:N:CT] if COUNT == "list" else rows(T, "cm", a, a + 1), lambda T, a=a: T["gt" + Z][:, a:N:CT],
+                    lambda T, a=a: T[PV][:, 0:B, a:128:CT], A.is_lt, nb("gt", 0, B) + pvs, nb("cm", a, a + 1), banks=[PV], order=[len(ops) - 1] if a else [])
+            for a in range(CT) if COUNT == "list" else ():
+                k = op(P, "pn%d" % a, lambda g, T, x, a=a: [
+                    g.tensor.matmul(pn(T), T.sr[:, 15 - i:143 - i], T["cm" + Z][:, i:N:16], False, i == 15 and (not KEEP or x.get("stop", False))) for i in range(a, 16, CT)],
+                    nb("cm", a, a + 1) + ["sr"], pnt, 16 // CT, banks=[PN], order=(k,))
+            if COUNT != "list":
+                op(P, "pc", lambda g, T, x: [g.tensor.matmul(T[PO][:, 2, 2 * k:2 * k + 2], T["cm" + Z][:, k:N:4], T.indb[:], True, True) for k in range(4)],
+                   nb("cm", 0, 4) + ["indb"], nm("@pm", "@open"), 4, banks=[PO])
+                pm = lambda T: T[PO][:, 2, 0:8]
+                if COUNT == "f32":
+                    op(V, "nt", lambda g, T, x: [g.vector.transpose(T["nt" + Z][:], pm(T))], nm("@pm"), nm("nt"), banks=[PO])
                 else:
-                    op(P, "ps%d" % a, lambda g, T, x, a=a: [
-                        g.tensor.matmul(T[PO][0:32, H + 64 * a:H + 64 * a + 64], T.zt[:, 3 - k:35 - k],
-                                        T["pp" + Z][:, a * L // 2:a * L // 2 + L // 2, k, :], k == 0, k == 3) for k in range(4)],
-                       nm("pp%d" % a) + ["zt"], [], 4, banks=[PO])
+                    copy(COUNT, "nb", whole("nb"), pm, nm("@pm"), nm("nb"), banks=[PO])
+                    op(V, "nt", lambda g, T, x: [g.vector.transpose(T["nt" + Z][:], T["nb" + Z][:])], nm("nb"), nm("nt"))
+                k = op(P, "bm", lambda g, T, x: [bm(g, T)], nm("oh") + ["eyeb"], nm("@pn", "@open"), banks=[PO])
+                op(P, "pn", lambda g, T, x: [g.tensor.matmul(pn(T), T.pm[:], T["nt" + Z][:], False, True)], nm("nt") + ["pm"], nm("@pn"), banks=[PO], order=(k,))
+            copy(OFQ, "of", lambda T: T.off[:, cols], pn, pnt, nm("off"), banks=[PN])
+            to = "oh" if r < RO - 1 else "ob"
+            if r == RO - 1 or not KEEP:
+                copy(OBQ, "ob", lambda T, to=to: T[to][:, cols], pn, pnt, nm(to), banks=[PN])
+            fin = r == RO - 1 and q == FIN
+            for z, (a, b) in enumerate(GA if r < RO - 1 or q == FIN else GL):
+                if S0Q == S and r < RO - 1 and TJQ:
+                    op(S, "ga%d" % z, lambda g, T, x, a=a, b=b: [
+                        g.scalar.activation(rows(T, "ga", a, b), T["tj" if x["rank"] == 1 else "ti"][:, 0:W].indirect(T.off[:, c0 + 8 * a:c0 + 8 * b]),
+                                            *((ActivationFunctionType.Identity, T.sb[:, 1:2], T.sb[:, 0:1]) if x["rank"] == 1 and TJQ == S else (CPY, 0.0, T.sc[:])))],
+                       ti + ["sc", "sb"] + ["tj%d" % y for y in range(TJ)] + nm("off"), nb("ga", a, b))
+                else:
+                    gather("ga%d" % z, "ga", "ti", a, b, ti + ["sc"], scale="sc")
+                if CA is None:
+                    two("ca%d" % z, lambda T, a=a, b=b: rows(T, "cc", a, b), lambda T, a=a, b=b: rows(T, "ga", a, b), lambda T, a=a, b=b: T[PV][:, a:b],
+                        A.is_lt, nb("ga", a, b) + pvs[a:b], nb("cc", a, b), banks=[PV])
+            for z, (a, b) in enumerate((CA if r < RO - 1 else CL) or ()):
+                two("ca%d" % z, lambda T, a=a, b=b: rows(T, "cc", a, b), lambda T, a=a, b=b: rows(T, "ga", a, b), lambda T, a=a, b=b: T[PV][:, a:b],
+                    A.is_lt, nb("ga", a, b) + pvs[a:b], nb("cc", a, b), banks=[PV])
+            if r == RO - 1 and not fin:
+                break
+            for z, (a, b, bank, at0) in enumerate(DD or ()):
+                reg = pos if bank == "po" else pvs
+                op(P, "dd%d" % z, lambda g, T, x, a=a, b=b, bank=bank, at0=at0: [
+                    g.tensor.matmul(T[bank + Z][:, at0:at0 + b - a], T.dm[:], rows(T, "cc", a, b), True, True)],
+                   nb("cc", a, b) + ["dm"], reg[at0:at0 + b - a] + (nm("@open") if bank == "po" else []), banks=[bank + Z])
+                for y, (c, d) in enumerate(MU):
+                    if a <= c < b:
+                        two("mu%d" % y, lambda T, c=c, d=d: rows(T, "pp", c, d), lambda T, c=c, d=d: rows(T, "ga", c, d),
+                            lambda T, u=at0 + c - a, v=at0 + d - a, bank=bank: T[bank + Z][:, u:v], A.mult,
+                            nb("ga", c, d) + reg[at0 + c - a:at0 + d - a], nb("pp", c, d), banks=[bank + Z])
+            for b in range(0 if DD else B):
+                bank, at0, tok = (PO, b // 2, "@d%d%d" % (q, b // 2)) if b % 2 == 0 else ("pz", q, "@z" + Z)
+                pd = lambda T, bank=bank, at0=at0: T[bank][:, at0]
+                op(P, "dd%d" % b, lambda g, T, x, b=b, pd=pd: [g.tensor.matmul(pd(T), T.dm[:], rows(T, "cc", b, b + 1), True, True)],
+                   nb("cc", b, b + 1) + ["dm"], [tok] + (nm("@open") if bank == PO else []), banks=[bank])
+                if not fin:
+                    two("mu%d" % b, lambda T, b=b: rows(T, "pp", b, b + 1), lambda T, b=b: rows(T, "ga", b, b + 1), pd, A.mult,
+                        nb("ga", b, b + 1) + [tok], nb("pp", b, b + 1), banks=[bank])
+                    continue
+                op(V, "mu%d" % b, lambda g, T, x, b=b, bank=bank, at0=at0: [
+                    g.vector.tensor_tensor(T.pl[:, f, 8 * b:8 * b + 8], T["ga" + Z][:, 128 * b + f:128 * b + 128:2], T[bank][:, at0, :, :, f], A.mult) for f in (0, 1)],
+                   nb("ga", b, b + 1) + [tok], nb("pp", b, b + 1), 2, banks=[bank])
+                op(P, "ps%d" % b, lambda g, T, x, b=b: [
+                    g.tensor.matmul(T.pv0[0:32, 0:2, 16 * b:16 * b + 16], T.zt[:, 3 - k:35 - k], T.pl[:, :, 8 * b:8 * b + 8, k, :], k == 0, k == 3)
+                    for k in range(4)], nb("pp", b, b + 1) + ["zt"], ["@pv00", "@pv10", "@fin%d" % b], 4, banks=["pv0"])
+            if not fin:
+                for b in range(B):
+                    sums(b, "pp")
             if r < RO - 1:
                 send(r + 1)
-        if q in FIN:
-            op(V, "e6", lambda g, T, x: [g.vector.tensor_copy(T["oc" + Z][0:32, L * b:L * b + L], T[PO][0:32, H + b:H + 128:4]) for b in range(4)],
-               [], nm("oc"), 4, banks=[PO])
+        if q == FIN:
+            op(V, "e6", lambda g, T, x: [g.vector.tensor_copy(T.oo[0:32, 2 * e:2 * e + 2, cols], T.pv0[0:32, 0:2, e:16 * B:2]) for e in (0, 1)],
+               ["@fin%d" % b for b in range(B)], nm("oc"), 2, banks=["pv0"])
+        elif LAST == 4:
+            for z, (a, b) in enumerate(CL or GL):
+                op(P, "dd%d" % z, lambda g, T, x, a=a, b=b: [g.tensor.matmul(T[PO][:, a:b], T.dm[:], rows(T, "cc", a, b), True, True)],
+                   nb("cc", a, b) + ["dm"], pos[a:b], banks=[PO])
+            for b in range(4):
+                two("mu%d" % b, lambda T, b=b: rows(T, "pp", b, b + 1), lambda T, b=b: T["ga" + Z][:, b:N:4], lambda T, b=b: T[PO][:, :, :, b // 2, b % 2],
+                    A.mult, nb("ga", 0, 4) + pos, nb("pp", b, b + 1), banks=[PO])
+            for k in range(4):
+                op(P, "ps%d" % k, lambda g, T, x, k=k: [g.tensor.matmul(T[PV][:, 0, k:32:4], T["pp" + Z][:, k:N:4], T.zt[:, 3:35:4], True, True)],
+                   nb("pp", 0, 4) + ["zt"], nm("@pv0") + nb("@yc", k, k + 1), banks=[PV])
+            op(V, "e6", lambda g, T, x: [g.vector.transpose(T.oc[:, cols], T[PV][:, 0, 0:32])], nb("@yc", 0, 4), nm("oc"), banks=[PV])
         else:
-            for a in (0, 1):
-                h = slice(a * H, a * H + H)
-                op(P, "dd%d" % a, lambda g, T, x, h=h: [g.tensor.matmul(T[PO][:, h], T.dm[:], T["cc" + Z][:, h], True, True)],
-                   nm("cc%d" % a) + ["dm"], [], banks=[PO])
-            for a in (0, 1):
-                op(V, "mu%d" % a, lambda g, T, x, a=a: [g.vector.tensor_tensor(T["pp" + Z][:, :, :, a:4:2], T["ga" + Z][:, a:N:2], T[PO][:, a:N:2], A.mult)],
-                   nm("ga0", "ga1"), nm("pp%d" % a, "pp%d" % (2 * a)), banks=[PO])
-            for a in (0, 1):
-                op(P, "ps%d" % a, lambda g, T, x, a=a: [
-                    g.tensor.matmul(T[PV][:, 0, 8 * k:8 * k + 8], T["pp" + Z][:, :, :, k], T.indf[:], True, True) for k in (a, a + 2)],
-                   nm("pp%d" % a) + ["indf"], [], 2, banks=[PV])
-            op(V, "e1", lambda g, T, x: [g.vector.tensor_copy(T["yp" + Z][:, 0:F], T[PV][:, 0, 0:F])], [], nm("yp"), banks=[PV])
-            op(V, "e2", lambda g, T, x: [g.vector.tensor_tensor(T["yp" + Z][:, F:2 * F], T[PV][:, 0, 0:F], T["yp" + Z][:, 0:F], A.subtract)],
-               nm("yp"), nm("yq"), banks=[PV])
-            op(P, "e3", lambda g, T, x: [g.tensor.matmul(T[PO][0:64, 0:128], T["yp" + Z][:], T.eyeb[:], True, True)], nm("yp", "yq") + ["eyeb"], [], banks=[PO])
-            op(S, "e4", lambda g, T, x: [g.scalar.activation(T["ft" + Z][0:64, :], T[PO][0:64, 0:128], CPY)], [], nm("ft"), banks=[PO])
-            op(P, "e5", lambda g, T, x: [g.tensor.matmul(T[PO][:, 384:384 + L], T.cv[0:64, 12 - 4 * w:140 - 4 * w], T["ft" + Z][0:64, w:128:4], w == 0, w == 3)
-                                         for w in range(4)], nm("ft") + ["cv"], [], 4, banks=[PO])
-            op(V, "e6", lambda g, T, x: [g.vector.tensor_copy(T["oc" + Z][:, 0:L], T[PO][:, 384:384 + L])], [], nm("oc"), banks=[PO])
-        store("yb", q, lambda T: T.ob[:, cols], "ob" + Z)
-        store("yc", q, lambda T: T["oc" + Z][0:32, :] if q in FIN else T["oc" + Z][:, 0:L], "oc" + Z)
+            for h, bank, tok in ((0, PO, ["@d%d0" % q, "@d%d1" % q]), (1, PV, pvs[0:2])):
+                op(P, "dd%d" % h, lambda g, T, x, h=h, bank=bank: [g.tensor.matmul(T[bank][:, 0:2], T.dm[:], rows(T, "cc", 2 * h, 2 * h + 2), True, True)],
+                   nb("cc", 2 * h, 2 * h + 2) + ["dm"], tok, banks=[bank])
+                op(V, "mu%d" % h, lambda g, T, x, h=h: [
+                    g.vector.tensor_tensor(T["pp" + Z][:, 128 * b + 64 * h:128 * b + 64 * h + 64], T["ga" + Z][:, 256 * h + b:256 * h + 256:4],
+                                           T[PV][:, 0:2, b:128:4] if h else T[PO][:, 0:2, :, b // 2, b % 2], A.mult) for b in range(4)],
+                   nb("ga", 2 * h, 2 * h + 2) + tok, ["pq%d" % h + Z] + nb("pp", 0, 4 - 4 * h), 4, banks=[bank])
+            for k in range(4):
+                op(P, "ps%d" % k, lambda g, T, x, k=k: [g.tensor.matmul(T[PO][:, 2, 0:8, k // 2, k % 2], T["pp" + Z][:, k:N:4], T.zt[:, 3:35:4], True, True)],
+                   nm("pq0", "pq1") + ["zt"], nm("@pm") + nb("@yc", k, k + 1), banks=[PO])
+            op(V, "e6", lambda g, T, x: [g.vector.transpose(T.oc[:, cols], T[PO][:, 2, 0:8])], nb("@yc", 0, 4), nm("oc"), banks=[PO])
+        PH, ph = HB[q], ["@" + HB[q]]
+        op(P, "h1", lambda g, T, x: [g.tensor.matmul(T[PH][0:120, :, 8 * b:8 * b + 8], T["pc" + Z][:, b, 0:120], T.eyep[:], True, True) for b in range(B)],
+           nb("pc", 0, 15) + ["eyep"], ph, B, banks=[PH])
+        copy(H2Q, "h2", lambda T: T["fa" + Z][0:120, :], lambda T: T[PH][0:120, :, 0:L], ph, nm("fa"), banks=[PH])
+        zs = (0, 1) if RELU else (1,)
+        op(P, "h3", lambda g, T, x: [g.tensor.matmul(T[PH][:, z, 0:L], T.cu[0:120, z, 3 - k:131 - k], T["fa" + Z][0:120, k:N:4], k == 0, k == 3 and z == zs[0])
+                                     for z in zs for k in range(4)], nm("fa") + ["cu"], ph, 4 * len(zs), banks=[PH])
+        if RELU:
+            op(S, "h4", lambda g, T, x: [g.scalar.activation(T["zr" + Z][:], T[PH][:, 0, 0:L], ActivationFunctionType.Relu, bias=-BIG)], ph, nm("zr"), banks=[PH])
+            op(P, "h5", lambda g, T, x: [g.tensor.matmul(T[PH][:, 1, 0:L], T.sm[:], T["zr" + Z][:], False, True)], nm("zr") + ["sm"], ph, banks=[PH])
+        copy(H6Q, "h6", lambda T: T.oo[64:128, :, cols], lambda T: T[PH][64:128, 1, 0:L], ph, nm("oo"), banks=[PH])
 
-    def last(q):
-        Z = str(q)
-        at[:] = [q, RO - 1]
-        op(S, "hf", lambda g, T, x: [g.scalar.activation(T["hf" + Z][:, h, 0:64], T["pc" + Z][:, :, 2 * h:2 * h + 2, 2, :], CPY, scale=0.03125) for h in (0, 1)],
-           ["pc%d_%d_n" % (q, r) for r in range(RO)], ["hf" + Z], 2)
-        op(P, "h1", lambda g, T, x: [g.tensor.matmul(T.pf0[:, 2 * i + h, :], T[b + Z][:, h], T.eyeb[:], True, True) for i, b in enumerate(("hv", "hf")) for h in (0, 1)],
-           ["hv%d" % r + Z for r in range(RO)] + ["hf" + Z, "pz" + Z, "eyeb"], [], 4, banks=["pf0"])
-        op(H2, "h2", lambda g, T, x: [g.scalar.activation(T["fa" + Z][:], T.pf0[:], CPY) if H2 == S else g.vector.tensor_copy(T["fa" + Z][:], T.pf0[:])],
-           [], ["fa" + Z], banks=["pf0"])
-        op(P, "h3", lambda g, T, x: [g.tensor.matmul(T.pf1[:, 0:2 * L], T.cu[:, 14 - 2 * w:142 - 2 * w], T["fa" + Z][:, w:512:8], w == 0, w == 7)
-                                     for w in range(8)], ["fa" + Z, "cu"], [], 8, banks=["pf1"])
-        op(S, "h4", lambda g, T, x: [g.scalar.activation(T["oo" + Z][:], T.pf1[:, 0:2 * L], CPY)], [], ["oo" + Z], banks=["pf1"])
-        store("yh", q, lambda T: T["oo" + Z][:, L:2 * L], "oo" + Z)
-        store("ys", q, lambda T: T["oo" + Z][:, 0:L], "oo" + Z)
     for q in range(NC):
         chunk(q)
-    for q in range(NC):
-        last(q)
+    if TIW is not None:
+        ops[l1]["deps"].add([o["n"] for o in ops if o["name"] == "s0" and o["at"] == (TIW, -1)][0])
+        ops[l1]["order"].add([o["n"] for o in ops if o["name"] == "ex" and o["at"] == (TIW, -1)][0])
+    at[:] = [None, RO]
+
+    def store(queue, dst, src, tok):
+        op(queue, "out", lambda g, T, x: [(g.sync if queue == "sync" else g.scalar).dma_start(dst(T), src(T))], tok, [], 16)
+    every = lambda k: [k + str(q) for q in range(NC)]
+    for y, src, tok in (("yb", lambda T: T.ob[:], "ob"), ("ys", lambda T: T.oo[64:96], "oo"), ("yh", lambda T: T.oo[96:128], "oo")):
+        store("sync", lambda T, y=y: T[y][:], src, every(tok))
+    n = 96 if FIN is None else 64
+    for b in range(4):
+        store(YQ[b], lambda T, b=b: T.yc[b:128:4, 0:n], lambda T, b=b: T.oc[32 * b:32 * b + 32, 0:n], every("oc")[:n // 32])
+    if FIN is not None:
+        store("sync", lambda T: T.yc[:, n:96], lambda T: T.oo[0:32, :, n:96], every("oc")[2:])
     return ops
 
 
@@ -309,7 +520,7 @@ def schedule(ops, key):
     left = {o["n"]: len(o["deps"] | o["order"]) for o in ops}
     ready, order = [n for n in left if left[n] == 0], []
     while ready:
-        n = min(ready, key=lambda k: (key[k], k))
+        n = min(ready, key=lambda k: (key.get(k, k), k))
         order.append(n)
         ready.remove(n)
         for k in after[n]:
@@ -319,75 +530,87 @@ def schedule(ops, key):
     return order
 
 
-def plan():
+def plan(key, rank=1):
     ops = build()
-    order = schedule(ops, KEY or list(range(len(ops))))
+    order = [i for i in schedule(ops, key) if ops[i].get("only", rank) == rank]
     pos = {i: z for z, i in enumerate(order)}
-    known, clos, waits, waited = {}, {}, {}, set()
+    known, clos, waits, waiters, bank = {}, {}, {}, {}, {}
     for i in order:
         o = ops[i]
         q = o["q"]
         if q == "remote":
             clos[i] = 1 << i
             continue
+        deps = set(d for d in o["deps"] if d in pos)
+        for b in o["banks"]:
+            acc = bank.get(b, [])
+            deps.update(d for d in acc if ops[d]["q"] != q)
+            bank[b] = [d for d in acc if ops[d]["q"] == q] + [i]
         k = known.get(q, 0)
-        ws = []
-        for d in sorted(o["deps"], key=lambda d: -pos[d]):
-            if not (k >> d) & 1:
-                if ops[d]["ninc"] == 0 and ops[d]["q"] != "remote":
-                    continue
-                ws.append(d)
+        waits[i] = []
+        for d in sorted(deps, key=lambda d: -pos[d]):
+            if not (k >> d) & 1 and (ops[d]["ninc"] or ops[d]["q"] == "remote"):
+                waits[i].append(d)
+                waiters.setdefault(d, set()).add(i)
                 k |= clos[d]
-        ws = [d for d in ws if not any(e != d and (clos[e] >> d) & 1 for e in ws)]
-        waits[i] = ws
-        waited.update(ws)
         known[q] = k
         clos[i] = k | (1 << i)
-    cnt, val = {}, {}
+    val, pool, cnt = {}, {}, {}
     for i in order:
         o = ops[i]
-        if o["q"] != "remote" and o["ninc"] and (i in waited or o["sem"] == "out"):
-            cnt[o["sem"]] = cnt.get(o["sem"], 0) + o["ninc"]
-            val[i] = cnt[o["sem"]]
-    return ops, order, waits, val, cnt
+        if o["q"] == "remote":
+            val[i] = (o["sem"], None)
+        elif o["ninc"] and (i in waiters or o["name"] == "out"):
+            sem = o["name"]
+            if o["q"] != "sync" and sem != "out":
+                undone = {s: [d for d in on if not (clos[i] >> d) & 1] for s, on in pool.items() if ops[on[0]]["q"] == o["q"]}
+                fit = [s for s, on in undone.items() if all(waiters[d] <= waiters[i] for d in on)]
+                sem = max(fit, key=lambda s: len(undone[s])) if fit else "s%d" % len(pool)
+                pool.setdefault(sem, []).append(i)
+            cnt[sem] = cnt.get(sem, 0) + o["ninc"]
+            val[i] = (sem, cnt[sem])
+    need = {i: {} for i in waits}
+    for i in waits:
+        for d in waits[i]:
+            sem, n = val[d]
+            need[i][sem] = n if n is None else max(n, need[i].get(sem, 0))
+    return ops, order, need, val, cnt
 
 
-OPS, ORDER, WAITS, VAL, CNT = plan()
-SEMAPHORES = sorted(CNT) + ["ar%d_%d" % (q, r) for q in range(NC) for r in range(RO)] + ["sent"]
+PLANS = [plan(KEY, rank) for rank in (0, 1)]
+SEMAPHORES = sorted(set(PLANS[0][4]) | set(PLANS[1][4])) + ["ar%d_%d" % (q, r) for q in range(NC) for r in range(RO)] + ["sent"]
+
+
+def context(rank, core, T, topo):
+    peers = [c for c in T.cores if c != core]
+    chip = topo.cores_of(core)
+    far = [c for c in peers if c not in chip]
+    near = [c for c in peers if c in chip]
+    out = topo.engines(core, far[0])
+    ins = [k for k in topo.engines(core, near[0]) if k not in out][:len(out) // len(far)]
+    bits = lambda e: sum(1 << k for k in e)
+    return {"rank": rank, "peers": [([topo.addr(c, core) for c in far], bits(out)), ([topo.addr(c, core) for c in near], bits(ins))],
+            "inn": len(out) * len(far) + len(ins) * len(near), "sent": len(out) + len(ins)}
 
 
 def rank_program(g, core, T, topo):
     rank = T.rank_of(core)
     if rank is None:
         return
-    peers = [c for c in T.cores if c != core]
-    chip = topo.cores_of(core)
-    far = [c for c in peers if c not in chip]
-    near = [c for c in peers if c in chip]
-    masks = {}
-    used = []
-    for i, c in enumerate(far):
-        e = topo.engines(core, c)
-        e = e[i * (len(e) // len(far)):(i + 1) * (len(e) // len(far))]
-        used += e
-        masks[c] = e
-    for i, c in enumerate(near):
-        e = [k for k in topo.engines(core, c) if k not in used][4 * i:4 * i + 4]
-        masks[c] = e
-    inn = sum(len(masks[c]) for c in peers)
-    x = {"rank": rank, "peers": [(topo.addr(c, core), sum(1 << k for k in masks[c])) for c in far + near]}
+    x = context(rank, core, T, topo)
+    OPS, ORDER, WAITS, VAL, CNT = PLANS[int(rank == 1)]
     queue = {"sync": g.sync, "scalar": g.scalar, "vector": g.vector, "tensor": g.tensor, "gpsimd": g}
     for i in ORDER:
         o = OPS[i]
         if o["q"] == "remote":
             continue
         e = queue[o["q"]]
-        for d in WAITS[i]:
-            p = OPS[d]
-            e.wait_ge(T.sem[p["sem"]], inn if p["q"] == "remote" else VAL[d])
+        for sem, n in WAITS[i].items():
+            e.wait_ge(T.sem[sem], x["inn"] if n is None else n)
+        x["stop"] = i == [k for k in ORDER if OPS[k]["name"][:2] == "pn"][-1]
         ins = o["emit"](g, T, x)
         if i in VAL:
             for k in ins:
-                k.then_inc(T.sem[o["sem"]], o["ninc"] // len(ins))
+                k.then_inc(T.sem[VAL[i][0]], o["ninc"] // len(ins))
     g.sync.wait_ge(T.sem["out"], CNT["out"])
-    g.wait_ge(T.sem["sent"], inn * NC * RO)
+    g.wait_ge(T.sem["sent"], x["sent"] * NC * RO)

import numpy as np
from concourse.bass import DstId, RemoteDMATransfer
from concourse.mybir import AluOpType, ActivationFunctionType, AxisListType

RO, NR, W, END = 4, 4, 1536, 2 ** 20 - 1
BIG = float(2 ** 21)
BL = (4, 4, 4)
NC = len(BL)
FIN = None
ZV, ZS = 704, 1216
TA = 24
CT = 4
GA = ((0, 2), (2, 3), (3, 4))
GT = ((0, 2), (2, 4))
G0 = ((0, 1, "vector"), (1, 2, "scalar"), (2, 3, "vector"), (3, 4, "scalar"))
PESUM, RELU, COUNT = False, False, "f32"
GL = ((0, 2), (2, 4))
PSB, CA, CL, DD, MU, LAST = "pv", None, None, None, None, 8
S0Q, TJ, HB, HIQ = "vector", 1, ("pf", "pf", "pf"), "vector"
TJQ, KEEP, TI, TIW = "scalar", False, 1, None
YQ = ("sync", "scalar", "sync", "scalar")
OFQ, OBQ, H2Q, H6Q = "scalar", "scalar", "scalar", "scalar"
SEQ = [
    0,5,2,3,1,4,6,9,18,14,13,17,47,7,441,244,12,19,36,11,15,21,41,16,22,45,24,27,46,28,44,10,20,267,464,23,70,48,8,50,49,52,53,54,245,35,51,55,42,248,60,
    246,56,31,29,249,32,33,57,250,30,61,247,34,443,442,251,445,252,454,446,253,254,59,444,447,25,257,256,448,449,450,455,37,258,453,26,451,38,58,62,66,63,
    64,65,255,67,68,39,69,263,259,260,71,75,72,76,73,74,264,77,78,452,261,456,262,460,457,79,265,458,459,83,266,461,80,81,85,462,463,87,84,91,268,269,270,
    82,271,105,86,465,272,273,274,89,275,88,92,276,93,469,90,94,95,466,96,278,280,282,467,97,98,99,100,470,468,471,472,281,279,101,284,115,283,286,102,
    473,288,285,290,106,289,287,292,291,294,479,477,295,480,293,475,478,474,277,296,297,481,485,476,301,312,298,104,486,483,487,482,303,484,498,299,489,
    488,490,40,43,103,491,492,493,494,495,496,107,302,111,499,108,109,112,110,500,113,114,116,300,117,304,118,119,305,306,308,309,307,120,121,122,123,124,
    126,310,311,509,497,501,125,128,505,502,503,132,313,317,314,315,316,318,506,319,320,130,129,504,321,136,127,134,507,508,325,133,323,131,137,140,135,
    138,142,143,510,514,326,333,327,329,511,512,513,139,328,141,324,515,516,517,144,145,518,334,330,331,335,160,146,147,519,337,332,151,520,526,336,322,
    338,521,339,527,340,341,342,522,523,528,343,357,524,529,530,149,348,525,344,531,532,533,534,346,536,537,538,347,535,539,554,540,150,541,148,156,545,
    544,152,345,543,153,154,155,157,158,159,349,161,351,350,353,162,163,164,352,354,165,166,167,168,169,171,542,355,356,550,546,548,547,173,358,359,360,
    361,175,172,549,551,362,363,364,177,365,179,174,181,366,552,553,176,180,368,178,183,370,182,187,374,555,184,556,185,186,188,559,189,560,190,557,558,
    369,371,372,191,373,561,562,378,375,376,380,563,196,379,192,565,382,377,170,367,381,384,385,386,566,573,567,383,569,568,387,205,571,564,575,570,388,
    402,195,574,389,576,572,391,577,393,578,579,581,582,580,194,583,584,599,585,588,193,197,586,201,589,198,199,590,392,202,200,203,204,206,207,390,394,
    208,398,587,209,395,396,399,210,211,397,400,212,213,214,401,591,215,595,403,407,404,408,405,406,218,216,222,220,592,593,409,410,411,217,224,596,594,
    631,219,226,221,413,597,598,223,225,415,227,414,600,232,228,233,632,601,421,419,416,229,230,604,605,417,422,602,423,633,634,603,424,231,420,412,606,
    607,418,608,427,234,235,425,635,429,428,610,426,612,611,614,236,237,430,431,618,432,613,619,238,616,433,609,621,637,434,622,239,620,615,435,436,623,
    617,240,636,437,241,438,627,624,625,242,243,439,440,639,628,638,626,629,630,640]
SEQ = [
0,2,3,5,40,9,4,15,14,19,20,13,24,1,11,16,17,6,7,25,33,10,38,21,28,26,41,42,22,46,27,43,29,18,32,45,8,47,48,30,
230,229,49,50,232,51,52,53,54,233,416,414,231,413,234,235,236,23,237,417,56,238,418,57,425,241,228,415,419,420,31,412,
240,421,44,422,34,12,35,239,55,424,58,62,59,36,60,63,61,64,242,246,65,66,243,244,247,423,426,245,248,428,249,69,70,
71,72,250,430,427,431,73,75,74,429,432,253,76,433,434,77,79,83,67,254,255,256,68,81,251,437,438,257,258,259,260,261,
439,440,441,443,80,87,82,442,267,84,85,88,89,86,252,444,91,268,263,435,90,265,92,93,94,445,264,95,96,269,266,447,97,
270,271,98,272,449,277,278,448,273,275,451,450,436,274,455,452,453,457,279,276,280,456,454,459,458,78,284,99,468,461,
281,462,463,100,460,464,102,106,282,104,103,107,465,466,105,108,109,110,37,112,446,111,467,101,283,113,114,115,116,286,
117,290,287,288,291,285,469,39,118,289,292,293,470,119,474,120,121,294,472,471,475,295,473,476,297,477,262,125,123,298,
122,299,144,127,478,126,300,301,303,124,129,133,481,302,304,305,131,482,483,484,485,487,128,130,137,307,309,132,135,486,
488,489,134,136,308,296,310,138,139,140,480,313,315,479,141,314,321,142,491,316,322,311,492,499,495,497,312,317,493,500,
319,145,512,496,318,320,494,498,323,329,503,513,328,143,324,504,501,505,325,502,490,146,506,507,508,150,326,147,148,151,
149,152,509,153,327,155,510,154,156,157,158,159,160,330,334,331,161,162,163,335,332,336,511,333,339,337,518,514,164,165,
338,519,515,516,306,520,167,517,168,521,175,341,342,343,344,522,524,340,188,169,170,171,176,189,345,347,346,172,173,177,
348,349,174,181,525,526,527,528,182,179,529,178,180,351,523,530,353,352,355,183,184,185,531,532,533,354,359,357,356,166,
186,361,360,363,535,358,362,365,364,366,536,537,538,539,373,367,541,542,372,557,368,543,540,369,187,545,556,549,544,547,
546,190,194,550,551,548,552,191,195,192,196,193,370,553,554,197,200,198,199,224,225,534,201,202,203,204,350,205,371,378,
374,207,379,376,375,380,377,226,555,206,208,383,381,382,384,558,562,559,227,408,560,209,563,561,564,385,565,386,213,409,
566,387,388,389,568,567,391,410,569,570,571,390,392,211,572,573,575,212,393,411,395,397,214,215,574,216,217,576,577,592,
593,218,396,398,579,219,220,221,399,400,401,402,594,222,580,581,223,595,582,403,404,583,584,585,586,394,210,598,597,578,
405,406,407,596,587,588,589,590,591,601,600,602,599]
SEQ2 = SEQ
GA = CA = CL = MU = ((0, 2), (2, 4))
COUNT, CT, DD, PSB, LAST, HB, S0Q = "list", 2, ((0, 2, "po", 0), (2, 4, "pv", 0)), "po", 4, ("pf", "pz", "pf"), "scalar"
SEQ = [
2,0,1,3,15,14,5,19,20,9,24,44,16,4,10,38,21,25,28,18,13,29,17,33,39,32,6,47,48,49,50,7,8,205,203,206,204,360,51,52,53,54,55,56,
30,359,207,208,209,210,362,59,214,215,22,361,211,363,212,45,31,364,46,365,366,202,12,57,26,71,58,367,368,11,34,43,27,42,358,23,227,
383,60,64,371,35,213,216,36,40,370,220,217,218,221,369,65,62,219,222,61,372,223,63,66,224,376,67,374,68,373,228,229,230,231,377,375,
378,70,379,380,72,73,232,74,75,234,384,386,235,236,385,76,237,238,239,387,240,78,80,242,243,82,79,241,244,81,388,390,245,246,84,83,86,
391,247,85,392,233,87,88,89,90,249,393,394,395,91,396,397,262,37,69,226,248,251,255,225,77,250,253,252,398,256,254,399,400,401,402,403,
106,257,381,92,258,95,99,93,41,96,97,100,259,405,263,264,404,389,101,98,407,265,406,94,266,411,267,268,102,103,408,409,412,410,413,414,
415,107,108,418,269,284,419,271,109,110,420,270,272,111,273,274,421,422,113,115,275,276,114,116,277,278,117,118,279,280,423,425,281,119,
120,105,426,282,121,122,123,124,424,283,382,297,427,428,125,429,430,126,112,285,431,432,129,141,433,127,104,261,290,286,291,260,434,435,
436,437,438,287,288,440,292,289,417,128,295,293,453,130,294,134,131,132,135,133,136,298,137,138,441,439,299,442,446,300,301,142,143,443,
447,444,144,145,302,304,448,445,416,146,303,449,296,450,140,306,148,454,455,456,457,150,152,149,151,305,153,154,155,308,307,156,157,158,
159,458,461,309,459,310,311,160,161,460,462,147,312,463,313,314,315,316,464,452,465,176,163,319,164,466,467,468,451,469,470,471,472,475,
139,162,165,332,169,166,317,167,170,473,318,168,171,476,320,172,174,488,175,325,321,173,326,474,177,322,198,178,323,327,324,330,199,179,
180,181,200,477,328,481,182,329,478,479,482,183,201,184,331,480,354,483,333,355,335,484,334,485,486,185,186,336,337,187,188,338,339,489,
490,487,190,189,341,192,340,491,492,493,496,510,356,495,343,494,342,514,344,191,193,194,498,348,511,497,195,500,196,499,512,513,357,516,
345,347,346,502,349,350,501,503,504,351,352,197,515,353,505,506,507,508,509,517,520,518,519]
SEQ3 = SEQ
TJQ, TJ, TI, KEEP, HB = "vector", 2, 2, True, ("pf", "pf", "pf")
SEQ = [
5,0,1,2,3,10,4,20,6,16,48,17,21,11,18,22,346,25,46,34,19,14,45,197,26,49,51,50,52,47,29,199,200,201,7,348,61,30,33,53,8,9,54,
55,56,57,58,39,198,31,347,32,202,203,204,205,206,359,207,40,349,358,350,60,351,352,353,210,354,43,355,59,209,356,23,44,62,66,64,63,
208,357,67,12,41,65,68,211,69,215,70,212,213,27,216,214,73,74,217,360,364,218,24,361,365,75,76,28,362,77,78,366,219,222,224,363,223,
225,15,367,79,368,80,82,81,84,226,227,371,372,228,83,229,373,374,375,86,376,85,87,231,230,88,89,90,232,220,233,234,235,377,236,237,91,
378,238,380,239,240,72,379,382,392,381,71,383,35,384,36,221,13,385,386,387,388,92,94,93,95,241,99,97,96,100,370,98,391,389,37,101,369,
102,103,244,248,245,246,249,243,106,107,250,247,390,104,105,108,251,393,397,394,395,398,242,109,110,111,252,255,396,399,112,256,257,253,
254,258,259,400,113,401,114,404,405,115,117,116,260,118,261,262,406,407,408,119,409,120,263,402,121,122,123,410,264,265,266,268,269,267,
270,271,272,411,124,412,127,413,414,273,415,416,417,126,418,419,420,421,38,403,422,276,425,125,132,128,133,129,130,134,274,42,423,131,
135,277,281,275,136,278,279,282,139,140,283,280,426,430,284,428,138,427,431,286,424,137,141,142,143,285,144,429,145,432,288,290,433,434,
289,291,146,147,159,292,148,437,438,149,150,151,439,440,293,152,153,436,154,294,155,295,297,441,296,156,435,298,299,300,442,157,444,443,
287,301,302,457,445,303,446,447,304,305,306,160,158,448,449,161,165,450,451,452,453,454,162,455,163,309,166,164,167,458,168,169,307,171,
170,308,193,172,173,310,314,311,315,194,312,316,456,174,175,176,177,195,313,179,196,319,317,318,459,463,178,320,461,460,342,343,464,321,
462,465,322,468,323,466,324,325,467,326,181,183,344,180,182,327,470,471,472,473,328,474,345,476,184,185,329,331,330,332,469,187,186,491,
334,333,478,188,477,479,492,189,190,191,480,336,335,475,495,481,482,493,484,483,485,494,497,192,337,338,339,340,341,496,486,487,488,489,
490,499,498,500,501]
KEEP, HB, PESUM = False, ("pf", "pz", "pf"), True
SEQ = [
5,0,2,3,20,1,4,40,10,16,21,6,7,23,8,9,48,17,18,26,22,27,46,35,14,41,30,50,11,19,49,51,52,28,206,208,31,53,54,55,56,361,57,364,
58,32,205,62,204,207,365,362,363,61,366,209,33,210,60,211,216,212,213,214,367,368,369,217,218,44,360,24,45,370,59,63,47,64,65,215,373,
374,371,34,67,68,66,219,69,372,385,229,223,70,29,71,220,375,221,224,74,75,222,376,377,73,379,225,380,378,25,381,76,77,226,72,78,79,
230,231,80,382,386,387,82,232,233,388,81,83,389,234,235,84,236,228,85,86,87,237,390,88,89,238,90,91,15,384,239,240,241,242,243,92,93,
392,394,393,391,244,245,246,247,248,396,108,97,395,227,398,397,95,249,96,253,399,36,37,400,401,402,403,94,98,102,404,420,251,407,264,
13,383,405,100,99,12,42,38,409,101,103,104,107,106,250,254,105,109,258,252,111,255,256,110,259,408,406,112,113,114,115,257,260,261,262,
116,410,263,412,411,265,413,266,414,415,267,268,117,119,416,118,417,269,120,270,421,422,121,271,122,273,123,124,272,423,424,425,274,426,
125,126,275,127,276,128,427,277,132,278,279,429,280,428,281,282,143,299,283,431,430,433,130,288,432,435,434,419,436,437,438,418,284,131,
129,137,133,134,135,439,136,444,443,286,455,442,287,285,138,139,140,39,440,289,144,291,290,293,146,145,292,43,294,141,142,441,295,445,
297,298,147,148,296,447,446,300,301,149,150,449,450,152,448,151,153,302,303,304,451,154,155,156,305,452,307,157,456,306,457,308,158,159,
160,161,162,163,458,459,460,461,167,309,453,310,311,312,313,462,454,463,314,464,315,316,317,318,164,466,178,465,323,468,334,467,319,320,
168,469,470,165,170,169,171,172,166,321,173,174,177,471,472,473,176,474,475,477,322,175,200,179,324,325,478,201,328,479,326,329,181,327,
330,331,180,182,333,332,183,356,335,476,484,480,336,184,186,482,185,481,485,483,337,338,339,486,487,202,188,357,341,187,342,490,190,189,
491,492,489,193,493,494,495,488,343,340,191,358,203,344,194,345,192,346,348,347,498,500,512,195,497,499,196,197,198,496,502,501,349,350,
516,503,513,514,515,504,505,359,506,518,199,351,352,353,354,355,517,507,508,509,510,511,522,519,521,520]
SEQ5 = SEQ
TJQ, TI, TIW, ZS, OBQ = None, 2, 2, 1120, "vector"
SEQ = [
2,3,10,4,5,40,46,17,206,20,366,0,21,18,35,41,22,44,26,45,23,11,19,1,6,47,7,8,48,49,50,14,368,34,209,208,210,51,52,53,54,27,55,
72,207,16,370,367,60,211,212,213,30,369,28,31,59,12,214,56,371,372,373,374,218,215,216,32,15,375,392,376,9,219,58,232,42,220,217,24,
378,221,36,29,379,380,25,381,33,57,61,66,62,37,226,38,13,63,64,67,377,65,222,68,69,223,382,224,227,383,386,73,74,225,384,387,228,70,
385,230,75,76,77,71,231,79,390,229,388,389,80,233,235,234,236,237,393,81,83,391,395,239,82,84,85,240,394,86,87,88,396,397,241,89,90,
91,399,242,243,244,245,246,247,248,96,400,249,250,251,95,92,401,97,403,252,78,402,404,94,405,406,407,39,408,93,98,108,256,238,409,410,
411,102,257,268,415,412,255,99,100,103,414,101,416,417,104,253,258,398,105,106,413,428,259,260,262,43,254,109,110,263,261,264,107,111,
418,266,267,112,265,113,419,420,422,269,271,421,423,270,272,424,425,114,115,117,116,118,119,121,429,430,431,273,275,120,276,432,433,123,
122,124,277,278,125,126,127,435,279,280,281,282,283,128,436,434,437,284,285,286,287,132,438,439,133,130,290,440,441,442,129,288,144,427,
426,443,444,445,446,447,138,134,131,292,274,136,464,293,135,137,304,139,448,140,141,452,289,294,143,142,295,296,298,449,451,291,145,146,
453,450,297,299,147,148,149,300,301,454,302,458,303,456,455,151,305,307,306,308,457,459,153,155,152,460,309,311,154,156,461,465,466,157,
158,312,313,159,160,314,467,468,469,463,161,162,163,471,315,317,310,316,318,473,472,164,319,320,321,322,323,168,474,150,475,476,169,326,
324,477,478,340,166,180,479,480,462,328,481,482,165,483,174,170,172,171,173,329,175,325,488,489,176,177,178,167,179,484,485,487,327,486,
334,202,470,203,330,181,332,331,182,333,335,336,490,338,183,184,185,337,339,187,188,492,491,341,494,500,186,493,362,363,495,342,343,344,
345,496,497,499,189,190,498,348,501,502,191,192,346,194,503,504,347,505,196,350,204,205,364,349,193,506,352,507,351,522,508,195,197,354,
509,198,355,523,199,511,510,353,356,200,512,515,516,513,514,524,357,358,526,359,360,525,201,361,365,528,527,517,518,519,520,521,529,530,
531,532]
KEY = {n: z for z, n in enumerate(SEQ)}

SCRATCH = {
    "x0": ("sbuf", [128, W], "int32"), "tt": ("sbuf", [128, W], "int32"), "ti": ("sbuf", [128, W], "int32"),
    "stb": ("sbuf", [128, W // 16], "int32"), "off": ("sbuf", [128, W // 16], "uint16"),
    "zz": ("sbuf", [128, ZS - ZV], "bfloat16"), "dif": ("sbuf", [128, 128], "float32"),
    "indb": ("sbuf", [128, 8], "bfloat16"), "indf": ("sbuf", [128, 8], "float32"), "zt": ("sbuf", [128, 36], "float32"),
    "sg": ("sbuf", [128, 8], "float32"), "sc": ("sbuf", [128, 1], "float32"), "cw": ("sbuf", [128, 32], "bfloat16"),
    "eyeb": ("sbuf", [128, 128], "bfloat16"), "eyep": ("sbuf", [128, 4, 32], "bfloat16"), "eyeq": ("sbuf", [128, 128], "float32"),
    "dm": ("sbuf", [128, 128], "bfloat16"), "sr": ("sbuf", [128, 144], "bfloat16"), "bs": ("sbuf", [128, 64], "bfloat16"),
    "bc": ("sbuf", [128, 512], "bfloat16"), "cx": ("sbuf", [128, 32], "bfloat16"), "b8": ("sbuf", [128, 16], "bfloat16"),
    "pm": ("sbuf", [128, 128], "float32" if COUNT == "f32" else "bfloat16"), "cu": ("sbuf", [128, 2, 132], "bfloat16"), "sm": ("sbuf", [128, 128], "float32"),
    "wk": ("sbuf", [128, 6, 16], "float32"), "wq": ("sbuf", [128, 6], "float32"),
    "oh": ("sbuf", [128, W // 16], "float16"), "ob": ("sbuf", [128, W // 16], "float32"), "oo": ("sbuf", [128, 4, W // 16], "float32"),
    "tj": ("sbuf", [128, W], "float32"), "sb": ("sbuf", [128, 2], "float32"), "pl": ("sbuf", [128, 2, 32, 4, 2], "float32"), "oc": ("sbuf", [128, W // 16], "float32"),
    "pz": ("psum", [128, 4, 32, 2, 2], "float32"), "pf": ("psum", [128, 4, 32, 2, 2], "float32"),
}
for _q, _b in enumerate(BL):
    for _k, _s, _d in (("rc", [128, RO * NR * 8 * _b], "float32"), ("xx", [128, 16 * _b], "float32"), ("xn", [128, 16 * _b], "float32"),
                       ("mx", [128, 8 * _b], "float32"), ("mn", [128, 8 * _b], "float32"), ("pc", [128, _b, 128], "float16"),
                       ("lt", [128, 32 * _b], "float16"), ("gt", [128, 128 * _b], "float32"), ("cm", [128, 128 * _b], "bfloat16"),
                       ("ga", [128, 128 * _b], "float32"), ("cc", [128, 128 * _b], "bfloat16"), ("pp", [128, 128 * _b], "float32"),
                       ("fa", [128, 128 * _b], "float16"), ("zr", [128, 32 * _b], "float32"),
                       ("nb", [128, 32], "bfloat16"), ("nt", [128, 32], "float32" if COUNT == "f32" else "bfloat16")):
        SCRATCH["%s%d" % (_k, _q)] = ("sbuf", _s, _d)
    SCRATCH["pv%d" % _q] = ("psum", [128, 4, 128], "float32")
    SCRATCH["po%d" % _q] = ("psum", [128, 4, 32, 2, 2], "float32")


def build():
    ops, lastw, readers, at = [], {}, {}, [None, -1]

    def op(queue, name, emit, reads, writes, ninc=1, after=(), banks=(), order=()):
        n = len(ops)
        o = {"n": n, "q": queue, "name": name, "at": tuple(at), "emit": emit, "ninc": ninc, "deps": set(after), "order": set(order), "banks": banks}
        for t in reads:
            if t in lastw:
                o["deps"].add(lastw[t])
        for t in writes:
            for i in ([lastw[t]] if t in lastw else []) + list(readers.get(t, ())):
                o["order" if t[0] == "@" and ops[i]["q"] == queue else "deps"].add(i)
        for t in reads:
            readers.setdefault(t, set()).add(n)
        for t in writes:
            lastw[t] = n
            readers[t] = set()
        o["deps"].discard(n)
        o["order"] -= o["deps"] | {n}
        ops.append(o)
        return n

    A = AluOpType
    CPY = ActivationFunctionType.Copy
    V, S, P, G = "vector", "scalar", "tensor", "gpsimd"

    def load(name, dst, src, writes, **k):
        return op("sync", name, lambda g, T, x: [g.sync.dma_start(dst(T), src(T))], [], writes, 16, **k)
    ls = load("l_st", lambda T: T.stb[:], lambda T: T.st[:], ["stb"])
    la = load("l_ta", lambda T: T.tt[0:TA, :], lambda T: T.tops[0:TA, :], ["tta"], order=(ls,))
    zz = op(V, "c_z", lambda g, T, x: [g.vector.memset(T.zz[:], 0.0)], [], ["zz"])
    za = op(V, "c_x0", lambda g, T, x: [g.vector.memset(T.x0[:, 0:ZV], 0)], [], [], order=(zz,))
    zb = op(S, "c_x1", lambda g, T, x: [g.scalar.activation(T.x0[:, ZV:ZS], T.zz[:], CPY)], ["zz"], [])
    zc = op(G, "c_x2", lambda g, T, x: [g.iota(T.x0[:, ZS:W], [[0, W - ZS]], 0, 0)], [], [])
    l0 = load("l_x0", lambda T: T.x0[0:128:16, :], lambda T: T.ids[0:128:16, :], ["x0"], after=(za, zb, zc), order=(la,))
    l1 = load("l_tt", lambda T: T.tt[TA:128, :], lambda T: T.tops[TA:128, :], ["ttb"], order=(l0,))
    for z in range(TI):
        c = slice(z * W // TI, (z + 1) * W // TI)
        l1 = load("l_ti%d" % z, lambda T, c=c: T.ti[:, c], lambda T, c=c: T.ids[:, c], ["ti%d" % z], order=(l1,))
    ti = ["ti%d" % z for z in range(TI)]

    for z, (buf, v) in enumerate((("indb", 1.0), ("sg", 1.0), ("zt", 0.0), ("cu", 0.0), ("cx", 0.0), ("wk", 0.0))):
        op(V, "c_m%d" % z, lambda g, T, x, buf=buf, v=v: [g.vector.memset(T[buf][:], v)], [], [buf])
    op(V, "c_cw", lambda g, T, x: [g.vector.memset(T.cw[:, a:b], v) for a, b, v in ((0, 8, 0.5), (8, 24, 32.0), (24, 32, 0.0))], [], ["cw"], 3)

    def sel(name, buf, pat, cmp, v, base, cm=1):
        op(G, name, lambda g, T, x: [g.affine_select(T[buf][:], T[buf][:], pat, cmp, v, base, cm)], [buf], [buf])
    sel("c_i1", "indb", [[-16, 8]], A.is_ge, 0.0, 0)
    sel("c_i2", "indb", [[16, 8]], A.is_ge, 0.0, 15, -1)
    sel("c_sg", "sg", [[-16, 8]], A.not_equal, -1.0, -15)
    op(G, "c_df", lambda g, T, x: [g.iota(T.dif[:], [[1, 128]], 0, -1, allow_small_or_imprecise_dtypes=True)], [], ["dif"])
    op(V, "c_ey", lambda g, T, x: [g.vector.tensor_scalar(T.eyeb[:], T.dif[:], 0.0, None, A.is_equal)], ["dif"], ["eyeb"])
    if PESUM:
        op(V, "c_eq", lambda g, T, x: [g.vector.tensor_scalar(T.eyeq[:], T.dif[:], 0.0, 1.0 / NR, A.is_equal, A.mult)], ["dif"], ["eyeq"])
    op(S, "c_ep", lambda g, T, x: [g.scalar.activation(T.eyep[:, b], T.eyeb[:, b:128:4], CPY) for b in range(4)], ["eyeb"], ["eyep"], 4)

    def copy(queue, name, out, src, reads, writes, **k):
        return op(queue, name, lambda g, T, x: [g.vector.tensor_copy(out(T), src(T)) if queue == V else g.scalar.activation(out(T), src(T), CPY)], reads, writes, **k)

    def two(name, out, a, b, alu, reads, writes, **k):
        return op(V, name, lambda g, T, x: [g.vector.tensor_tensor(out(T), a(T), b(T), alu)], reads, writes, **k)

    def fold(name, to, buf, n):
        two(name, lambda T: T[to][:, 0:n], lambda T: T[buf][:, 0:n], lambda T: T[buf][:, n:2 * n], A.add, [buf], [to])
    two("c_d1", lambda T: T.dm[:, 1:128], lambda T: T.eyeb[:, 0:127], lambda T: T.eyeb[:, 1:128], A.subtract, ["eyeb"], ["dm"])
    op(V, "c_d2", lambda g, T, x: [g.vector.tensor_tensor(T.dm[:, 0:128:16], T.eyeb[:, 15:128:16], T.eyeb[:, 0:128:16], A.subtract),
                                   g.vector.tensor_scalar(T.dm[:, 15:128:16], T.eyeb[:, 14:128:16], -1.0, None, A.mult)], ["eyeb"], ["dm"], 2)
    fold("c_b1", "bs", "eyeb", 64)
    fold("c_b2", "bs", "bs", 32)
    fold("c_b6", "b8", "bs", 16)
    fold("c_b7", "b8", "b8", 8)
    two("c_b3", lambda T: T.cw[:], lambda T: T.cw[:], lambda T: T.bs[:, 0:32], A.mult, ["bs", "cw"], ["cw"])
    fold("c_b4", "cw", "cw", 16)
    op(V, "c_b5", lambda g, T, x: [g.vector.tensor_tensor(T.cx[32 * b:32 * b + 32, 8 * b:8 * b + 8], T.cw[32 * b:32 * b + 32, 0:8], T.cw[32 * b:32 * b + 32, 8:16], A.add)
                                   for b in range(4)], ["cw"], ["cx"], 4)
    op(V, "c_bc", lambda g, T, x: [g.vector.tensor_copy(T.bc[:, i:512:16], T.cx[:]) for i in range(16)], ["cx"], ["bc"], 16)
    op(V, "c_sc", lambda g, T, x: [g.vector.tensor_reduce(T.sc[:], T.sg[:], AxisListType.X, A.min)], ["sg"], ["sc"])
    op(S, "c_if", lambda g, T, x: [g.scalar.activation(T.indf[:], T.indb[:], CPY, scale=0.03125)], ["indb"], ["indf"])
    wk = [(r, 3 * r, 3 * r + 1, 1, BIG) for r in range(RO)] + [(r, 3 * r + 1, 3 * r + 3, 1, 32.0) for r in range(RO + 1)] + [(5, 0, 12, 3, 1.0)]
    wa = list(enumerate((0, 32, 64, 96, 0, 96)))
    if not RELU:
        wk = [(3, 0, 12, 3, 32.0), (3, 1, 12, 3, 32.0), (4, 12, 14, 1, 32.0), (5, 2, 12, 3, 1.0)]
        wa = [(3, 64), (4, 0), (5, 96)]
    op(V, "c_w2", lambda g, T, x: [g.vector.memset(T.wk[:, z, a:b:s], v) for z, a, b, s, v in wk], ["wk"], ["wk"], len(wk))
    sel("c_w3", "wk", [[0, 6], [-8, 16]], A.is_ge, 0.0, 0)
    sel("c_w4", "wk", [[0, 6], [8, 16]], A.is_ge, 0.0, 7, -1)
    op(V, "c_w5", lambda g, T, x: [g.vector.tensor_reduce(T.wq[:, k:k + 1], T.wk[:, k], AxisListType.X, A.add) for k in range(6)], ["wk"], ["wq"], 6)
    if COUNT == "list":
        op(V, "c_r1", lambda g, T, x: [g.vector.memset(T.sr[:], 0.0)], [], ["sr"])
        op(S, "c_sr", lambda g, T, x: [g.scalar.activation(T.sr[:, 15:143:16], T.indb[:], CPY)], ["indb"], ["sr"])
    op(S, "c_zt", lambda g, T, x: [g.scalar.activation(T.zt[:, 3:35:4], T.indb[:], CPY)], ["indb"], ["zt"])
    op(S, "c_cu", lambda g, T, x: [g.scalar.activation(T.cu[:, z // 4 if RELU else 1, 3 + a:35 + a:4], T.b8[:, 0:8], CPY, scale=T.wq[:, z:z + 1])
                                   for z, a in wa], ["b8", "wq", "cu"], ["cu"], len(wa))
    if COUNT != "list":
        op(V, "c_p1", lambda g, T, x: [g.vector.memset(T.pm[:], 1.0)], [], ["pm"])
        sel("c_pm", "pm", [[1, 8], [8, 4], [32, 4]], A.is_equal, 0.0, 0, -1)
    if RELU:
        op(V, "c_s1", lambda g, T, x: [g.vector.memset(T.sm[:], 0.0)], [], ["sm"])
        op(S, "c_sm", lambda g, T, x: [g.scalar.activation(T.sm[:, 64:96], T.bs[:, 0:32], CPY)], ["bs"], ["sm"])
    if S0Q == S and TJQ == V:
        for z in range(TJ):
            ops[op(V, "c_tj%d" % z, lambda g, T, x, c=slice(z * W // TJ, (z + 1) * W // TJ): [
                g.vector.tensor_scalar(T.tj[:, c], T.ti[:, c], END - 0.25, None, A.min)], [ti[z * TI // TJ]], ["tj%d" % z])]["only"] = 1
    elif S0Q == S and TJQ:
        ops[op(V, "c_sb", lambda g, T, x: [g.vector.tensor_scalar(T.sb[:, z:z + 1], T.sc[:], v, None, A.mult) for z, v in enumerate((-1.0, END - 0.25))],
               ["sc"], ["sb"], 2)]["only"] = 1
        for z in range(TJ):
            ops[op(S, "c_tj%d" % z, lambda g, T, x, c=slice(z * W // TJ, (z + 1) * W // TJ): [
                g.scalar.activation(T.tj[:, c], T.ti[:, c], ActivationFunctionType.Relu, END - 0.25, -1.0)], [ti[z * TI // TJ]], ["tj%d" % z])]["only"] = 1
    op(V, "c_oi", lambda g, T, x: [g.vector.tensor_copy(T.off[:], T.stb[:])], ["stb"], ["off%d" % q for q in range(NC)])
    op(V, "c_ob", lambda g, T, x: [g.vector.tensor_copy(T.oh[:], T.stb[:])], ["stb"], ["oh%d" % q for q in range(NC)])
    if KEEP:
        keep = op(P, "c_bm", lambda g, T, x: [g.tensor.matmul(T.pz[:, 0, 0:24], T.eyeb[:], T.oh[:], True, False)], ["oh0", "eyeb"],
                  ["@pk%d" % q for q in range(NC)], banks=["pz"])

    def chunk(q):
        B = BL[q]
        N, L, c0 = 128 * B, 8 * B, 8 * sum(BL[:q])
        cols = slice(c0, c0 + L)
        Z = str(q)
        PV, PO = "pv" + Z, "po" + Z
        at[:] = [q, -1]

        def nm(*a):
            return [k + Z for k in a]

        def nb(k, a, b):
            return ["%s%d_%d" % (k, q, i) for i in range(a, b)]

        def rows(T, buf, a, b):
            return T[buf + Z][:, 128 * a:128 * b]

        def gather(name, out, table, a, b, reads, queue=S, **k):
            def emit(g, T, x):
                i = T[table][:, 0:W].indirect(T.off[:, c0 + 8 * a:c0 + 8 * b])
                if queue == V:
                    return [g.vector.tensor_copy(rows(T, out, a, b), i)]
                return [g.scalar.activation(rows(T, out, a, b), i, CPY, **{n: T[v][:] for n, v in k.items()})]
            op(queue, name, emit, reads + nm("off"), nb(out, a, b))

        PS, pst = (PV, nm("@pv0")) if PSB == "pv" else (PO, nm("@pm"))

        def rc(T, r, a, b):
            return T["rc" + Z][:, (r * NR + a) * L:(r * NR + b) * L]

        def sums(b, buf):
            op(P, "ps%d" % b, lambda g, T, x: [g.tensor.matmul(T[PV][:, 0, 8 * b:8 * b + 8] if PS == PV else T[PO][:, 2, 2 * b:2 * b + 2],
                                                               rows(T, buf, b, b + 1), T.indf[:], True, True)],
               nb(buf, b, b + 1) + ["indf"], pst + nb("@ps", b, b + 1) + (nm("@open") if PS == PO else []), banks=[PS])

        def send(r):
            def s0(g, T, x):
                o, i = rc(T, r, x["rank"], x["rank"] + 1), T[PV][:, 0, 0:L] if PS == PV else T[PO][:, 2, 0:8]
                if r and S0Q == S:
                    return [g.scalar.activation(o, i, CPY)]
                if x["rank"] == 1 and TJQ:
                    return [g.vector.tensor_scalar(o, i, (END - 0.25) / 32.0, None, A.min)]
                return [g.vector.tensor_copy(o, i)]
            op(S0Q if r else V, "s0", s0, nb("@ps", 0, B) + pst, ["own%d_%d" % (q, r)], banks=[PS])

            def ex(g, T, x):
                s = rc(T, r, x["rank"], x["rank"] + 1)
                tr = [RemoteDMATransfer(dst_ids=[DstId(rid=a[0], pnc=a[1]) for a in to], dma_engine_mask=m, remote_sem=T.sem["ar%d_%d" % (q, r)],
                                        srcs=[s], dsts=[s] * len(to), alu_op=0) for to, m in x["peers"]]
                g.remote_dma_fused(tr, local_sem=T.sem["sent"])
                return []
            k = op(G, "ex", ex, ["own%d_%d" % (q, r)], [], 0)
            ops[op("remote", "ar", None, [], ["arr%d_%d" % (q, r)], 0, after=(k,))]["sem"] = "ar%d_%d" % (q, r)

        op(V, "pz", lambda g, T, x: [g.vector.memset(T["pc" + Z][:], 0.0)], [], nb("pc", 0, 16))
        plane = lambda a: lambda T: T["pc" + Z][:, :, 8 * a:8 * a + 8]
        for z, (a, b, queue) in enumerate(G0):
            gather("g%d" % z, "ga", "x0", a, b, ["x0"], queue)
        for b in range(B):
            sums(b, "ga")
        send(0)
        pvs = nm("@pv0", "@pv1", "@pv2", "@pv3")[:B]
        pos = ["@d%d0" % q, "@d%d1" % q, "@pm" + Z, "@pn" + Z]
        for r in range(RO):
            at[1] = r - 1
            for z, (a, b) in enumerate(GT):
                gather("gt%d" % z, "gt", "tt", a, b, ["tta", "ttb"])
            src = ["arr%d_%d" % (q, r), "own%d_%d" % (q, r)]
            eq = 3 * r + (0 if RELU else 2)
            whole = lambda b: lambda T: T[b + Z][:]
            part = lambda b, a: lambda T: T[b + Z][:, a * L:a * L + L]
            ranks = lambda a, r=r: lambda T: rc(T, r, a, a + 2)
            mean = lambda T: T[PV][:, 1, 0:L]
            if TJQ is None:
                op(V, "cl", lambda g, T, x, r=r: [g.vector.tensor_scalar(T["mn" + Z][:], rc(T, r, x["rank"], x["rank"] + 1), (END - 0.25) / 32.0, None, A.min)],
                   src[1:], nm("mn"))
                k = op(P, "sa", lambda g, T, x: [g.tensor.matmul(mean(T), T.eyeq[:], T["mn" + Z][:], True, False)], nm("mn") + ["eyeq"], nm("@pv1", "@pv0"), banks=[PV])
            elif PESUM:
                k = op(P, "sa", lambda g, T, x, r=r: [g.tensor.matmul(mean(T), T.eyeq[:], rc(T, r, x["rank"], x["rank"] + 1), True, False)],
                       src[1:] + ["eyeq"], nm("@pv1", "@pv0"), banks=[PV])
            at[1] = r
            two("xx", whole("xx"), ranks(0), ranks(2), A.max, src, nm("xx"))
            two("mx", whole("mx"), part("xx", 0), part("xx", 1), A.max, nm("xx"), nm("mx"))
            if HIQ == V:
                two("hi", plane(eq + 1), part("xx", 0), part("xx", 1), A.max, nm("xx"), nb("pc", eq + 1, eq + 2))
            else:
                copy(S, "hi", plane(eq + 1), whole("mx"), nm("mx"), nb("pc", eq + 1, eq + 2))
            two("lo", plane(eq + 2), whole("mx"), plane(eq + 1), A.subtract, nm("mx") + nb("pc", eq + 1, eq + 2), nb("pc", eq + 2, eq + 3))
            if PESUM:
                op(P, "sb", lambda g, T, x, r=r: [g.tensor.matmul(mean(T), T.eyeq[:], rc(T, r, a, a + 1), False, z == NR - 2)
                                                  for z, a in enumerate(a for a in range(NR) if a != x["rank"])], src[:1] + ["eyeq"], nm("@pv1"), NR - 1, banks=[PV], order=(k,))
                two("eq", plane(eq), whole("mx"), mean, A.is_equal, nm("mx", "@pv1"), nb("pc", eq, eq + 1), banks=[PV])
            else:
                two("xn", whole("xn"), ranks(0), ranks(2), A.min, src, nm("xn"))
                two("mn", whole("mn"), part("xn", 0), part("xn", 1), A.min, nm("xn"), nm("mn"))
                two("eq", plane(eq), whole("mx"), whole("mn"), A.is_equal, nm("mx", "mn"), nb("pc", eq, eq + 1))
            op(V, "vt", lambda g, T, x, eq=eq: [g.vector.transpose(T["lt" + Z][:], T["pc" + Z][:, :, 8 * eq:8 * eq + 32])], nb("pc", eq, eq + 4), nm("lt"))
            op(P, "pb", lambda g, T, x: [g.tensor.matmul(T[PV][:, 0:B, 32 * b:32 * b + 32], T.bc[:, 128 * b:128 * b + 128], T["lt" + Z][:], True, True)
                                         for b in range(4)], nm("lt") + ["bc"], pvs, 4, banks=[PV])
            for a in () if RELU else (0, 1):
                two("hv%d" % a, plane(3 * r + a), plane(eq + 1 + a), plane(eq), A.mult, nb("pc", eq, eq + 1) + nb("pc", eq + 1 + a, eq + 2 + a),
                    nb("pc", 3 * r + a, 3 * r + a + 1))
            pn = lambda T: T.pz[:, 0, 8 * q:8 * q + 8] if KEEP else T[PO][:, 3, 0:L // 4]
            bm = lambda g, T: g.tensor.matmul(pn(T), T.eyeb[:], T.oh[:, cols], True, False)
            PN, pnt = ("pz", nm("@pk")) if KEEP else (PO, nm("@pn"))
            if KEEP:
                k = keep
            elif COUNT == "list":
                k = op(P, "bm", lambda g, T, x: [bm(g, T)], nm("oh") + ["eyeb"], nm("@pn", "@open"), banks=[PO])
            for a in range(CT):
                two("ct%d" % a, lambda T, a=a: T["cm" + Z][:, a:N:CT] if COUNT == "list" else rows(T, "cm", a, a + 1), lambda T, a=a: T["gt" + Z][:, a:N:CT],
                    lambda T, a=a: T[PV][:, 0:B, a:128:CT], A.is_lt, nb("gt", 0, B) + pvs, nb("cm", a, a + 1), banks=[PV], order=[len(ops) - 1] if a else [])
            for a in range(CT) if COUNT == "list" else ():
                k = op(P, "pn%d" % a, lambda g, T, x, a=a: [
                    g.tensor.matmul(pn(T), T.sr[:, 15 - i:143 - i], T["cm" + Z][:, i:N:16], False, i == 15 and (not KEEP or x.get("stop", False))) for i in range(a, 16, CT)],
                    nb("cm", a, a + 1) + ["sr"], pnt, 16 // CT, banks=[PN], order=(k,))
            if COUNT != "list":
                op(P, "pc", lambda g, T, x: [g.tensor.matmul(T[PO][:, 2, 2 * k:2 * k + 2], T["cm" + Z][:, k:N:4], T.indb[:], True, True) for k in range(4)],
                   nb("cm", 0, 4) + ["indb"], nm("@pm", "@open"), 4, banks=[PO])
                pm = lambda T: T[PO][:, 2, 0:8]
                if COUNT == "f32":
                    op(V, "nt", lambda g, T, x: [g.vector.transpose(T["nt" + Z][:], pm(T))], nm("@pm"), nm("nt"), banks=[PO])
                else:
                    copy(COUNT, "nb", whole("nb"), pm, nm("@pm"), nm("nb"), banks=[PO])
                    op(V, "nt", lambda g, T, x: [g.vector.transpose(T["nt" + Z][:], T["nb" + Z][:])], nm("nb"), nm("nt"))
                k = op(P, "bm", lambda g, T, x: [bm(g, T)], nm("oh") + ["eyeb"], nm("@pn", "@open"), banks=[PO])
                op(P, "pn", lambda g, T, x: [g.tensor.matmul(pn(T), T.pm[:], T["nt" + Z][:], False, True)], nm("nt") + ["pm"], nm("@pn"), banks=[PO], order=(k,))
            copy(OFQ, "of", lambda T: T.off[:, cols], pn, pnt, nm("off"), banks=[PN])
            to = "oh" if r < RO - 1 else "ob"
            if r == RO - 1 or not KEEP:
                copy(OBQ, "ob", lambda T, to=to: T[to][:, cols], pn, pnt, nm(to), banks=[PN])
            fin = r == RO - 1 and q == FIN
            for z, (a, b) in enumerate(GA if r < RO - 1 or q == FIN else GL):
                if S0Q == S and r < RO - 1 and TJQ:
                    op(S, "ga%d" % z, lambda g, T, x, a=a, b=b: [
                        g.scalar.activation(rows(T, "ga", a, b), T["tj" if x["rank"] == 1 else "ti"][:, 0:W].indirect(T.off[:, c0 + 8 * a:c0 + 8 * b]),
                                            *((ActivationFunctionType.Identity, T.sb[:, 1:2], T.sb[:, 0:1]) if x["rank"] == 1 and TJQ == S else (CPY, 0.0, T.sc[:])))],
                       ti + ["sc", "sb"] + ["tj%d" % y for y in range(TJ)] + nm("off"), nb("ga", a, b))
                else:
                    gather("ga%d" % z, "ga", "ti", a, b, ti + ["sc"], scale="sc")
                if CA is None:
                    two("ca%d" % z, lambda T, a=a, b=b: rows(T, "cc", a, b), lambda T, a=a, b=b: rows(T, "ga", a, b), lambda T, a=a, b=b: T[PV][:, a:b],
                        A.is_lt, nb("ga", a, b) + pvs[a:b], nb("cc", a, b), banks=[PV])
            for z, (a, b) in enumerate((CA if r < RO - 1 else CL) or ()):
                two("ca%d" % z, lambda T, a=a, b=b: rows(T, "cc", a, b), lambda T, a=a, b=b: rows(T, "ga", a, b), lambda T, a=a, b=b: T[PV][:, a:b],
                    A.is_lt, nb("ga", a, b) + pvs[a:b], nb("cc", a, b), banks=[PV])
            if r == RO - 1 and not fin:
                break
            for z, (a, b, bank, at0) in enumerate(DD or ()):
                reg = pos if bank == "po" else pvs
                op(P, "dd%d" % z, lambda g, T, x, a=a, b=b, bank=bank, at0=at0: [
                    g.tensor.matmul(T[bank + Z][:, at0:at0 + b - a], T.dm[:], rows(T, "cc", a, b), True, True)],
                   nb("cc", a, b) + ["dm"], reg[at0:at0 + b - a] + (nm("@open") if bank == "po" else []), banks=[bank + Z])
                for y, (c, d) in enumerate(MU):
                    if a <= c < b:
                        two("mu%d" % y, lambda T, c=c, d=d: rows(T, "pp", c, d), lambda T, c=c, d=d: rows(T, "ga", c, d),
                            lambda T, u=at0 + c - a, v=at0 + d - a, bank=bank: T[bank + Z][:, u:v], A.mult,
                            nb("ga", c, d) + reg[at0 + c - a:at0 + d - a], nb("pp", c, d), banks=[bank + Z])
            for b in range(0 if DD else B):
                bank, at0, tok = (PO, b // 2, "@d%d%d" % (q, b // 2)) if b % 2 == 0 else ("pz", q, "@z" + Z)
                pd = lambda T, bank=bank, at0=at0: T[bank][:, at0]
                op(P, "dd%d" % b, lambda g, T, x, b=b, pd=pd: [g.tensor.matmul(pd(T), T.dm[:], rows(T, "cc", b, b + 1), True, True)],
                   nb("cc", b, b + 1) + ["dm"], [tok] + (nm("@open") if bank == PO else []), banks=[bank])
                if not fin:
                    two("mu%d" % b, lambda T, b=b: rows(T, "pp", b, b + 1), lambda T, b=b: rows(T, "ga", b, b + 1), pd, A.mult,
                        nb("ga", b, b + 1) + [tok], nb("pp", b, b + 1), banks=[bank])
                    continue
                op(V, "mu%d" % b, lambda g, T, x, b=b, bank=bank, at0=at0: [
                    g.vector.tensor_tensor(T.pl[:, f, 8 * b:8 * b + 8], T["ga" + Z][:, 128 * b + f:128 * b + 128:2], T[bank][:, at0, :, :, f], A.mult) for f in (0, 1)],
                   nb("ga", b, b + 1) + [tok], nb("pp", b, b + 1), 2, banks=[bank])
                op(P, "ps%d" % b, lambda g, T, x, b=b: [
                    g.tensor.matmul(T.pv0[0:32, 0:2, 16 * b:16 * b + 16], T.zt[:, 3 - k:35 - k], T.pl[:, :, 8 * b:8 * b + 8, k, :], k == 0, k == 3)
                    for k in range(4)], nb("pp", b, b + 1) + ["zt"], ["@pv00", "@pv10", "@fin%d" % b], 4, banks=["pv0"])
            if not fin:
                for b in range(B):
                    sums(b, "pp")
            if r < RO - 1:
                send(r + 1)
        if q == FIN:
            op(V, "e6", lambda g, T, x: [g.vector.tensor_copy(T.oo[0:32, 2 * e:2 * e + 2, cols], T.pv0[0:32, 0:2, e:16 * B:2]) for e in (0, 1)],
               ["@fin%d" % b for b in range(B)], nm("oc"), 2, banks=["pv0"])
        elif LAST == 4:
            for z, (a, b) in enumerate(CL or GL):
                op(P, "dd%d" % z, lambda g, T, x, a=a, b=b: [g.tensor.matmul(T[PO][:, a:b], T.dm[:], rows(T, "cc", a, b), True, True)],
                   nb("cc", a, b) + ["dm"], pos[a:b], banks=[PO])
            for b in range(4):
                two("mu%d" % b, lambda T, b=b: rows(T, "pp", b, b + 1), lambda T, b=b: T["ga" + Z][:, b:N:4], lambda T, b=b: T[PO][:, :, :, b // 2, b % 2],
                    A.mult, nb("ga", 0, 4) + pos, nb("pp", b, b + 1), banks=[PO])
            for k in range(4):
                op(P, "ps%d" % k, lambda g, T, x, k=k: [g.tensor.matmul(T[PV][:, 0, k:32:4], T["pp" + Z][:, k:N:4], T.zt[:, 3:35:4], True, True)],
                   nb("pp", 0, 4) + ["zt"], nm("@pv0") + nb("@yc", k, k + 1), banks=[PV])
            op(V, "e6", lambda g, T, x: [g.vector.transpose(T.oc[:, cols], T[PV][:, 0, 0:32])], nb("@yc", 0, 4), nm("oc"), banks=[PV])
        else:
            for h, bank, tok in ((0, PO, ["@d%d0" % q, "@d%d1" % q]), (1, PV, pvs[0:2])):
                op(P, "dd%d" % h, lambda g, T, x, h=h, bank=bank: [g.tensor.matmul(T[bank][:, 0:2], T.dm[:], rows(T, "cc", 2 * h, 2 * h + 2), True, True)],
                   nb("cc", 2 * h, 2 * h + 2) + ["dm"], tok, banks=[bank])
                op(V, "mu%d" % h, lambda g, T, x, h=h: [
                    g.vector.tensor_tensor(T["pp" + Z][:, 128 * b + 64 * h:128 * b + 64 * h + 64], T["ga" + Z][:, 256 * h + b:256 * h + 256:4],
                                           T[PV][:, 0:2, b:128:4] if h else T[PO][:, 0:2, :, b // 2, b % 2], A.mult) for b in range(4)],
                   nb("ga", 2 * h, 2 * h + 2) + tok, ["pq%d" % h + Z] + nb("pp", 0, 4 - 4 * h), 4, banks=[bank])
            for k in range(4):
                op(P, "ps%d" % k, lambda g, T, x, k=k: [g.tensor.matmul(T[PO][:, 2, 0:8, k // 2, k % 2], T["pp" + Z][:, k:N:4], T.zt[:, 3:35:4], True, True)],
                   nm("pq0", "pq1") + ["zt"], nm("@pm") + nb("@yc", k, k + 1), banks=[PO])
            op(V, "e6", lambda g, T, x: [g.vector.transpose(T.oc[:, cols], T[PO][:, 2, 0:8])], nb("@yc", 0, 4), nm("oc"), banks=[PO])
        PH, ph = HB[q], ["@" + HB[q]]
        op(P, "h1", lambda g, T, x: [g.tensor.matmul(T[PH][0:120, :, 8 * b:8 * b + 8], T["pc" + Z][:, b, 0:120], T.eyep[:], True, True) for b in range(B)],
           nb("pc", 0, 15) + ["eyep"], ph, B, banks=[PH])
        copy(H2Q, "h2", lambda T: T["fa" + Z][0:120, :], lambda T: T[PH][0:120, :, 0:L], ph, nm("fa"), banks=[PH])
        zs = (0, 1) if RELU else (1,)
        op(P, "h3", lambda g, T, x: [g.tensor.matmul(T[PH][:, z, 0:L], T.cu[0:120, z, 3 - k:131 - k], T["fa" + Z][0:120, k:N:4], k == 0, k == 3 and z == zs[0])
                                     for z in zs for k in range(4)], nm("fa") + ["cu"], ph, 4 * len(zs), banks=[PH])
        if RELU:
            op(S, "h4", lambda g, T, x: [g.scalar.activation(T["zr" + Z][:], T[PH][:, 0, 0:L], ActivationFunctionType.Relu, bias=-BIG)], ph, nm("zr"), banks=[PH])
            op(P, "h5", lambda g, T, x: [g.tensor.matmul(T[PH][:, 1, 0:L], T.sm[:], T["zr" + Z][:], False, True)], nm("zr") + ["sm"], ph, banks=[PH])
        copy(H6Q, "h6", lambda T: T.oo[64:128, :, cols], lambda T: T[PH][64:128, 1, 0:L], ph, nm("oo"), banks=[PH])

    for q in range(NC):
        chunk(q)
    if TIW is not None:
        ops[l1]["deps"].add([o["n"] for o in ops if o["name"] == "s0" and o["at"] == (TIW, -1)][0])
        ops[l1]["order"].add([o["n"] for o in ops if o["name"] == "ex" and o["at"] == (TIW, -1)][0])
    at[:] = [None, RO]

    def store(queue, dst, src, tok):
        op(queue, "out", lambda g, T, x: [(g.sync if queue == "sync" else g.scalar).dma_start(dst(T), src(T))], tok, [], 16)
    every = lambda k: [k + str(q) for q in range(NC)]
    for y, src, tok in (("yb", lambda T: T.ob[:], "ob"), ("ys", lambda T: T.oo[64:96], "oo"), ("yh", lambda T: T.oo[96:128], "oo")):
        store("sync", lambda T, y=y: T[y][:], src, every(tok))
    n = 96 if FIN is None else 64
    for b in range(4):
        store(YQ[b], lambda T, b=b: T.yc[b:128:4, 0:n], lambda T, b=b: T.oc[32 * b:32 * b + 32, 0:n], every("oc")[:n // 32])
    if FIN is not None:
        store("sync", lambda T: T.yc[:, n:96], lambda T: T.oo[0:32, :, n:96], every("oc")[2:])
    return ops


def schedule(ops, key):
    after = {o["n"]: [] for o in ops}
    for o in ops:
        for d in o["deps"] | o["order"]:
            after[d].append(o["n"])
    left = {o["n"]: len(o["deps"] | o["order"]) for o in ops}
    ready, order = [n for n in left if left[n] == 0], []
    while ready:
        n = min(ready, key=lambda k: (key.get(k, k), k))
        order.append(n)
        ready.remove(n)
        for k in after[n]:
            left[k] -= 1
            if left[k] == 0:
                ready.append(k)
    return order


def plan(key, rank=1):
    ops = build()
    order = [i for i in schedule(ops, key) if ops[i].get("only", rank) == rank]
    pos = {i: z for z, i in enumerate(order)}
    known, clos, waits, waiters, bank = {}, {}, {}, {}, {}
    for i in order:
        o = ops[i]
        q = o["q"]
        if q == "remote":
            clos[i] = 1 << i
            continue
        deps = set(d for d in o["deps"] if d in pos)
        for b in o["banks"]:
            acc = bank.get(b, [])
            deps.update(d for d in acc if ops[d]["q"] != q)
            bank[b] = [d for d in acc if ops[d]["q"] == q] + [i]
        k = known.get(q, 0)
        waits[i] = []
        for d in sorted(deps, key=lambda d: -pos[d]):
            if not (k >> d) & 1 and (ops[d]["ninc"] or ops[d]["q"] == "remote"):
                waits[i].append(d)
                waiters.setdefault(d, set()).add(i)
                k |= clos[d]
        known[q] = k
        clos[i] = k | (1 << i)
    val, pool, cnt = {}, {}, {}
    for i in order:
        o = ops[i]
        if o["q"] == "remote":
            val[i] = (o["sem"], None)
        elif o["ninc"] and (i in waiters or o["name"] == "out"):
            sem = o["name"]
            if o["q"] != "sync" and sem != "out":
                undone = {s: [d for d in on if not (clos[i] >> d) & 1] for s, on in pool.items() if ops[on[0]]["q"] == o["q"]}
                fit = [s for s, on in undone.items() if all(waiters[d] <= waiters[i] for d in on)]
                sem = max(fit, key=lambda s: len(undone[s])) if fit else "s%d" % len(pool)
                pool.setdefault(sem, []).append(i)
            cnt[sem] = cnt.get(sem, 0) + o["ninc"]
            val[i] = (sem, cnt[sem])
    need = {i: {} for i in waits}
    for i in waits:
        for d in waits[i]:
            sem, n = val[d]
            need[i][sem] = n if n is None else max(n, need[i].get(sem, 0))
    return ops, order, need, val, cnt


PLANS = [plan(KEY, rank) for rank in (0, 1)]
SEMAPHORES = sorted(set(PLANS[0][4]) | set(PLANS[1][4])) + ["ar%d_%d" % (q, r) for q in range(NC) for r in range(RO)] + ["sent"]


def context(rank, core, T, topo):
    peers = [c for c in T.cores if c != core]
    chip = topo.cores_of(core)
    far = [c for c in peers if c not in chip]
    near = [c for c in peers if c in chip]
    out = topo.engines(core, far[0])
    ins = [k for k in topo.engines(core, near[0]) if k not in out][:len(out) // len(far)]
    bits = lambda e: sum(1 << k for k in e)
    return {"rank": rank, "peers": [([topo.addr(c, core) for c in far], bits(out)), ([topo.addr(c, core) for c in near], bits(ins))],
            "inn": len(out) * len(far) + len(ins) * len(near), "sent": len(out) + len(ins)}


def rank_program(g, core, T, topo):
    rank = T.rank_of(core)
    if rank is None:
        return
    x = context(rank, core, T, topo)
    OPS, ORDER, WAITS, VAL, CNT = PLANS[int(rank == 1)]
    queue = {"sync": g.sync, "scalar": g.scalar, "vector": g.vector, "tensor": g.tensor, "gpsimd": g}
    for i in ORDER:
        o = OPS[i]
        if o["q"] == "remote":
            continue
        e = queue[o["q"]]
        for sem, n in WAITS[i].items():
            e.wait_ge(T.sem[sem], x["inn"] if n is None else n)
        x["stop"] = i == [k for k in ORDER if OPS[k]["name"][:2] == "pn"][-1]
        ins = o["emit"](g, T, x)
        if i in VAL:
            for k in ins:
                k.then_inc(T.sem[VAL[i][0]], o["ninc"] // len(ins))
    g.sync.wait_ge(T.sem["out"], CNT["out"])
    g.wait_ge(T.sem["sent"], x["sent"] * NC * RO)
